import numpy as np
import ml_dtypes


def mxq(x, axis, fmt="e4m3"):
    dtype, down = {"e4m3": (ml_dtypes.float8_e4m3fn, 7), "e5m2": (ml_dtypes.float8_e5m2, 14)}[fmt]
    v = np.moveaxis(np.asarray(x, np.float32).astype(ml_dtypes.bfloat16).astype(np.float64), axis, -1)
    blocks = v.reshape(v.shape[:-1] + (-1, 32))
    amax = np.abs(blocks).max(-1, keepdims=True)
    byte = np.maximum(np.where(amax > 0, np.frexp(amax)[1] - 1 + 127, 0) - down, 1)
    scale = np.exp2(byte - 127.0)
    codes = (blocks / scale).astype(np.float32).astype(dtype).astype(np.float64)
    return np.moveaxis((codes * scale).reshape(v.shape), -1, axis)


WIDE = False


def mx_kscale(k):
    if not WIDE:
        return np.ones(k)
    levels = np.array([24, -24, 12, -12, 0])
    if k % 512:
        return np.exp2(np.random.permutation(np.resize(levels, k // 32))).repeat(32)
    a = np.empty((k // 512, 16))
    for p in range(k // 512):
        a[p, :8] = np.random.permutation(np.resize(levels, 8))
        for g in range(8):
            far = levels[np.abs(levels - a[p, g]) >= 10]
            a[p, g + 8] = far[np.random.randint(len(far))]
    return np.exp2(a.ravel()).repeat(32)


def f64(x):
    return np.asarray(x).astype(np.float64)


def striped(idx):
    return np.tile(idx.reshape(-1, 16).T, (8, 1)).astype(np.uint16)


def unstriped(offs):
    return offs[:16].T.reshape(-1).astype(np.int64)


E2M1 = np.array([0.0, 0.5, 1.0, 1.5, 2.0, 3.0, 4.0, 6.0, -0.0, -0.5, -1.0, -1.5, -2.0, -3.0, -4.0, -6.0])


def pack_weight(w, fmt):
    k, n = w.shape
    w = f64(np.asarray(w, np.float32).astype(ml_dtypes.bfloat16)).reshape(k // 32, 32, n)
    amax = np.abs(w).max(1)
    if fmt == "e4m3":
        byte = np.frexp(amax)[1] - 1 + 127 - 7
    else:
        mant, ex = np.frexp(amax / 6.0)
        byte = np.where(mant > 0.5, ex, ex - 1) + 127
    byte = np.clip(np.where(amax > 0, byte, 1), 1, 254)
    scaled = (w * np.exp2(127.0 - byte)[:, None, :]).reshape(k, n).astype(np.float32)
    by_word = np.ascontiguousarray(scaled.reshape(k // 512, 128, 4, n).transpose(0, 1, 3, 2))
    if fmt == "e4m3":
        words = by_word.astype(ml_dtypes.float8_e4m3fn).view(np.uint8)
    else:
        c = by_word.astype(ml_dtypes.float4_e2m1fn).view(np.uint8) & 0xF
        words = (c[..., 0::2] | (c[..., 1::2] << 4)).reshape(k // 512, 128, 2 * n)
    return np.ascontiguousarray(words), np.ascontiguousarray(byte.astype(np.uint8).reshape(k // 512, 16, n))


def unpack_weight(words, scales, fmt):
    g, _, n = scales.shape
    words = np.ascontiguousarray(words).reshape(g, 128, n, -1)
    if fmt == "e4m3":
        vals = words.view(ml_dtypes.float8_e4m3fn).astype(np.float64)
    else:
        nib = np.empty((g, 128, n, 4), np.uint8)
        nib[..., 0::2] = words & 0xF
        nib[..., 1::2] = words >> 4
        vals = E2M1[nib]
    vals = vals * np.repeat(np.exp2(scales.astype(np.float64) - 127.0), 8, axis=1)[..., None]
    return vals.transpose(0, 1, 3, 2).reshape(g * 512, n)


def sigm(f):
    return 1.0 / (1.0 + np.exp(-np.maximum(f, -700.0)))


K, N, T, J = 1024, 512, 2048, 1024


def setup_inputs():
    n = np.random.standard_normal
    s = mx_kscale(K)[:, None]
    p_tab = pack_weight(n((K, T)) * s, "e4m3")
    p_wb = pack_weight(n((K, N)) / np.sqrt(2 * K) / s, "e4m3")
    return {
        "tab_words": p_tab[0],
        "tab_scales": p_tab[1],
        "wa": (n((K, N)) / np.sqrt(2 * K) / s).astype(np.float32),
        "wb_words": p_wb[0],
        "wb_scales": p_wb[1],
        "wc": (n((K, N)) / np.sqrt(K) / s).astype(np.float32),
        "rT": (n((N, T))).astype(np.float32),
        "wgo": np.tile(np.random.uniform(0.5, 2.0, J), (128, 1)).astype(np.float32),
        "offs": striped(np.random.permutation(T)[:J]),
        "offs2": striped(np.random.permutation(T)[:J]),
    }


def reference(tab_words, tab_scales, wa, wb_words, wb_scales, wc, rT, wgo, offs, offs2):
    idx = unstriped(offs)
    idx2 = unstriped(offs2)
    tab_ = unpack_weight(tab_words, tab_scales, "e4m3")[:, idx]
    tabb_ = unpack_weight(tab_words, tab_scales, "e4m3")[:, idx2]
    wa_ = mxq(f64(wa), 0, "e4m3")
    wb_ = unpack_weight(wb_words, wb_scales, "e4m3")
    za = wa_.T @ tabb_ + wb_.T @ tab_
    eta = sigm(za)
    wc_ = mxq(f64(wc), 0, "e4m3")
    ms = wc_.T @ tab_
    out = np.zeros((N, T))
    out[:, idx2] = f64(wgo)[0] * (eta * ms + f64(rT)[:, idx2])
    return out

@@ -1,0 +1,180 @@
+from contextlib import ExitStack
+
+import concourse.mybir as mybir
+
+K, N, T, J = 1024, 512, 2048, 1024
+FLOPS = 3 * 2 * K * N * J
+
+F32 = mybir.dt.float32
+BF16 = mybir.dt.bfloat16
+I32 = mybir.dt.int32
+U32 = mybir.dt.uint32
+U16 = mybir.dt.uint16
+U8 = mybir.dt.uint8
+FP8X4 = mybir.dt.float8_e4m3fn_x4
+ALU = mybir.AluOpType
+ACT = mybir.ActivationFunctionType
+
+P = 128
+PACK = 4
+K_PASS = P * PACK
+PASSES = K // K_PASS
+JH = 512
+NH = 256
+LIST_COLS = J // 16
+
+
+def tile_list_rgg_L_kernel(
+    tc, tab_words, tab_scales, wa, wb_words, wb_scales, wc, rT, wgo, offs, offs2, out
+):
+    nc = tc.nc
+    with ExitStack() as ctx:
+        keep = ctx.enter_context(tc.tile_pool(name="keep", bufs=1))
+        ring = ctx.enter_context(tc.tile_pool(name="ring", bufs=2))
+        psum = ctx.enter_context(tc.psum_pool(name="psum", bufs=4))
+
+        src_list = keep.tile([P, LIST_COLS], U16, name="src_list")
+        dst_list = keep.tile([P, LIST_COLS], U16, name="dst_list")
+        nc.sync.dma_start(src_list[:], offs)
+        nc.sync.dma_start(dst_list[:], offs2)
+        lists = (src_list, dst_list)
+
+        def load_planes(planes, scales):
+            for q in range(4):
+                nc.sync.dma_start(
+                    planes[32 * q : 32 * q + 4 * PASSES, :].bitcast(I32),
+                    scales[:, 4 * q : 4 * q + 4, :].bitcast(I32),
+                )
+
+        tab_planes = keep.tile([P, T], U8, name="tab_planes", align_bytes=64)
+        nc.vector.memset(tab_planes[:].bitcast(I32), 0)
+        load_planes(tab_planes, tab_scales)
+
+        pages = [keep.tile([P, T], F32, name="page%d" % i) for i in range(2)]
+        for page in pages:
+            nc.vector.memset(page[:], 0.0)
+
+        tab = [keep.tile([P, T], U32, name="tab%d" % a) for a in range(PASSES)]
+
+        def load_tab(a):
+            nc.sync.dma_start(
+                tab[a][:].bitcast(I32), tab_words[a].rearrange("p t i -> p (t i)").bitcast(I32)
+            )
+
+        raw = {}
+
+        def load_weights(h):
+            for name, w in (("wa", wa), ("wc", wc)):
+                for a in range(PASSES):
+                    raw[name, a, h] = keep.tile([P, PACK, NH], F32, name="raw_%s%d%d" % (name, a, h))
+                    nc.sync.dma_start(
+                        raw[name, a, h][:],
+                        w[a * K_PASS : (a + 1) * K_PASS, h * NH : (h + 1) * NH].rearrange("(p i) n -> p i n", i=PACK),
+                    )
+
+        state = [keep.tile([P, T], F32, name="state%d" % m) for m in range(N // P)]
+
+        def load_state(m):
+            nc.sync.dma_start(state[m][:], rT[m * P : (m + 1) * P, :])
+
+        load_tab(0)
+        load_weights(0)
+        wb_codes = keep.tile([P, PASSES, N], U32, name="wb_codes", align_bytes=64)
+        wb_planes = keep.tile([P, N], U8, name="wb_planes", align_bytes=64)
+        load_planes(wb_planes, wb_scales)
+        nc.sync.dma_start(
+            wb_codes[:].bitcast(I32), wb_words.rearrange("a p n i -> p a (n i)").bitcast(I32)
+        )
+        load_tab(1)
+        load_state(0)
+        edge_weight = keep.tile([P, J], F32, name="edge_weight")
+        nc.sync.dma_start(edge_weight[:], wgo)
+        load_state(1)
+        load_weights(1)
+        load_state(2)
+        load_state(3)
+
+        picked_planes = []
+        for li in range(2):
+            planes = keep.tile([P, J], U8, name="picked_planes%d" % li, align_bytes=64)
+            nc.vector.tensor_copy(planes[:], tab_planes[:].indirect(lists[li][:]))
+            picked_planes.append(planes)
+
+        picked = {}
+
+        def gather_words(a):
+            for h in range(J // JH):
+                for li in range(2):
+                    picked[li, a, h] = keep.tile([P, JH], U32, name="picked%d%d%d" % (li, a, h), align_bytes=64)
+                    cols = lists[li][:, h * JH // 16 : (h + 1) * JH // 16]
+                    nc.vector.tensor_copy(picked[li, a, h][:], tab[a][:].indirect(cols))
+
+        codes = {}
+        scales = {}
+
+        def quantise_weights(h):
+            for name in ("wa", "wc"):
+                for a in range(PASSES):
+                    grouped = keep.tile([P, NH, PACK], BF16, name="grp_%s%d%d" % (name, a, h), align_bytes=64)
+                    nc.scalar.copy(grouped[:], raw[name, a, h][:].rearrange("p i n -> p n i"))
+                    codes[name, a, h] = keep.tile([P, NH], U32, name="codes_%s%d%d" % (name, a, h), align_bytes=64)
+                    scales[name, a, h] = keep.tile([P, NH], U8, name="scales_%s%d%d" % (name, a, h), align_bytes=64)
+                    nc.vector.quantize_mx(
+                        out=codes[name, a, h][:].bitcast(FP8X4),
+                        scales=scales[name, a, h][:],
+                        in_=grouped[:].rearrange("p n i -> p (n i)"),
+                    )
+
+        def product(acc, w_codes, w_scales, li, a, h, start, stop):
+            nc.tensor.matmul_mx(
+                out=acc[:],
+                lhsT=w_codes.bitcast(FP8X4),
+                lhsT_scale=w_scales,
+                rhs=picked[li, a, h][:].bitcast(FP8X4),
+                rhs_scale=picked_planes[li][4 * a :, h * JH : (h + 1) * JH],
+                start=start,
+                stop=stop,
+            )
+
+        gated = {}
+        summed = {}
+
+        def gate(m):
+            nh, c0 = divmod(m * P, NH)
+            cols = slice(c0, c0 + P)
+            wb_cols = slice(m * P, (m + 1) * P)
+            gated[m] = ring.tile([P, J], F32, name="gated")
+            for h in range(J // JH):
+                za = psum.tile([P, JH], F32, name="za")
+                ms = psum.tile([P, JH], F32, name="ms")
+                for a in range(PASSES):
+                    last = a == PASSES - 1
+                    product(za, wb_codes[:, a, wb_cols], wb_planes[4 * a :, wb_cols], 0, a, h, a == 0, False)
+                    product(za, codes["wa", a, nh][:, cols], scales["wa", a, nh][:, cols], 1, a, h, False, last)
+                    product(ms, codes["wc", a, nh][:, cols], scales["wc", a, nh][:, cols], 0, a, h, a == 0, last)
+                eta = ring.tile([P, JH], F32, name="eta", bufs=4)
+                nc.scalar.activation(eta[:], za[:], ACT.Sigmoid)
+                nc.vector.tensor_tensor(gated[m][:, h * JH : (h + 1) * JH], ms[:], eta[:], ALU.mult)
+
+        def add_state(m):
+            summed[m] = ring.tile([P, J], F32, name="summed")
+            nc.vector.tensor_tensor(summed[m][:], state[m][:].indirect(dst_list[:]), gated[m][:], ALU.add)
+
+        def place(m):
+            page = pages[m % 2]
+            nc.vector.tensor_tensor(page[:].indirect(dst_list[:]), summed[m][:], edge_weight[:], ALU.mult)
+            nc.sync.dma_start(out[m * P : (m + 1) * P, :], page[:])
+
+        gather_words(0)
+        quantise_weights(0)
+        gather_words(1)
+        gate(0)
+        add_state(0)
+        gate(1)
+        place(0)
+        quantise_weights(1)
+        for m in range(1, N // P):
+            add_state(m)
+            if m + 1 < N // P:
+                gate(m + 1)
+            place(m)

@@ -35,8 +35,6 @@ def tile_list_rgg_L_kernel(
 
         src_list = keep.tile([P, LIST_COLS], U16, name="src_list")
         dst_list = keep.tile([P, LIST_COLS], U16, name="dst_list")
-        nc.sync.dma_start(src_list[:], offs)
-        nc.sync.dma_start(dst_list[:], offs2)
         lists = (src_list, dst_list)
 
         def load_planes(planes, scales):
@@ -48,11 +46,10 @@ def tile_list_rgg_L_kernel(
 
         tab_planes = keep.tile([P, T], U8, name="tab_planes", align_bytes=64)
         nc.vector.memset(tab_planes[:].bitcast(I32), 0)
-        load_planes(tab_planes, tab_scales)
 
         pages = [keep.tile([P, T], F32, name="page%d" % i) for i in range(2)]
         for page in pages:
-            nc.vector.memset(page[:], 0.0)
+            nc.gpsimd.memset(page[:], 0.0)
 
         tab = [keep.tile([P, T], U32, name="tab%d" % a) for a in range(PASSES)]
 
@@ -78,6 +75,9 @@ def tile_list_rgg_L_kernel(
             nc.sync.dma_start(state[m][:], rT[m * P : (m + 1) * P, :])
 
         load_tab(0)
+        nc.sync.dma_start(src_list[:], offs)
+        nc.sync.dma_start(dst_list[:], offs2)
+        load_planes(tab_planes, tab_scales)
         load_weights(0)
         wb_codes = keep.tile([P, PASSES, N], U32, name="wb_codes", align_bytes=64)
         wb_planes = keep.tile([P, N], U8, name="wb_planes", align_bytes=64)
@@ -87,11 +87,11 @@ def tile_list_rgg_L_kernel(
         )
         load_tab(1)
         load_state(0)
+        load_weights(1)
+        load_state(1)
+        load_state(2)
         edge_weight = keep.tile([P, J], F32, name="edge_weight")
         nc.sync.dma_start(edge_weight[:], wgo)
-        load_state(1)
-        load_weights(1)
-        load_state(2)
         load_state(3)
 
         picked_planes = []
@@ -136,15 +136,20 @@ def tile_list_rgg_L_kernel(
                 stop=stop,
             )
 
-        gated = {}
-        summed = {}
+        weighted = {}
+        picked_state = {}
+
+        def gather_state(m):
+            picked_state[m] = keep.tile([P, J], F32, name="picked_state%d" % m)
+            nc.vector.tensor_copy(picked_state[m][:], state[m][:].indirect(dst_list[:]))
 
         def gate(m):
             nh, c0 = divmod(m * P, NH)
             cols = slice(c0, c0 + P)
             wb_cols = slice(m * P, (m + 1) * P)
-            gated[m] = ring.tile([P, J], F32, name="gated")
+            gated = keep.tile([P, J], F32, name="gated")
             for h in range(J // JH):
+                edges = slice(h * JH, (h + 1) * JH)
                 za = psum.tile([P, JH], F32, name="za")
                 ms = psum.tile([P, JH], F32, name="ms")
                 for a in range(PASSES):
@@ -154,27 +159,28 @@ def tile_list_rgg_L_kernel(
                     product(ms, codes["wc", a, nh][:, cols], scales["wc", a, nh][:, cols], 0, a, h, a == 0, last)
                 eta = ring.tile([P, JH], F32, name="eta", bufs=4)
                 nc.scalar.activation(eta[:], za[:], ACT.Sigmoid)
-                nc.vector.tensor_tensor(gated[m][:, h * JH : (h + 1) * JH], ms[:], eta[:], ALU.mult)
-
-        def add_state(m):
-            summed[m] = ring.tile([P, J], F32, name="summed")
-            nc.vector.tensor_tensor(summed[m][:], state[m][:].indirect(dst_list[:]), gated[m][:], ALU.add)
+                message = ring.tile([P, JH], F32, name="message", bufs=4)
+                nc.scalar.copy(message[:], ms[:])
+                nc.gpsimd.tensor_tensor(gated[:, edges], message[:], eta[:], ALU.mult)
+            nc.gpsimd.tensor_tensor(gated[:], gated[:], picked_state[m][:], ALU.add)
+            weighted[m] = keep.tile([P, J], F32, name="weighted%d" % m)
+            nc.gpsimd.tensor_tensor(weighted[m][:], gated[:], edge_weight[:], ALU.mult)
 
         def place(m):
             page = pages[m % 2]
-            nc.vector.tensor_tensor(page[:].indirect(dst_list[:]), summed[m][:], edge_weight[:], ALU.mult)
+            nc.vector.tensor_copy(page[:].indirect(dst_list[:]), weighted[m][:])
             nc.sync.dma_start(out[m * P : (m + 1) * P, :], page[:])
 
         gather_words(0)
         quantise_weights(0)
         gather_words(1)
+        gather_state(0)
         gate(0)
-        add_state(0)
-        gate(1)
-        place(0)
         quantise_weights(1)
-        for m in range(1, N // P):
-            add_state(m)
-            if m + 1 < N // P:
-                gate(m + 1)
+        gather_state(1)
+        gate(1)
+        for m in range(2, N // P):
+            gather_state(m)
+            gate(m)
+        for m in range(N // P):
             place(m)

@@ -20,8 +20,8 @@ PACK = 4
 K_PASS = P * PACK
 PASSES = K // K_PASS
 JH = 512
-NH = 256
 LIST_COLS = J // 16
+TILES = N // P
 
 
 def tile_list_rgg_L_kernel(
@@ -30,7 +30,7 @@ def tile_list_rgg_L_kernel(
     nc = tc.nc
     with ExitStack() as ctx:
         keep = ctx.enter_context(tc.tile_pool(name="keep", bufs=1))
-        ring = ctx.enter_context(tc.tile_pool(name="ring", bufs=2))
+        ring = ctx.enter_context(tc.tile_pool(name="ring", bufs=4))
         psum = ctx.enter_context(tc.psum_pool(name="psum", bufs=4))
 
         src_list = keep.tile([P, LIST_COLS], U16, name="src_list")
@@ -45,8 +45,7 @@ def tile_list_rgg_L_kernel(
                 )
 
         tab_planes = keep.tile([P, T], U8, name="tab_planes", align_bytes=64)
-        nc.vector.memset(tab_planes[:].bitcast(I32), 0)
-
+        nc.gpsimd.memset(tab_planes[:].bitcast(I32), 0)
         pages = [keep.tile([P, T], F32, name="page%d" % i) for i in range(2)]
         for page in pages:
             nc.gpsimd.memset(page[:], 0.0)
@@ -60,127 +59,150 @@ def tile_list_rgg_L_kernel(
 
         raw = {}
 
-        def load_weights(h):
+        def load_weights(a):
             for name, w in (("wa", wa), ("wc", wc)):
-                for a in range(PASSES):
-                    raw[name, a, h] = keep.tile([P, PACK, NH], F32, name="raw_%s%d%d" % (name, a, h))
-                    nc.sync.dma_start(
-                        raw[name, a, h][:],
-                        w[a * K_PASS : (a + 1) * K_PASS, h * NH : (h + 1) * NH].rearrange("(p i) n -> p i n", i=PACK),
-                    )
+                raw[name, a] = keep.tile([P, PACK, N], F32, name="raw_%s%d" % (name, a))
+                nc.sync.dma_start(
+                    raw[name, a][:],
+                    w[a * K_PASS : (a + 1) * K_PASS, :].rearrange("(p i) n -> p i n", i=PACK),
+                )
 
-        state = [keep.tile([P, T], F32, name="state%d" % m) for m in range(N // P)]
-
-        def load_state(m):
-            nc.sync.dma_start(state[m][:], rT[m * P : (m + 1) * P, :])
+        state = [keep.tile([P, T], F32, name="state%d" % m, tag="state%d" % m) for m in range(TILES)]
+        wb_codes = keep.tile([P, PASSES, N], U32, name="wb_codes", align_bytes=64)
+        wb_planes = keep.tile([P, N], U8, name="wb_planes", align_bytes=64)
+        edge_weight = keep.tile([P, J], F32, name="edge_weight")
 
         load_tab(0)
         nc.sync.dma_start(src_list[:], offs)
         nc.sync.dma_start(dst_list[:], offs2)
         load_planes(tab_planes, tab_scales)
-        load_weights(0)
-        wb_codes = keep.tile([P, PASSES, N], U32, name="wb_codes", align_bytes=64)
-        wb_planes = keep.tile([P, N], U8, name="wb_planes", align_bytes=64)
         load_planes(wb_planes, wb_scales)
+        load_weights(0)
+        load_tab(1)
+        load_weights(1)
         nc.sync.dma_start(
             wb_codes[:].bitcast(I32), wb_words.rearrange("a p n i -> p a (n i)").bitcast(I32)
         )
-        load_tab(1)
-        load_state(0)
-        load_weights(1)
-        load_state(1)
-        load_state(2)
-        edge_weight = keep.tile([P, J], F32, name="edge_weight")
-        nc.sync.dma_start(edge_weight[:], wgo)
-        load_state(3)
+        for m in (1, 0, 2, 3):
+            nc.sync.dma_start(state[m][:], rT[m * P : (m + 1) * P, :])
+            if m == 2:
+                nc.sync.dma_start(edge_weight[:], wgo)
 
         picked_planes = []
-        for li in range(2):
-            planes = keep.tile([P, J], U8, name="picked_planes%d" % li, align_bytes=64)
-            nc.vector.tensor_copy(planes[:], tab_planes[:].indirect(lists[li][:]))
-            picked_planes.append(planes)
+
+        def gather_planes():
+            for li in range(2):
+                planes = keep.tile([P, J], U8, name="picked_planes%d" % li, align_bytes=64)
+                nc.vector.tensor_copy(planes[:], tab_planes[:].indirect(lists[li][:]))
+                picked_planes.append(planes)
 
         picked = {}
 
-        def gather_words(a):
-            for h in range(J // JH):
+        def gather_words(a, width):
+            for j0 in range(0, J, width):
                 for li in range(2):
-                    picked[li, a, h] = keep.tile([P, JH], U32, name="picked%d%d%d" % (li, a, h), align_bytes=64)
-                    cols = lists[li][:, h * JH // 16 : (h + 1) * JH // 16]
-                    nc.vector.tensor_copy(picked[li, a, h][:], tab[a][:].indirect(cols))
+                    words = keep.tile([P, width], U32, name="picked%d%d_%d" % (li, a, j0), align_bytes=64)
+                    cols = lists[li][:, j0 // 16 : (j0 + width) // 16]
+                    nc.vector.tensor_copy(words[:], tab[a][:].indirect(cols))
+                    for j in range(0, width, JH):
+                        picked[li, a, (j0 + j) // JH] = words[:, j : j + JH]
 
         codes = {}
         scales = {}
 
-        def quantise_weights(h):
+        def quantise_weights(a):
             for name in ("wa", "wc"):
-                for a in range(PASSES):
-                    grouped = keep.tile([P, NH, PACK], BF16, name="grp_%s%d%d" % (name, a, h), align_bytes=64)
-                    nc.scalar.copy(grouped[:], raw[name, a, h][:].rearrange("p i n -> p n i"))
-                    codes[name, a, h] = keep.tile([P, NH], U32, name="codes_%s%d%d" % (name, a, h), align_bytes=64)
-                    scales[name, a, h] = keep.tile([P, NH], U8, name="scales_%s%d%d" % (name, a, h), align_bytes=64)
-                    nc.vector.quantize_mx(
-                        out=codes[name, a, h][:].bitcast(FP8X4),
-                        scales=scales[name, a, h][:],
-                        in_=grouped[:].rearrange("p n i -> p (n i)"),
-                    )
+                grouped = keep.tile([P, N, PACK], BF16, name="grouped_%s%d" % (name, a), tag="grouped_%s%d" % (name, a), align_bytes=64)
+                nc.scalar.copy(
+                    grouped[:].rearrange("p (c n) i -> p c i n", n=4),
+                    raw[name, a][:].rearrange("p i (c n) -> p c i n", n=4),
+                )
+                codes[name, a] = keep.tile([P, N], U32, name="codes_%s%d" % (name, a), align_bytes=64)
+                scales[name, a] = keep.tile([P, N], U8, name="scales_%s%d" % (name, a), align_bytes=64)
+                nc.vector.quantize_mx(
+                    out=codes[name, a][:].bitcast(FP8X4),
+                    scales=scales[name, a][:],
+                    in_=grouped[:].rearrange("p n i -> p (n i)"),
+                )
 
         def product(acc, w_codes, w_scales, li, a, h, start, stop):
             nc.tensor.matmul_mx(
                 out=acc[:],
                 lhsT=w_codes.bitcast(FP8X4),
                 lhsT_scale=w_scales,
-                rhs=picked[li, a, h][:].bitcast(FP8X4),
+                rhs=picked[li, a, h].bitcast(FP8X4),
                 rhs_scale=picked_planes[li][4 * a :, h * JH : (h + 1) * JH],
                 start=start,
                 stop=stop,
             )
 
-        weighted = {}
-        picked_state = {}
+        messages = {}
 
-        def gather_state(m):
-            picked_state[m] = keep.tile([P, J], F32, name="picked_state%d" % m)
-            nc.vector.tensor_copy(picked_state[m][:], state[m][:].indirect(dst_list[:]))
+        def sums(m, h):
+            cols = slice(m * P, (m + 1) * P)
+            za = psum.tile([P, JH], F32, name="za")
+            ms = psum.tile([P, JH], F32, name="ms")
+            for a in range(PASSES):
+                last = a == PASSES - 1
+                product(za, codes["wa", a][:, cols], scales["wa", a][:, cols], 1, a, h, a == 0, False)
+                product(za, wb_codes[:, a, cols], wb_planes[4 * a :, cols], 0, a, h, False, last)
+                product(ms, codes["wc", a][:, cols], scales["wc", a][:, cols], 0, a, h, a == 0, last)
+            eta = ring.tile([P, JH], F32, name="eta")
+            nc.scalar.activation(eta[:], za[:], ACT.Sigmoid)
+            return eta, ms
 
-        def gate(m):
-            nh, c0 = divmod(m * P, NH)
-            cols = slice(c0, c0 + P)
-            wb_cols = slice(m * P, (m + 1) * P)
-            gated = keep.tile([P, J], F32, name="gated")
+        def first_tile():
+            gated = keep.tile([P, J], F32, name="gated_first", tag="state1")
             for h in range(J // JH):
-                edges = slice(h * JH, (h + 1) * JH)
-                za = psum.tile([P, JH], F32, name="za")
-                ms = psum.tile([P, JH], F32, name="ms")
-                for a in range(PASSES):
-                    last = a == PASSES - 1
-                    product(za, wb_codes[:, a, wb_cols], wb_planes[4 * a :, wb_cols], 0, a, h, a == 0, False)
-                    product(za, codes["wa", a, nh][:, cols], scales["wa", a, nh][:, cols], 1, a, h, False, last)
-                    product(ms, codes["wc", a, nh][:, cols], scales["wc", a, nh][:, cols], 0, a, h, a == 0, last)
-                eta = ring.tile([P, JH], F32, name="eta", bufs=4)
-                nc.scalar.activation(eta[:], za[:], ACT.Sigmoid)
-                message = ring.tile([P, JH], F32, name="message", bufs=4)
+                eta, ms = sums(0, h)
+                nc.vector.tensor_tensor(gated[:, h * JH : (h + 1) * JH], ms[:], eta[:], ALU.mult)
+            work = keep.tile([P, J], F32, name="work")
+            nc.vector.tensor_tensor(work[:], state[0][:].indirect(dst_list[:]), gated[:], ALU.add)
+            messages[0] = keep.tile([P, J], F32, name="messages0", tag="messages0")
+            nc.gpsimd.tensor_tensor(messages[0][:], work[:], edge_weight[:], ALU.mult)
+
+        picked_states = {}
+
+        def gather_state(m, tag, **align):
+            picked_states[m] = keep.tile([P, J], F32, name="picked_state%d" % m, tag=tag, **align)
+            nc.vector.tensor_copy(picked_states[m][:], state[m][:].indirect(dst_list[:]))
+
+        def later_tile(m):
+            picked_state = picked_states[m]
+            work = keep.tile([P, J], F32, name="work")
+            for h in range(J // JH):
+                eta, ms = sums(m, h)
+                message = ring.tile([P, JH], F32, name="message")
                 nc.scalar.copy(message[:], ms[:])
-                nc.gpsimd.tensor_tensor(gated[:, edges], message[:], eta[:], ALU.mult)
-            nc.gpsimd.tensor_tensor(gated[:], gated[:], picked_state[m][:], ALU.add)
-            weighted[m] = keep.tile([P, J], F32, name="weighted%d" % m)
-            nc.gpsimd.tensor_tensor(weighted[m][:], gated[:], edge_weight[:], ALU.mult)
+                nc.gpsimd.tensor_tensor(work[:, h * JH : (h + 1) * JH], message[:], eta[:], ALU.mult)
+            messages[m] = keep.tile([P, J], F32, name="messages%d" % m)
+            if m == TILES - 1:
+                nc.gpsimd.tensor_tensor(messages[m][:], work[:], picked_state[:], ALU.add)
+            else:
+                nc.gpsimd.tensor_tensor(work[:], work[:], picked_state[:], ALU.add)
+                nc.gpsimd.tensor_tensor(messages[m][:], work[:], edge_weight[:], ALU.mult)
 
         def place(m):
             page = pages[m % 2]
-            nc.vector.tensor_copy(page[:].indirect(dst_list[:]), weighted[m][:])
+            if m == TILES - 1:
+                nc.vector.tensor_tensor(page[:].indirect(dst_list[:]), messages[m][:], edge_weight[:], ALU.mult)
+            else:
+                nc.vector.tensor_copy(page[:].indirect(dst_list[:]), messages[m][:])
             nc.sync.dma_start(out[m * P : (m + 1) * P, :], page[:])
 
-        gather_words(0)
+        gather_words(0, J)
+        gather_planes()
         quantise_weights(0)
-        gather_words(1)
-        gather_state(0)
-        gate(0)
+        gather_words(1, J)
         quantise_weights(1)
-        gather_state(1)
-        gate(1)
-        for m in range(2, N // P):
-            gather_state(m)
-            gate(m)
-        for m in range(N // P):
-            place(m)
+        gather_state(1, "grouped_wc1", align_bytes=64)
+        first_tile()
+        gather_state(2, "state1")
+        later_tile(1)
+        place(0)
+        gather_state(3, "messages0")
+        later_tile(2)
+        place(1)
+        later_tile(3)
+        place(2)
+        place(3)

@@ -22,6 +22,7 @@ PASSES = K // K_PASS
 JH = 512
 LIST_COLS = J // 16
 TILES = N // P
+NH = N // 2
 
 
 def tile_list_rgg_L_kernel(
@@ -31,6 +32,7 @@ def tile_list_rgg_L_kernel(
     with ExitStack() as ctx:
         keep = ctx.enter_context(tc.tile_pool(name="keep", bufs=1))
         ring = ctx.enter_context(tc.tile_pool(name="ring", bufs=4))
+        pair = ctx.enter_context(tc.tile_pool(name="pair", bufs=1))
         psum = ctx.enter_context(tc.psum_pool(name="psum", bufs=4))
 
         src_list = keep.tile([P, LIST_COLS], U16, name="src_list")
@@ -59,34 +61,51 @@ def tile_list_rgg_L_kernel(
 
         raw = {}
 
-        def load_weights(a):
+        def load_weight(name, w, a):
+            raw[name, a] = keep.tile([P, PACK, N], F32, name="raw_%s%d" % (name, a))
+            nc.sync.dma_start(
+                raw[name, a][:],
+                w[a * K_PASS : (a + 1) * K_PASS, :].rearrange("(p i) n -> p i n", i=PACK),
+            )
+
+        def load_weight_halves(u):
             for name, w in (("wa", wa), ("wc", wc)):
-                raw[name, a] = keep.tile([P, PACK, N], F32, name="raw_%s%d" % (name, a))
+                raw[name, 1, u] = keep.tile([P, PACK, NH], F32, name="raw_%s1_%d" % (name, u))
                 nc.sync.dma_start(
-                    raw[name, a][:],
-                    w[a * K_PASS : (a + 1) * K_PASS, :].rearrange("(p i) n -> p i n", i=PACK),
+                    raw[name, 1, u][:],
+                    w[K_PASS:, u * NH : (u + 1) * NH].rearrange("(p i) n -> p i n", i=PACK),
                 )
 
         state = [keep.tile([P, T], F32, name="state%d" % m, tag="state%d" % m) for m in range(TILES)]
-        wb_codes = keep.tile([P, PASSES, N], U32, name="wb_codes", align_bytes=64)
+        wb_codes = [keep.tile([P, N], U32, name="wb_codes%d" % a, align_bytes=64) for a in range(PASSES)]
         wb_planes = keep.tile([P, N], U8, name="wb_planes", align_bytes=64)
         edge_weight = keep.tile([P, J], F32, name="edge_weight")
 
-        load_tab(0)
+        def load_wb(a):
+            nc.sync.dma_start(
+                wb_codes[a][:].bitcast(I32), wb_words[a].rearrange("p n i -> p (n i)").bitcast(I32)
+            )
+
+        def load_state(m):
+            nc.sync.dma_start(state[m][:], rT[m * P : (m + 1) * P, :])
+
         nc.sync.dma_start(src_list[:], offs)
         nc.sync.dma_start(dst_list[:], offs2)
+        load_wb(0)
         load_planes(tab_planes, tab_scales)
+        load_tab(0)
+        load_weight("wa", wa, 0)
+        load_weight("wc", wc, 0)
         load_planes(wb_planes, wb_scales)
-        load_weights(0)
         load_tab(1)
-        load_weights(1)
-        nc.sync.dma_start(
-            wb_codes[:].bitcast(I32), wb_words.rearrange("a p n i -> p a (n i)").bitcast(I32)
-        )
-        for m in (1, 0, 2, 3):
-            nc.sync.dma_start(state[m][:], rT[m * P : (m + 1) * P, :])
-            if m == 2:
-                nc.sync.dma_start(edge_weight[:], wgo)
+        load_weight_halves(0)
+        load_wb(1)
+        load_state(0)
+        nc.sync.dma_start(edge_weight[:], wgo)
+        load_state(1)
+        load_weight_halves(1)
+        load_state(2)
+        load_state(3)
 
         picked_planes = []
 
@@ -98,32 +117,52 @@ def tile_list_rgg_L_kernel(
 
         picked = {}
 
-        def gather_words(a, width):
-            for j0 in range(0, J, width):
-                for li in range(2):
-                    words = keep.tile([P, width], U32, name="picked%d%d_%d" % (li, a, j0), align_bytes=64)
-                    cols = lists[li][:, j0 // 16 : (j0 + width) // 16]
-                    nc.vector.tensor_copy(words[:], tab[a][:].indirect(cols))
-                    for j in range(0, width, JH):
-                        picked[li, a, (j0 + j) // JH] = words[:, j : j + JH]
+        def gather_words(a, j0, width, tags):
+            for li in range(2):
+                words = keep.tile([P, width], U32, name="picked%d%d_%d" % (li, a, j0), tag=tags[li], align_bytes=64)
+                cols = lists[li][:, j0 // 16 : (j0 + width) // 16]
+                nc.vector.tensor_copy(words[:], tab[a][:].indirect(cols))
+                for j in range(0, width, JH):
+                    picked[li, a, (j0 + j) // JH] = words[:, j : j + JH]
 
         codes = {}
         scales = {}
 
-        def quantise_weights(a):
+        def interleave(grouped, rows):
+            nc.scalar.copy(
+                grouped.rearrange("p (c n) i -> p c i n", n=4),
+                rows.rearrange("p i (c n) -> p c i n", n=4),
+            )
+
+        def quantise(grouped, label):
+            words = keep.tile([P, N], U32, name="codes_" + label, align_bytes=64)
+            planes = keep.tile([P, N], U8, name="scales_" + label, align_bytes=64)
+            nc.vector.quantize_mx(
+                out=words[:].bitcast(FP8X4),
+                scales=planes[:],
+                in_=grouped[:].rearrange("p n i -> p (n i)"),
+            )
+            return words, planes
+
+        def quantise_first_pass():
             for name in ("wa", "wc"):
-                grouped = keep.tile([P, N, PACK], BF16, name="grouped_%s%d" % (name, a), tag="grouped_%s%d" % (name, a), align_bytes=64)
-                nc.scalar.copy(
-                    grouped[:].rearrange("p (c n) i -> p c i n", n=4),
-                    raw[name, a][:].rearrange("p i (c n) -> p c i n", n=4),
-                )
-                codes[name, a] = keep.tile([P, N], U32, name="codes_%s%d" % (name, a), align_bytes=64)
-                scales[name, a] = keep.tile([P, N], U8, name="scales_%s%d" % (name, a), align_bytes=64)
-                nc.vector.quantize_mx(
-                    out=codes[name, a][:].bitcast(FP8X4),
-                    scales=scales[name, a][:],
-                    in_=grouped[:].rearrange("p n i -> p (n i)"),
-                )
+                grouped = keep.tile([P, N, PACK], BF16, name="grouped_%s0" % name, align_bytes=64)
+                interleave(grouped[:], raw[name, 0][:])
+                words, planes = quantise(grouped, name + "0")
+                for m in range(TILES):
+                    codes[name, 0, m] = words[:, m * P : (m + 1) * P]
+                    scales[name, 0, m] = planes[:, m * P : (m + 1) * P]
+
+        def quantise_second_pass(u):
+            grouped = keep.tile([P, 2 * NH, PACK], BF16, name="grouped_half%d" % u, align_bytes=64)
+            for w, name in enumerate(("wa", "wc")):
+                interleave(grouped[:, w * NH : (w + 1) * NH, :], raw[name, 1, u][:])
+            words, planes = quantise(grouped, "half%d" % u)
+            for w, name in enumerate(("wa", "wc")):
+                for t in range(TILES // 2):
+                    cols = slice(w * NH + t * P, w * NH + (t + 1) * P)
+                    codes[name, 1, 2 * u + t] = words[:, cols]
+                    scales[name, 1, 2 * u + t] = planes[:, cols]
 
         def product(acc, w_codes, w_scales, li, a, h, start, stop):
             nc.tensor.matmul_mx(
@@ -144,43 +183,40 @@ def tile_list_rgg_L_kernel(
             ms = psum.tile([P, JH], F32, name="ms")
             for a in range(PASSES):
                 last = a == PASSES - 1
-                product(za, codes["wa", a][:, cols], scales["wa", a][:, cols], 1, a, h, a == 0, False)
-                product(za, wb_codes[:, a, cols], wb_planes[4 * a :, cols], 0, a, h, False, last)
-                product(ms, codes["wc", a][:, cols], scales["wc", a][:, cols], 0, a, h, a == 0, last)
+                product(za, codes["wa", a, m], scales["wa", a, m], 1, a, h, a == 0, False)
+                product(za, wb_codes[a][:, cols], wb_planes[4 * a :, cols], 0, a, h, False, last)
+                product(ms, codes["wc", a, m], scales["wc", a, m], 0, a, h, a == 0, last)
             eta = ring.tile([P, JH], F32, name="eta")
             nc.scalar.activation(eta[:], za[:], ACT.Sigmoid)
             return eta, ms
 
-        def first_tile():
-            gated = keep.tile([P, J], F32, name="gated_first", tag="state1")
-            for h in range(J // JH):
-                eta, ms = sums(0, h)
-                nc.vector.tensor_tensor(gated[:, h * JH : (h + 1) * JH], ms[:], eta[:], ALU.mult)
-            work = keep.tile([P, J], F32, name="work")
-            nc.vector.tensor_tensor(work[:], state[0][:].indirect(dst_list[:]), gated[:], ALU.add)
-            messages[0] = keep.tile([P, J], F32, name="messages0", tag="messages0")
-            nc.gpsimd.tensor_tensor(messages[0][:], work[:], edge_weight[:], ALU.mult)
-
         picked_states = {}
 
-        def gather_state(m, tag, **align):
-            picked_states[m] = keep.tile([P, J], F32, name="picked_state%d" % m, tag=tag, **align)
+        def gather_state(m):
+            picked_states[m] = keep.tile([P, J], F32, name="picked_state%d" % m)
             nc.vector.tensor_copy(picked_states[m][:], state[m][:].indirect(dst_list[:]))
+
+        def gate(m, h, gated):
+            eta, ms = sums(m, h)
+            message = ring.tile([P, JH], F32, name="message")
+            nc.scalar.copy(message[:], ms[:])
+            nc.gpsimd.tensor_tensor(gated, message[:], eta[:], ALU.mult)
 
         def later_tile(m):
             picked_state = picked_states[m]
-            work = keep.tile([P, J], F32, name="work")
+            work = pair.tile([P, J], F32, name="work")
             for h in range(J // JH):
-                eta, ms = sums(m, h)
-                message = ring.tile([P, JH], F32, name="message")
-                nc.scalar.copy(message[:], ms[:])
-                nc.gpsimd.tensor_tensor(work[:, h * JH : (h + 1) * JH], message[:], eta[:], ALU.mult)
-            messages[m] = keep.tile([P, J], F32, name="messages%d" % m)
+                gate(m, h, work[:, h * JH : (h + 1) * JH])
+            spent = {"tag": "grouped_half1", "align_bytes": 64} if m == 0 else {}
+            messages[m] = keep.tile([P, J], F32, name="messages%d" % m, **spent)
             if m == TILES - 1:
                 nc.gpsimd.tensor_tensor(messages[m][:], work[:], picked_state[:], ALU.add)
             else:
                 nc.gpsimd.tensor_tensor(work[:], work[:], picked_state[:], ALU.add)
                 nc.gpsimd.tensor_tensor(messages[m][:], work[:], edge_weight[:], ALU.mult)
+
+        def store(m):
+            nc.sync.dma_start(out[m * P : (m + 1) * P, :], pages[m % 2][:])
 
         def place(m):
             page = pages[m % 2]
@@ -188,21 +224,19 @@ def tile_list_rgg_L_kernel(
                 nc.vector.tensor_tensor(page[:].indirect(dst_list[:]), messages[m][:], edge_weight[:], ALU.mult)
             else:
                 nc.vector.tensor_copy(page[:].indirect(dst_list[:]), messages[m][:])
-            nc.sync.dma_start(out[m * P : (m + 1) * P, :], page[:])
+            store(m)
 
-        gather_words(0, J)
         gather_planes()
-        quantise_weights(0)
-        gather_words(1, J)
-        quantise_weights(1)
-        gather_state(1, "grouped_wc1", align_bytes=64)
-        first_tile()
-        gather_state(2, "state1")
-        later_tile(1)
-        place(0)
-        gather_state(3, "messages0")
-        later_tile(2)
-        place(1)
-        later_tile(3)
-        place(2)
-        place(3)
+        gather_words(0, 0, J, ("picked_src0", "picked_dst0"))
+        quantise_first_pass()
+        gather_words(1, 0, JH, ("grouped_wc0", "grouped_wa0"))
+        quantise_second_pass(0)
+        gather_words(1, JH, JH, ("grouped_half0", "picked_dst1"))
+        gather_state(0)
+        gather_state(1)
+        quantise_second_pass(1)
+        gather_state(2)
+        gather_state(3)
+        for m in range(TILES):
+            later_tile(m)
+            place(m)

@@ -1,6 +1,7 @@
 from contextlib import ExitStack
 
 import concourse.mybir as mybir
+from concourse.masks import make_identity
 
 K, N, T, J = 1024, 512, 2048, 1024
 FLOPS = 3 * 2 * K * N * J
@@ -22,6 +23,7 @@ PASSES = K // K_PASS
 JH = 512
 LIST_COLS = J // 16
 TILES = N // P
+BLOCKS = JH // P
 NH = N // 2
 
 
@@ -31,9 +33,10 @@ def tile_list_rgg_L_kernel(
     nc = tc.nc
     with ExitStack() as ctx:
         keep = ctx.enter_context(tc.tile_pool(name="keep", bufs=1))
-        ring = ctx.enter_context(tc.tile_pool(name="ring", bufs=4))
+        ring = ctx.enter_context(tc.tile_pool(name="ring", bufs=3))
         pair = ctx.enter_context(tc.tile_pool(name="pair", bufs=1))
-        psum = ctx.enter_context(tc.psum_pool(name="psum", bufs=4))
+        psum = ctx.enter_context(tc.psum_pool(name="psum", bufs=3))
+        turns = ctx.enter_context(tc.psum_pool(name="turns", bufs=1))
 
         src_list = keep.tile([P, LIST_COLS], U16, name="src_list")
         dst_list = keep.tile([P, LIST_COLS], U16, name="dst_list")
@@ -48,6 +51,10 @@ def tile_list_rgg_L_kernel(
 
         tab_planes = keep.tile([P, T], U8, name="tab_planes", align_bytes=64)
         nc.gpsimd.memset(tab_planes[:].bitcast(I32), 0)
+        weight_rows = keep.tile([P, P], F32, name="weight_rows")
+        nc.gpsimd.memset(weight_rows[:], 0.0)
+        identity = keep.tile([P, P], F32, name="identity")
+        make_identity(nc, identity[:])
         pages = [keep.tile([P, T], F32, name="page%d" % i) for i in range(2)]
         for page in pages:
             nc.gpsimd.memset(page[:], 0.0)
@@ -97,15 +104,21 @@ def tile_list_rgg_L_kernel(
         load_weight("wa", wa, 0)
         load_weight("wc", wc, 0)
         load_planes(wb_planes, wb_scales)
+        nc.sync.dma_start(weight_rows[0:BLOCKS, :], wgo[0, 0:JH].rearrange("(b j) -> b j", j=P))
         load_tab(1)
         load_weight_halves(0)
         load_wb(1)
         load_state(0)
-        nc.sync.dma_start(edge_weight[:], wgo)
         load_state(1)
-        load_weight_halves(1)
         load_state(2)
         load_state(3)
+        load_weight_halves(1)
+        nc.sync.dma_start(edge_weight[:], wgo)
+
+        turned_weight = turns.tile([P, JH], F32, name="turned")
+        nc.tensor.transpose(turned_weight[:, 0:P], weight_rows[:], identity[:])
+        weight_cols = keep.tile([P, BLOCKS], F32, name="weight_cols")
+        nc.scalar.copy(weight_cols[:], turned_weight[:, 0:BLOCKS])
 
         picked_planes = []
 
@@ -207,13 +220,34 @@ def tile_list_rgg_L_kernel(
             work = pair.tile([P, J], F32, name="work")
             for h in range(J // JH):
                 gate(m, h, work[:, h * JH : (h + 1) * JH])
-            spent = {"tag": "grouped_half1", "align_bytes": 64} if m == 0 else {}
-            messages[m] = keep.tile([P, J], F32, name="messages%d" % m, **spent)
+            messages[m] = keep.tile([P, J], F32, name="messages%d" % m)
             if m == TILES - 1:
                 nc.gpsimd.tensor_tensor(messages[m][:], work[:], picked_state[:], ALU.add)
             else:
                 nc.gpsimd.tensor_tensor(work[:], work[:], picked_state[:], ALU.add)
                 nc.gpsimd.tensor_tensor(messages[m][:], work[:], edge_weight[:], ALU.mult)
+
+        def mixed_tile(m):
+            messages[m] = keep.tile([P, J], F32, name="messages%d" % m)
+            work = pair.tile([P, J], F32, name="work")
+            for h in range(J // JH):
+                gate(m, h, work[:, h * JH : (h + 1) * JH])
+            turned = turns.tile([P, JH], F32, name="turned")
+            for b in range(BLOCKS):
+                cols = slice(b * P, (b + 1) * P)
+                nc.tensor.matmul(turned[:, cols], picked_states[m][:, cols], identity[:], start=True, stop=False, is_transpose=True)
+                nc.tensor.matmul(turned[:, cols], work[:, cols], identity[:], start=False, stop=True, is_transpose=True)
+            weighted = ring.tile([P, JH], F32, name="weighted")
+            for b in range(BLOCKS):
+                cols = slice(b * P, (b + 1) * P)
+                nc.scalar.activation(weighted[:, cols], turned[:, cols], ACT.Copy, scale=weight_cols[:, b : b + 1])
+            back = turns.tile([P, JH], F32, name="back")
+            for b in range(BLOCKS):
+                cols = slice(b * P, (b + 1) * P)
+                nc.tensor.transpose(back[:, cols], weighted[:, cols], identity[:])
+            nc.scalar.copy(messages[m][:, :JH], back[:])
+            nc.gpsimd.tensor_tensor(work[:, JH:], work[:, JH:], picked_states[m][:, JH:], ALU.add)
+            nc.gpsimd.tensor_tensor(messages[m][:, JH:], work[:, JH:], edge_weight[:, JH:], ALU.mult)
 
         def store(m):
             nc.sync.dma_start(out[m * P : (m + 1) * P, :], pages[m % 2][:])
@@ -234,9 +268,12 @@ def tile_list_rgg_L_kernel(
         gather_words(1, JH, JH, ("grouped_half0", "picked_dst1"))
         gather_state(0)
         gather_state(1)
-        quantise_second_pass(1)
         gather_state(2)
         gather_state(3)
+        quantise_second_pass(1)
         for m in range(TILES):
-            later_tile(m)
+            if m in (1, 2):
+                mixed_tile(m)
+            else:
+                later_tile(m)
             place(m)

@@ -33,7 +33,7 @@ def tile_list_rgg_L_kernel(
     nc = tc.nc
     with ExitStack() as ctx:
         keep = ctx.enter_context(tc.tile_pool(name="keep", bufs=1))
-        ring = ctx.enter_context(tc.tile_pool(name="ring", bufs=3))
+        ring = ctx.enter_context(tc.tile_pool(name="ring", bufs=8))
         pair = ctx.enter_context(tc.tile_pool(name="pair", bufs=1))
         psum = ctx.enter_context(tc.psum_pool(name="psum", bufs=3))
         turns = ctx.enter_context(tc.psum_pool(name="turns", bufs=1))
@@ -104,16 +104,17 @@ def tile_list_rgg_L_kernel(
         load_weight("wa", wa, 0)
         load_weight("wc", wc, 0)
         load_planes(wb_planes, wb_scales)
-        nc.sync.dma_start(weight_rows[0:BLOCKS, :], wgo[0, 0:JH].rearrange("(b j) -> b j", j=P))
+        nc.sync.dma_start(weight_rows[0:BLOCKS, :], wgo[0, JH:].rearrange("(b j) -> b j", j=P))
         load_tab(1)
         load_weight_halves(0)
         load_wb(1)
         load_state(0)
         load_state(1)
         load_state(2)
-        load_state(3)
+        nc.sync.dma_start(edge_weight[:, :JH], wgo[:, :JH])
         load_weight_halves(1)
-        nc.sync.dma_start(edge_weight[:], wgo)
+        load_state(3)
+        nc.sync.dma_start(edge_weight[:, JH:], wgo[:, JH:])
 
         turned_weight = turns.tile([P, JH], F32, name="turned")
         nc.tensor.transpose(turned_weight[:, 0:P], weight_rows[:], identity[:])
@@ -227,17 +228,16 @@ def tile_list_rgg_L_kernel(
                 nc.gpsimd.tensor_tensor(work[:], work[:], picked_state[:], ALU.add)
                 nc.gpsimd.tensor_tensor(messages[m][:], work[:], edge_weight[:], ALU.mult)
 
-        def mixed_tile(m):
-            messages[m] = keep.tile([P, J], F32, name="messages%d" % m)
-            work = pair.tile([P, J], F32, name="work")
-            for h in range(J // JH):
-                gate(m, h, work[:, h * JH : (h + 1) * JH])
+        first, second = slice(0, JH), slice(JH, J)
+
+        def finish_by_transposes(m, gated, result):
             turned = turns.tile([P, JH], F32, name="turned")
             for b in range(BLOCKS):
                 cols = slice(b * P, (b + 1) * P)
-                nc.tensor.matmul(turned[:, cols], picked_states[m][:, cols], identity[:], start=True, stop=False, is_transpose=True)
-                nc.tensor.matmul(turned[:, cols], work[:, cols], identity[:], start=False, stop=True, is_transpose=True)
-            weighted = ring.tile([P, JH], F32, name="weighted")
+                picked_cols = slice(JH + b * P, JH + (b + 1) * P)
+                nc.tensor.matmul(turned[:, cols], picked_states[m][:, picked_cols], identity[:], start=True, stop=False, is_transpose=True)
+                nc.tensor.matmul(turned[:, cols], gated[:, cols], identity[:], start=False, stop=True, is_transpose=True)
+            weighted = keep.tile([P, JH], F32, name="weighted")
             for b in range(BLOCKS):
                 cols = slice(b * P, (b + 1) * P)
                 nc.scalar.activation(weighted[:, cols], turned[:, cols], ACT.Copy, scale=weight_cols[:, b : b + 1])
@@ -245,9 +245,32 @@ def tile_list_rgg_L_kernel(
             for b in range(BLOCKS):
                 cols = slice(b * P, (b + 1) * P)
                 nc.tensor.transpose(back[:, cols], weighted[:, cols], identity[:])
-            nc.scalar.copy(messages[m][:, :JH], back[:])
-            nc.gpsimd.tensor_tensor(work[:, JH:], work[:, JH:], picked_states[m][:, JH:], ALU.add)
-            nc.gpsimd.tensor_tensor(messages[m][:, JH:], work[:, JH:], edge_weight[:, JH:], ALU.mult)
+            nc.scalar.copy(result, back[:])
+
+        def finish_on_gpsimd(m, gated, result):
+            nc.gpsimd.tensor_tensor(gated, gated, picked_states[m][:, first], ALU.add)
+            nc.gpsimd.tensor_tensor(result, gated, edge_weight[:, first], ALU.mult)
+
+        def mixed_tile(m):
+            messages[m] = keep.tile([P, J], F32, name="messages%d" % m)
+            work = pair.tile([P, J], F32, name="work")
+            gate(m, 1, work[:, second])
+            finish_by_transposes(m, work[:, second], messages[m][:, second])
+            gate(m, 0, work[:, first])
+            finish_on_gpsimd(m, work[:, first], messages[m][:, first])
+
+        def first_tile():
+            work = pair.tile([P, JH], F32, name="work")
+            gate(0, 0, work[:])
+            early = keep.tile([P, JH], F32, name="early")
+            finish_on_gpsimd(0, work[:], early[:])
+            nc.vector.tensor_copy(pages[0][:].indirect(dst_list[:, : JH // 16]), early[:])
+            gated = keep.tile([P, JH], F32, name="gated")
+            gate(0, 1, gated[:])
+            late = keep.tile([P, JH], F32, name="late", tag="grouped_half1", align_bytes=64)
+            finish_by_transposes(0, gated[:], late[:])
+            nc.vector.tensor_copy(pages[0][:].indirect(dst_list[:, JH // 16 :]), late[:])
+            store(0)
 
         def store(m):
             nc.sync.dma_start(out[m * P : (m + 1) * P, :], pages[m % 2][:])
@@ -269,9 +292,10 @@ def tile_list_rgg_L_kernel(
         gather_state(0)
         gather_state(1)
         gather_state(2)
-        gather_state(3)
         quantise_second_pass(1)
-        for m in range(TILES):
+        gather_state(3)
+        first_tile()
+        for m in range(1, TILES):
             if m in (1, 2):
                 mixed_tile(m)
             else:

@@ -49,8 +49,9 @@ def tile_list_rgg_L_kernel(
                     scales[:, 4 * q : 4 * q + 4, :].bitcast(I32),
                 )
 
-        tab_planes = keep.tile([P, T], U8, name="tab_planes", align_bytes=64)
-        nc.gpsimd.memset(tab_planes[:].bitcast(I32), 0)
+        scale_rows = keep.tile([P, T], U8, name="scale_rows", align_bytes=64)
+        nc.gpsimd.memset(scale_rows[32:64, :].bitcast(I32), 0)
+        nc.gpsimd.memset(scale_rows[64:128, :].bitcast(I32), 0)
         weight_rows = keep.tile([P, P], F32, name="weight_rows")
         nc.gpsimd.memset(weight_rows[:], 0.0)
         identity = keep.tile([P, P], F32, name="identity")
@@ -98,8 +99,9 @@ def tile_list_rgg_L_kernel(
 
         nc.sync.dma_start(src_list[:], offs)
         nc.sync.dma_start(dst_list[:], offs2)
-        load_wb(0)
-        load_planes(tab_planes, tab_scales)
+        nc.sync.dma_start(
+            scale_rows[0:32, :].bitcast(I32), tab_scales.rearrange("a q t -> (a q) t").bitcast(I32)
+        )
         load_tab(0)
         load_weight("wa", wa, 0)
         load_weight("wc", wc, 0)
@@ -107,6 +109,7 @@ def tile_list_rgg_L_kernel(
         nc.sync.dma_start(weight_rows[0:BLOCKS, :], wgo[0, JH:].rearrange("(b j) -> b j", j=P))
         load_tab(1)
         load_weight_halves(0)
+        load_wb(0)
         load_wb(1)
         load_state(0)
         load_state(1)
@@ -121,13 +124,18 @@ def tile_list_rgg_L_kernel(
         weight_cols = keep.tile([P, BLOCKS], F32, name="weight_cols")
         nc.scalar.copy(weight_cols[:], turned_weight[:, 0:BLOCKS])
 
-        picked_planes = []
+        picked_planes = [keep.tile([P, 2 * J], U8, name="picked_planes%d" % a, align_bytes=64) for a in range(PASSES)]
 
         def gather_planes():
+            picked_rows = keep.tile([P, 2 * J], U8, name="picked_rows", align_bytes=64)
             for li in range(2):
-                planes = keep.tile([P, J], U8, name="picked_planes%d" % li, align_bytes=64)
-                nc.vector.tensor_copy(planes[:], tab_planes[:].indirect(lists[li][:]))
-                picked_planes.append(planes)
+                nc.vector.tensor_copy(picked_rows[:, li * J : (li + 1) * J], scale_rows[:].indirect(lists[li][:]))
+            for a in range(PASSES):
+                for q in range(4):
+                    nc.gpsimd.dma_start(
+                        picked_planes[a][32 * q : 32 * q + 4, :].bitcast(I32),
+                        picked_rows[16 * a + 4 * q : 16 * a + 4 * q + 4, :].bitcast(I32),
+                    )
 
         picked = {}
 
@@ -184,7 +192,7 @@ def tile_list_rgg_L_kernel(
                 lhsT=w_codes.bitcast(FP8X4),
                 lhsT_scale=w_scales,
                 rhs=picked[li, a, h].bitcast(FP8X4),
-                rhs_scale=picked_planes[li][4 * a :, h * JH : (h + 1) * JH],
+                rhs_scale=picked_planes[a][:, li * J + h * JH : li * J + (h + 1) * JH],
                 start=start,
                 stop=stop,
             )

@@ -44,7 +44,7 @@ def tile_list_rgg_L_kernel(
 
         def load_planes(planes, scales):
             for q in range(4):
-                nc.sync.dma_start(
+                nc.gpsimd.dma_start(
                     planes[32 * q : 32 * q + 4 * PASSES, :].bitcast(I32),
                     scales[:, 4 * q : 4 * q + 4, :].bitcast(I32),
                 )
@@ -52,8 +52,8 @@ def tile_list_rgg_L_kernel(
         scale_rows = keep.tile([P, T], U8, name="scale_rows", align_bytes=64)
         nc.gpsimd.memset(scale_rows[32:64, :].bitcast(I32), 0)
         nc.gpsimd.memset(scale_rows[64:128, :].bitcast(I32), 0)
-        weight_rows = keep.tile([P, P], F32, name="weight_rows")
-        nc.gpsimd.memset(weight_rows[:], 0.0)
+        wb_planes = keep.tile([P, N], U8, name="wb_planes", align_bytes=64)
+        load_planes(wb_planes, wb_scales)
         identity = keep.tile([P, P], F32, name="identity")
         make_identity(nc, identity[:])
         pages = [keep.tile([P, T], F32, name="page%d" % i) for i in range(2)]
@@ -85,14 +85,8 @@ def tile_list_rgg_L_kernel(
                 )
 
         state = [keep.tile([P, T], F32, name="state%d" % m, tag="state%d" % m) for m in range(TILES)]
-        wb_codes = [keep.tile([P, N], U32, name="wb_codes%d" % a, align_bytes=64) for a in range(PASSES)]
-        wb_planes = keep.tile([P, N], U8, name="wb_planes", align_bytes=64)
+        wb_codes = keep.tile([P, PASSES, N], U32, name="wb_codes", align_bytes=64)
         edge_weight = keep.tile([P, J], F32, name="edge_weight")
-
-        def load_wb(a):
-            nc.sync.dma_start(
-                wb_codes[a][:].bitcast(I32), wb_words[a].rearrange("p n i -> p (n i)").bitcast(I32)
-            )
 
         def load_state(m):
             nc.sync.dma_start(state[m][:], rT[m * P : (m + 1) * P, :])
@@ -105,37 +99,41 @@ def tile_list_rgg_L_kernel(
         load_tab(0)
         load_weight("wa", wa, 0)
         load_weight("wc", wc, 0)
-        load_planes(wb_planes, wb_scales)
-        nc.sync.dma_start(weight_rows[0:BLOCKS, :], wgo[0, JH:].rearrange("(b j) -> b j", j=P))
         load_tab(1)
-        load_weight_halves(0)
-        load_wb(0)
-        load_wb(1)
-        load_state(0)
-        load_state(1)
-        load_state(2)
-        nc.sync.dma_start(edge_weight[:, :JH], wgo[:, :JH])
-        load_weight_halves(1)
-        load_state(3)
-        nc.sync.dma_start(edge_weight[:, JH:], wgo[:, JH:])
-
-        turned_weight = turns.tile([P, JH], F32, name="turned")
-        nc.tensor.transpose(turned_weight[:, 0:P], weight_rows[:], identity[:])
-        weight_cols = keep.tile([P, BLOCKS], F32, name="weight_cols")
-        nc.scalar.copy(weight_cols[:], turned_weight[:, 0:BLOCKS])
 
         picked_planes = [keep.tile([P, 2 * J], U8, name="picked_planes%d" % a, align_bytes=64) for a in range(PASSES)]
 
-        def gather_planes():
-            picked_rows = keep.tile([P, 2 * J], U8, name="picked_rows", align_bytes=64)
-            for li in range(2):
-                nc.vector.tensor_copy(picked_rows[:, li * J : (li + 1) * J], scale_rows[:].indirect(lists[li][:]))
-            for a in range(PASSES):
-                for q in range(4):
-                    nc.gpsimd.dma_start(
-                        picked_planes[a][32 * q : 32 * q + 4, :].bitcast(I32),
-                        picked_rows[16 * a + 4 * q : 16 * a + 4 * q + 4, :].bitcast(I32),
-                    )
+        picked_rows = keep.tile([P, 2 * J], U8, name="picked_rows", align_bytes=64)
+        for li in range(2):
+            nc.vector.tensor_copy(picked_rows[:, li * J : (li + 1) * J], scale_rows[:].indirect(lists[li][:]))
+
+        def move_planes(a):
+            for q in range(4):
+                nc.sync.dma_start(
+                    picked_planes[a][32 * q : 32 * q + 4, :].bitcast(I32),
+                    picked_rows[16 * a + 4 * q : 16 * a + 4 * q + 4, :].bitcast(I32),
+                )
+
+        move_planes(0)
+        load_weight_halves(0)
+        nc.sync.dma_start(
+            wb_codes[:].bitcast(I32), wb_words.rearrange("a p n i -> p a (n i)").bitcast(I32)
+        )
+        move_planes(1)
+        load_state(0)
+        load_state(1)
+        load_state(2)
+        nc.sync.dma_start(edge_weight[:], wgo)
+        load_weight_halves(1)
+        load_state(3)
+
+        turned_weight = turns.tile([P, JH], F32, name="turned")
+        for b in range(BLOCKS):
+            nc.tensor.transpose(
+                turned_weight[:, b * P : (b + 1) * P], edge_weight[:, JH + b * P : JH + (b + 1) * P], identity[:]
+            )
+        weight_cols = keep.tile([P, BLOCKS], F32, name="weight_cols")
+        nc.scalar.copy(weight_cols[:], turned_weight[:, 0:JH:P])
 
         picked = {}
 
@@ -206,7 +204,7 @@ def tile_list_rgg_L_kernel(
             for a in range(PASSES):
                 last = a == PASSES - 1
                 product(za, codes["wa", a, m], scales["wa", a, m], 1, a, h, a == 0, False)
-                product(za, wb_codes[a][:, cols], wb_planes[4 * a :, cols], 0, a, h, False, last)
+                product(za, wb_codes[:, a, cols], wb_planes[4 * a :, cols], 0, a, h, False, last)
                 product(ms, codes["wc", a, m], scales["wc", a, m], 0, a, h, a == 0, last)
             eta = ring.tile([P, JH], F32, name="eta")
             nc.scalar.activation(eta[:], za[:], ACT.Sigmoid)
@@ -273,7 +271,7 @@ def tile_list_rgg_L_kernel(
             early = keep.tile([P, JH], F32, name="early")
             finish_on_gpsimd(0, work[:], early[:])
             nc.vector.tensor_copy(pages[0][:].indirect(dst_list[:, : JH // 16]), early[:])
-            gated = keep.tile([P, JH], F32, name="gated")
+            gated = pair.tile([P, JH], F32, name="work")
             gate(0, 1, gated[:])
             late = keep.tile([P, JH], F32, name="late", tag="grouped_half1", align_bytes=64)
             finish_by_transposes(0, gated[:], late[:])
@@ -291,7 +289,6 @@ def tile_list_rgg_L_kernel(
                 nc.vector.tensor_copy(page[:].indirect(dst_list[:]), messages[m][:])
             store(m)
 
-        gather_planes()
         gather_words(0, 0, J, ("picked_src0", "picked_dst0"))
         quantise_first_pass()
         gather_words(1, 0, JH, ("grouped_wc0", "grouped_wa0"))

@@ -33,7 +33,7 @@ def tile_list_rgg_L_kernel(
     nc = tc.nc
     with ExitStack() as ctx:
         keep = ctx.enter_context(tc.tile_pool(name="keep", bufs=1))
-        ring = ctx.enter_context(tc.tile_pool(name="ring", bufs=8))
+        ring = ctx.enter_context(tc.tile_pool(name="ring", bufs=6))
         pair = ctx.enter_context(tc.tile_pool(name="pair", bufs=1))
         psum = ctx.enter_context(tc.psum_pool(name="psum", bufs=3))
         turns = ctx.enter_context(tc.psum_pool(name="turns", bufs=1))
@@ -91,11 +91,11 @@ def tile_list_rgg_L_kernel(
         def load_state(m):
             nc.sync.dma_start(state[m][:], rT[m * P : (m + 1) * P, :])
 
-        nc.sync.dma_start(src_list[:], offs)
-        nc.sync.dma_start(dst_list[:], offs2)
         nc.sync.dma_start(
             scale_rows[0:32, :].bitcast(I32), tab_scales.rearrange("a q t -> (a q) t").bitcast(I32)
         )
+        nc.sync.dma_start(src_list[:], offs)
+        nc.sync.dma_start(dst_list[:], offs2)
         load_tab(0)
         load_weight("wa", wa, 0)
         load_weight("wc", wc, 0)
@@ -122,9 +122,9 @@ def tile_list_rgg_L_kernel(
         move_planes(1)
         load_state(0)
         load_state(1)
+        load_weight_halves(1)
         load_state(2)
         nc.sync.dma_start(edge_weight[:], wgo)
-        load_weight_halves(1)
         load_state(3)
 
         turned_weight = turns.tile([P, JH], F32, name="turned")
@@ -174,7 +174,7 @@ def tile_list_rgg_L_kernel(
                     scales[name, 0, m] = planes[:, m * P : (m + 1) * P]
 
         def quantise_second_pass(u):
-            grouped = keep.tile([P, 2 * NH, PACK], BF16, name="grouped_half%d" % u, align_bytes=64)
+            grouped = keep.tile([P, 2 * NH, PACK], BF16, name="grouped_half%d" % u, tag="grouped_half%d" % u, align_bytes=64)
             for w, name in enumerate(("wa", "wc")):
                 interleave(grouped[:, w * NH : (w + 1) * NH, :], raw[name, 1, u][:])
             words, planes = quantise(grouped, "half%d" % u)
@@ -197,7 +197,7 @@ def tile_list_rgg_L_kernel(
 
         messages = {}
 
-        def sums(m, h):
+        def sums(m, h, eta):
             cols = slice(m * P, (m + 1) * P)
             za = psum.tile([P, JH], F32, name="za")
             ms = psum.tile([P, JH], F32, name="ms")
@@ -206,9 +206,8 @@ def tile_list_rgg_L_kernel(
                 product(za, codes["wa", a, m], scales["wa", a, m], 1, a, h, a == 0, False)
                 product(za, wb_codes[:, a, cols], wb_planes[4 * a :, cols], 0, a, h, False, last)
                 product(ms, codes["wc", a, m], scales["wc", a, m], 0, a, h, a == 0, last)
-            eta = ring.tile([P, JH], F32, name="eta")
-            nc.scalar.activation(eta[:], za[:], ACT.Sigmoid)
-            return eta, ms
+            nc.scalar.activation(eta, za[:], ACT.Sigmoid)
+            return ms
 
         picked_states = {}
 
@@ -217,10 +216,14 @@ def tile_list_rgg_L_kernel(
             nc.vector.tensor_copy(picked_states[m][:], state[m][:].indirect(dst_list[:]))
 
         def gate(m, h, gated):
-            eta, ms = sums(m, h)
-            message = ring.tile([P, JH], F32, name="message")
-            nc.scalar.copy(message[:], ms[:])
-            nc.gpsimd.tensor_tensor(gated, message[:], eta[:], ALU.mult)
+            if m == 1:
+                eta, message = after_quantise[:, 1 + 2 * h, :], after_quantise[:, 2 + 2 * h, :]
+            else:
+                eta = ring.tile([P, JH], F32, name="eta")[:]
+                message = ring.tile([P, JH], F32, name="message")[:]
+            ms = sums(m, h, eta)
+            nc.scalar.copy(message, ms[:])
+            nc.gpsimd.tensor_tensor(gated, message, eta, ALU.mult)
 
         def later_tile(m):
             picked_state = picked_states[m]
@@ -268,12 +271,12 @@ def tile_list_rgg_L_kernel(
         def first_tile():
             work = pair.tile([P, JH], F32, name="work")
             gate(0, 0, work[:])
-            early = keep.tile([P, JH], F32, name="early")
-            finish_on_gpsimd(0, work[:], early[:])
-            nc.vector.tensor_copy(pages[0][:].indirect(dst_list[:, : JH // 16]), early[:])
-            gated = pair.tile([P, JH], F32, name="work")
+            gated = keep.tile([P, JH], F32, name="gated")
             gate(0, 1, gated[:])
-            late = keep.tile([P, JH], F32, name="late", tag="grouped_half1", align_bytes=64)
+            early = after_quantise[:, 0, :]
+            finish_on_gpsimd(0, work[:], early)
+            nc.vector.tensor_copy(pages[0][:].indirect(dst_list[:, : JH // 16]), early)
+            late = keep.tile([P, JH], F32, name="late")
             finish_by_transposes(0, gated[:], late[:])
             nc.vector.tensor_copy(pages[0][:].indirect(dst_list[:, JH // 16 :]), late[:])
             store(0)
@@ -296,8 +299,9 @@ def tile_list_rgg_L_kernel(
         gather_words(1, JH, JH, ("grouped_half0", "picked_dst1"))
         gather_state(0)
         gather_state(1)
-        gather_state(2)
         quantise_second_pass(1)
+        after_quantise = keep.tile([P, 5, JH], F32, name="after_quantise", tag="grouped_half1", align_bytes=64)
+        gather_state(2)
         gather_state(3)
         first_tile()
         for m in range(1, TILES):

@@ -50,8 +50,8 @@ def tile_list_rgg_L_kernel(
                 )
 
         scale_rows = keep.tile([P, T], U8, name="scale_rows", align_bytes=64)
-        nc.gpsimd.memset(scale_rows[32:64, :].bitcast(I32), 0)
-        nc.gpsimd.memset(scale_rows[64:128, :].bitcast(I32), 0)
+        nc.vector.memset(scale_rows[32:64, :].bitcast(I32), 0)
+        nc.vector.memset(scale_rows[64:128, :].bitcast(I32), 0)
         wb_planes = keep.tile([P, N], U8, name="wb_planes", align_bytes=64)
         load_planes(wb_planes, wb_scales)
         identity = keep.tile([P, P], F32, name="identity")
@@ -76,16 +76,22 @@ def tile_list_rgg_L_kernel(
                 w[a * K_PASS : (a + 1) * K_PASS, :].rearrange("(p i) n -> p i n", i=PACK),
             )
 
-        def load_weight_halves(u):
-            for name, w in (("wa", wa), ("wc", wc)):
-                raw[name, 1, u] = keep.tile([P, PACK, NH], F32, name="raw_%s1_%d" % (name, u))
-                nc.sync.dma_start(
-                    raw[name, 1, u][:],
-                    w[K_PASS:, u * NH : (u + 1) * NH].rearrange("(p i) n -> p i n", i=PACK),
-                )
+        def load_weight_half(name, w, u):
+            raw[name, 1, u] = keep.tile([P, PACK, NH], F32, name="raw_%s1_%d" % (name, u), tag="raw_%s1_%d" % (name, u))
+            nc.sync.dma_start(
+                raw[name, 1, u][:],
+                w[K_PASS:, u * NH : (u + 1) * NH].rearrange("(p i) n -> p i n", i=PACK),
+            )
 
-        state = [keep.tile([P, T], F32, name="state%d" % m, tag="state%d" % m) for m in range(TILES)]
-        wb_codes = keep.tile([P, PASSES, N], U32, name="wb_codes", align_bytes=64)
+        state = [keep.tile([P, T], F32, name="state%d" % m, tag="state%d" % m, align_bytes=64) for m in range(TILES)]
+        wb_codes = [keep.tile([P, PASSES, NH], U32, name="wb_codes%d" % u, align_bytes=64) for u in range(2)]
+
+        def load_wb_half(u):
+            nc.sync.dma_start(
+                wb_codes[u][:].bitcast(I32),
+                wb_words[:, :, u * NH : (u + 1) * NH, :].rearrange("a p n i -> p a (n i)").bitcast(I32),
+            )
+
         edge_weight = keep.tile([P, J], F32, name="edge_weight")
 
         def load_state(m):
@@ -115,16 +121,17 @@ def tile_list_rgg_L_kernel(
                 )
 
         move_planes(0)
-        load_weight_halves(0)
-        nc.sync.dma_start(
-            wb_codes[:].bitcast(I32), wb_words.rearrange("a p n i -> p a (n i)").bitcast(I32)
-        )
+        load_weight_half("wa", wa, 0)
+        load_weight_half("wc", wc, 0)
+        load_wb_half(0)
         move_planes(1)
         load_state(0)
+        load_weight_half("wa", wa, 1)
         load_state(1)
-        load_weight_halves(1)
+        load_weight_half("wc", wc, 1)
         load_state(2)
         nc.sync.dma_start(edge_weight[:], wgo)
+        load_wb_half(1)
         load_state(3)
 
         turned_weight = turns.tile([P, JH], F32, name="turned")
@@ -154,8 +161,8 @@ def tile_list_rgg_L_kernel(
                 rows.rearrange("p i (c n) -> p c i n", n=4),
             )
 
-        def quantise(grouped, label):
-            words = keep.tile([P, N], U32, name="codes_" + label, align_bytes=64)
+        def quantise(grouped, label, tag=None):
+            words = keep.tile([P, N], U32, name="codes_" + label, tag=tag or "codes_" + label, align_bytes=64)
             planes = keep.tile([P, N], U8, name="scales_" + label, align_bytes=64)
             nc.vector.quantize_mx(
                 out=words[:].bitcast(FP8X4),
@@ -177,7 +184,7 @@ def tile_list_rgg_L_kernel(
             grouped = keep.tile([P, 2 * NH, PACK], BF16, name="grouped_half%d" % u, tag="grouped_half%d" % u, align_bytes=64)
             for w, name in enumerate(("wa", "wc")):
                 interleave(grouped[:, w * NH : (w + 1) * NH, :], raw[name, 1, u][:])
-            words, planes = quantise(grouped, "half%d" % u)
+            words, planes = quantise(grouped, "half%d" % u, "state1" if u else None)
             for w, name in enumerate(("wa", "wc")):
                 for t in range(TILES // 2):
                     cols = slice(w * NH + t * P, w * NH + (t + 1) * P)
@@ -204,7 +211,7 @@ def tile_list_rgg_L_kernel(
             for a in range(PASSES):
                 last = a == PASSES - 1
                 product(za, codes["wa", a, m], scales["wa", a, m], 1, a, h, a == 0, False)
-                product(za, wb_codes[:, a, cols], wb_planes[4 * a :, cols], 0, a, h, False, last)
+                product(za, wb_codes[m // 2][:, a, (m % 2) * P : (m % 2 + 1) * P], wb_planes[4 * a :, cols], 0, a, h, False, last)
                 product(ms, codes["wc", a, m], scales["wc", a, m], 0, a, h, a == 0, last)
             nc.scalar.activation(eta, za[:], ACT.Sigmoid)
             return ms
@@ -218,6 +225,8 @@ def tile_list_rgg_L_kernel(
         def gate(m, h, gated):
             if m == 1:
                 eta, message = after_quantise[:, 1 + 2 * h, :], after_quantise[:, 2 + 2 * h, :]
+            elif (m, h) == (0, 1):
+                eta, message = after_rounding[:, 0, :], after_rounding[:, 1, :]
             else:
                 eta = ring.tile([P, JH], F32, name="eta")[:]
                 message = ring.tile([P, JH], F32, name="message")[:]
@@ -271,11 +280,11 @@ def tile_list_rgg_L_kernel(
         def first_tile():
             work = pair.tile([P, JH], F32, name="work")
             gate(0, 0, work[:])
-            gated = keep.tile([P, JH], F32, name="gated")
-            gate(0, 1, gated[:])
             early = after_quantise[:, 0, :]
             finish_on_gpsimd(0, work[:], early)
             nc.vector.tensor_copy(pages[0][:].indirect(dst_list[:, : JH // 16]), early)
+            gated = pair.tile([P, JH], F32, name="work")
+            gate(0, 1, gated[:])
             late = keep.tile([P, JH], F32, name="late")
             finish_by_transposes(0, gated[:], late[:])
             nc.vector.tensor_copy(pages[0][:].indirect(dst_list[:, JH // 16 :]), late[:])
@@ -301,6 +310,7 @@ def tile_list_rgg_L_kernel(
         gather_state(1)
         quantise_second_pass(1)
         after_quantise = keep.tile([P, 5, JH], F32, name="after_quantise", tag="grouped_half1", align_bytes=64)
+        after_rounding = keep.tile([P, 2, JH], F32, name="after_rounding", tag="raw_wc1_1")
         gather_state(2)
         gather_state(3)
         first_tile()

@@ -70,14 +70,14 @@ def tile_list_rgg_L_kernel(
         raw = {}
 
         def load_weight(name, w, a):
-            raw[name, a] = keep.tile([P, PACK, N], F32, name="raw_%s%d" % (name, a))
+            raw[name, a] = keep.tile([P, PACK, N], F32, name="raw_%s%d" % (name, a), tag="raw_%s%d" % (name, a), align_bytes=64)
             nc.sync.dma_start(
                 raw[name, a][:],
                 w[a * K_PASS : (a + 1) * K_PASS, :].rearrange("(p i) n -> p i n", i=PACK),
             )
 
         def load_weight_half(name, w, u):
-            raw[name, 1, u] = keep.tile([P, PACK, NH], F32, name="raw_%s1_%d" % (name, u), tag="raw_%s1_%d" % (name, u))
+            raw[name, 1, u] = keep.tile([P, PACK, NH], F32, name="raw_%s1_%d" % (name, u), tag="raw_%s1_%d" % (name, u), align_bytes=64)
             nc.sync.dma_start(
                 raw[name, 1, u][:],
                 w[K_PASS:, u * NH : (u + 1) * NH].rearrange("(p i) n -> p i n", i=PACK),
@@ -130,7 +130,8 @@ def tile_list_rgg_L_kernel(
         load_state(1)
         load_weight_half("wc", wc, 1)
         load_state(2)
-        nc.sync.dma_start(edge_weight[:], wgo)
+        for cols in (slice(0, JH), slice(JH, J)):
+            nc.sync.dma_start(edge_weight[:, cols], wgo[:, cols])
         load_wb_half(1)
         load_state(3)
 
@@ -144,13 +145,13 @@ def tile_list_rgg_L_kernel(
 
         picked = {}
 
-        def gather_words(a, j0, width, tags):
+        def gather_words(a, j0, width, tag):
+            words = keep.tile([P, 2, width], U32, name="picked%d_%d" % (a, j0), tag=tag, align_bytes=64)
             for li in range(2):
-                words = keep.tile([P, width], U32, name="picked%d%d_%d" % (li, a, j0), tag=tags[li], align_bytes=64)
                 cols = lists[li][:, j0 // 16 : (j0 + width) // 16]
-                nc.vector.tensor_copy(words[:], tab[a][:].indirect(cols))
+                nc.vector.tensor_copy(words[:, li, :], tab[a][:].indirect(cols))
                 for j in range(0, width, JH):
-                    picked[li, a, (j0 + j) // JH] = words[:, j : j + JH]
+                    picked[li, a, (j0 + j) // JH] = words[:, li, j : j + JH]
 
         codes = {}
         scales = {}
@@ -234,9 +235,14 @@ def tile_list_rgg_L_kernel(
             nc.scalar.copy(message, ms[:])
             nc.gpsimd.tensor_tensor(gated, message, eta, ALU.mult)
 
+        def work_buffer(m):
+            if m % 2:
+                return keep.tile([P, J], F32, name="odd_work", tag="raw_wc1_1", align_bytes=64)
+            return pair.tile([P, J], F32, name="work")
+
         def later_tile(m):
             picked_state = picked_states[m]
-            work = pair.tile([P, J], F32, name="work")
+            work = work_buffer(m)
             for h in range(J // JH):
                 gate(m, h, work[:, h * JH : (h + 1) * JH])
             messages[m] = keep.tile([P, J], F32, name="messages%d" % m)
@@ -271,7 +277,7 @@ def tile_list_rgg_L_kernel(
 
         def mixed_tile(m):
             messages[m] = keep.tile([P, J], F32, name="messages%d" % m)
-            work = pair.tile([P, J], F32, name="work")
+            work = work_buffer(m)
             gate(m, 1, work[:, second])
             finish_by_transposes(m, work[:, second], messages[m][:, second])
             gate(m, 0, work[:, first])
@@ -301,16 +307,16 @@ def tile_list_rgg_L_kernel(
                 nc.vector.tensor_copy(page[:].indirect(dst_list[:]), messages[m][:])
             store(m)
 
-        gather_words(0, 0, J, ("picked_src0", "picked_dst0"))
+        gather_words(0, 0, J, "picked0")
         quantise_first_pass()
-        gather_words(1, 0, JH, ("grouped_wc0", "grouped_wa0"))
+        gather_words(1, 0, JH, "raw_wc0")
         quantise_second_pass(0)
-        gather_words(1, JH, JH, ("grouped_half0", "picked_dst1"))
+        gather_words(1, JH, JH, "raw_wc1_0")
         gather_state(0)
         gather_state(1)
         quantise_second_pass(1)
         after_quantise = keep.tile([P, 5, JH], F32, name="after_quantise", tag="grouped_half1", align_bytes=64)
-        after_rounding = keep.tile([P, 2, JH], F32, name="after_rounding", tag="raw_wc1_1")
+        after_rounding = keep.tile([P, 2, JH], F32, name="after_rounding", tag="raw_wc1_1", align_bytes=64)
         gather_state(2)
         gather_state(3)
         first_tile()

@@ -126,12 +126,11 @@ def tile_list_rgg_L_kernel(
         load_wb_half(0)
         move_planes(1)
         load_state(0)
-        load_weight_half("wa", wa, 1)
         load_state(1)
-        load_weight_half("wc", wc, 1)
         load_state(2)
-        for cols in (slice(0, JH), slice(JH, J)):
-            nc.sync.dma_start(edge_weight[:, cols], wgo[:, cols])
+        nc.sync.dma_start(edge_weight[:], wgo)
+        load_weight_half("wa", wa, 1)
+        load_weight_half("wc", wc, 1)
         load_wb_half(1)
         load_state(3)
 
@@ -162,8 +161,8 @@ def tile_list_rgg_L_kernel(
                 rows.rearrange("p i (c n) -> p c i n", n=4),
             )
 
-        def quantise(grouped, label, tag=None):
-            words = keep.tile([P, N], U32, name="codes_" + label, tag=tag or "codes_" + label, align_bytes=64)
+        def quantise(grouped, label):
+            words = keep.tile([P, N], U32, name="codes_" + label, align_bytes=64)
             planes = keep.tile([P, N], U8, name="scales_" + label, align_bytes=64)
             nc.vector.quantize_mx(
                 out=words[:].bitcast(FP8X4),
@@ -185,7 +184,7 @@ def tile_list_rgg_L_kernel(
             grouped = keep.tile([P, 2 * NH, PACK], BF16, name="grouped_half%d" % u, tag="grouped_half%d" % u, align_bytes=64)
             for w, name in enumerate(("wa", "wc")):
                 interleave(grouped[:, w * NH : (w + 1) * NH, :], raw[name, 1, u][:])
-            words, planes = quantise(grouped, "half%d" % u, "state1" if u else None)
+            words, planes = quantise(grouped, "half%d" % u)
             for w, name in enumerate(("wa", "wc")):
                 for t in range(TILES // 2):
                     cols = slice(w * NH + t * P, w * NH + (t + 1) * P)
@@ -224,9 +223,7 @@ def tile_list_rgg_L_kernel(
             nc.vector.tensor_copy(picked_states[m][:], state[m][:].indirect(dst_list[:]))
 
         def gate(m, h, gated):
-            if m == 1:
-                eta, message = after_quantise[:, 1 + 2 * h, :], after_quantise[:, 2 + 2 * h, :]
-            elif (m, h) == (0, 1):
+            if (m, h) == (1, 0):
                 eta, message = after_rounding[:, 0, :], after_rounding[:, 1, :]
             else:
                 eta = ring.tile([P, JH], F32, name="eta")[:]
@@ -235,14 +232,9 @@ def tile_list_rgg_L_kernel(
             nc.scalar.copy(message, ms[:])
             nc.gpsimd.tensor_tensor(gated, message, eta, ALU.mult)
 
-        def work_buffer(m):
-            if m % 2:
-                return keep.tile([P, J], F32, name="odd_work", tag="raw_wc1_1", align_bytes=64)
-            return pair.tile([P, J], F32, name="work")
-
         def later_tile(m):
             picked_state = picked_states[m]
-            work = work_buffer(m)
+            work = pair.tile([P, J], F32, name="work")
             for h in range(J // JH):
                 gate(m, h, work[:, h * JH : (h + 1) * JH])
             messages[m] = keep.tile([P, J], F32, name="messages%d" % m)
@@ -277,23 +269,24 @@ def tile_list_rgg_L_kernel(
 
         def mixed_tile(m):
             messages[m] = keep.tile([P, J], F32, name="messages%d" % m)
-            work = work_buffer(m)
+            work = pair.tile([P, J], F32, name="work")
             gate(m, 1, work[:, second])
             finish_by_transposes(m, work[:, second], messages[m][:, second])
-            gate(m, 0, work[:, first])
-            finish_on_gpsimd(m, work[:, first], messages[m][:, first])
+            gated = after_quantise[:, 1, :] if m == 1 else work[:, first]
+            gate(m, 0, gated)
+            finish_on_gpsimd(m, gated, messages[m][:, first])
 
         def first_tile():
             work = pair.tile([P, JH], F32, name="work")
             gate(0, 0, work[:])
-            early = after_quantise[:, 0, :]
+            early = keep.tile([P, JH], F32, name="early")[:]
             finish_on_gpsimd(0, work[:], early)
             nc.vector.tensor_copy(pages[0][:].indirect(dst_list[:, : JH // 16]), early)
             gated = pair.tile([P, JH], F32, name="work")
             gate(0, 1, gated[:])
-            late = keep.tile([P, JH], F32, name="late")
-            finish_by_transposes(0, gated[:], late[:])
-            nc.vector.tensor_copy(pages[0][:].indirect(dst_list[:, JH // 16 :]), late[:])
+            late = after_quantise[:, 0, :]
+            finish_by_transposes(0, gated[:], late)
+            nc.vector.tensor_copy(pages[0][:].indirect(dst_list[:, JH // 16 :]), late)
             store(0)
 
         def store(m):
@@ -314,10 +307,10 @@ def tile_list_rgg_L_kernel(
         gather_words(1, JH, JH, "raw_wc1_0")
         gather_state(0)
         gather_state(1)
-        quantise_second_pass(1)
-        after_quantise = keep.tile([P, 5, JH], F32, name="after_quantise", tag="grouped_half1", align_bytes=64)
-        after_rounding = keep.tile([P, 2, JH], F32, name="after_rounding", tag="raw_wc1_1", align_bytes=64)
         gather_state(2)
+        quantise_second_pass(1)
+        after_quantise = keep.tile([P, 2, JH], F32, name="after_quantise", tag="grouped_half1", align_bytes=64)
+        after_rounding = keep.tile([P, 2, JH], F32, name="after_rounding", tag="raw_wc1_1", align_bytes=64)
         gather_state(3)
         first_tile()
         for m in range(1, TILES):

@@ -144,13 +144,12 @@ def tile_list_rgg_L_kernel(
 
         picked = {}
 
-        def gather_words(a, j0, width, tag):
-            words = keep.tile([P, 2, width], U32, name="picked%d_%d" % (a, j0), tag=tag, align_bytes=64)
-            for li in range(2):
-                cols = lists[li][:, j0 // 16 : (j0 + width) // 16]
-                nc.vector.tensor_copy(words[:, li, :], tab[a][:].indirect(cols))
-                for j in range(0, width, JH):
-                    picked[li, a, (j0 + j) // JH] = words[:, li, j : j + JH]
+        def gather_words(li, a, j0, width, tag):
+            words = keep.tile([P, width], U32, name="picked%d%d_%d" % (li, a, j0), tag=tag, align_bytes=64)
+            cols = lists[li][:, j0 // 16 : (j0 + width) // 16]
+            nc.vector.tensor_copy(words[:], tab[a][:].indirect(cols))
+            for j in range(0, width, JH):
+                picked[li, a, (j0 + j) // JH] = words[:, j : j + JH]
 
         codes = {}
         scales = {}
@@ -162,8 +161,8 @@ def tile_list_rgg_L_kernel(
             )
 
         def quantise(grouped, label):
-            words = keep.tile([P, N], U32, name="codes_" + label, align_bytes=64)
-            planes = keep.tile([P, N], U8, name="scales_" + label, align_bytes=64)
+            words = keep.tile([P, grouped.shape[1]], U32, name="codes_" + label, align_bytes=64)
+            planes = keep.tile([P, grouped.shape[1]], U8, name="scales_" + label, align_bytes=64)
             nc.vector.quantize_mx(
                 out=words[:].bitcast(FP8X4),
                 scales=planes[:],
@@ -172,13 +171,15 @@ def tile_list_rgg_L_kernel(
             return words, planes
 
         def quantise_first_pass():
-            for name in ("wa", "wc"):
-                grouped = keep.tile([P, N, PACK], BF16, name="grouped_%s0" % name, align_bytes=64)
-                interleave(grouped[:], raw[name, 0][:])
-                words, planes = quantise(grouped, name + "0")
+            grouped = keep.tile([P, 2 * N, PACK], BF16, name="grouped_first", align_bytes=64)
+            for w, name in enumerate(("wa", "wc")):
+                interleave(grouped[:, w * N : (w + 1) * N, :], raw[name, 0][:])
+            words, planes = quantise(grouped, "first")
+            for w, name in enumerate(("wa", "wc")):
                 for m in range(TILES):
-                    codes[name, 0, m] = words[:, m * P : (m + 1) * P]
-                    scales[name, 0, m] = planes[:, m * P : (m + 1) * P]
+                    cols = slice(w * N + m * P, w * N + (m + 1) * P)
+                    codes[name, 0, m] = words[:, cols]
+                    scales[name, 0, m] = planes[:, cols]
 
         def quantise_second_pass(u):
             grouped = keep.tile([P, 2 * NH, PACK], BF16, name="grouped_half%d" % u, tag="grouped_half%d" % u, align_bytes=64)
@@ -209,9 +210,10 @@ def tile_list_rgg_L_kernel(
             za = psum.tile([P, JH], F32, name="za")
             ms = psum.tile([P, JH], F32, name="ms")
             for a in range(PASSES):
+                product(za, wb_codes[m // 2][:, a, (m % 2) * P : (m % 2 + 1) * P], wb_planes[4 * a :, cols], 0, a, h, a == 0, False)
+            for a in range(PASSES):
                 last = a == PASSES - 1
-                product(za, codes["wa", a, m], scales["wa", a, m], 1, a, h, a == 0, False)
-                product(za, wb_codes[m // 2][:, a, (m % 2) * P : (m % 2 + 1) * P], wb_planes[4 * a :, cols], 0, a, h, False, last)
+                product(za, codes["wa", a, m], scales["wa", a, m], 1, a, h, False, last)
                 product(ms, codes["wc", a, m], scales["wc", a, m], 0, a, h, a == 0, last)
             nc.scalar.activation(eta, za[:], ACT.Sigmoid)
             return ms
@@ -253,7 +255,7 @@ def tile_list_rgg_L_kernel(
                 picked_cols = slice(JH + b * P, JH + (b + 1) * P)
                 nc.tensor.matmul(turned[:, cols], picked_states[m][:, picked_cols], identity[:], start=True, stop=False, is_transpose=True)
                 nc.tensor.matmul(turned[:, cols], gated[:, cols], identity[:], start=False, stop=True, is_transpose=True)
-            weighted = keep.tile([P, JH], F32, name="weighted")
+            weighted = after_rounding[:, 2, :] if m == 0 else keep.tile([P, JH], F32, name="weighted")
             for b in range(BLOCKS):
                 cols = slice(b * P, (b + 1) * P)
                 nc.scalar.activation(weighted[:, cols], turned[:, cols], ACT.Copy, scale=weight_cols[:, b : b + 1])
@@ -300,17 +302,19 @@ def tile_list_rgg_L_kernel(
                 nc.vector.tensor_copy(page[:].indirect(dst_list[:]), messages[m][:])
             store(m)
 
-        gather_words(0, 0, J, "picked0")
+        gather_words(1, 0, 0, J, "picked_dst0")
+        gather_words(0, 0, 0, J, "picked_src0")
         quantise_first_pass()
-        gather_words(1, 0, JH, "raw_wc0")
+        gather_words(0, 1, 0, JH, "raw_wa0")
+        gather_words(1, 1, 0, J, "raw_wc0")
         quantise_second_pass(0)
-        gather_words(1, JH, JH, "raw_wc1_0")
+        gather_words(0, 1, JH, JH, "raw_wc1_0")
         gather_state(0)
         gather_state(1)
         gather_state(2)
         quantise_second_pass(1)
         after_quantise = keep.tile([P, 2, JH], F32, name="after_quantise", tag="grouped_half1", align_bytes=64)
-        after_rounding = keep.tile([P, 2, JH], F32, name="after_rounding", tag="raw_wc1_1", align_bytes=64)
+        after_rounding = keep.tile([P, 3, JH], F32, name="after_rounding", tag="raw_wc1_1", align_bytes=64)
         gather_state(3)
         first_tile()
         for m in range(1, TILES):

@@ -171,15 +171,13 @@ def tile_list_rgg_L_kernel(
             return words, planes
 
         def quantise_first_pass():
-            grouped = keep.tile([P, 2 * N, PACK], BF16, name="grouped_first", align_bytes=64)
-            for w, name in enumerate(("wa", "wc")):
-                interleave(grouped[:, w * N : (w + 1) * N, :], raw[name, 0][:])
-            words, planes = quantise(grouped, "first")
-            for w, name in enumerate(("wa", "wc")):
+            for name in ("wa", "wc"):
+                grouped = keep.tile([P, N, PACK], BF16, name="grouped_%s0" % name, align_bytes=64)
+                interleave(grouped[:], raw[name, 0][:])
+                words, planes = quantise(grouped, name + "0")
                 for m in range(TILES):
-                    cols = slice(w * N + m * P, w * N + (m + 1) * P)
-                    codes[name, 0, m] = words[:, cols]
-                    scales[name, 0, m] = planes[:, cols]
+                    codes[name, 0, m] = words[:, m * P : (m + 1) * P]
+                    scales[name, 0, m] = planes[:, m * P : (m + 1) * P]
 
         def quantise_second_pass(u):
             grouped = keep.tile([P, 2 * NH, PACK], BF16, name="grouped_half%d" % u, tag="grouped_half%d" % u, align_bytes=64)

@@ -290,7 +290,10 @@ def tile_list_rgg_L_kernel(
             store(0)
 
         def store(m):
-            nc.sync.dma_start(out[m * P : (m + 1) * P, :], pages[m % 2][:])
+            pieces = 2 if m < 2 else 1
+            for c in range(pieces):
+                cols = slice(c * T // pieces, (c + 1) * T // pieces)
+                nc.sync.dma_start(out[m * P : (m + 1) * P, cols], pages[m % 2][:, cols])
 
         def place(m):
             page = pages[m % 2]

@@ -21,6 +21,7 @@ PACK = 4
 K_PASS = P * PACK
 PASSES = K // K_PASS
 JH = 512
+JQ = 256
 LIST_COLS = J // 16
 TILES = N // P
 BLOCKS = JH // P
@@ -33,32 +34,31 @@ def tile_list_rgg_L_kernel(
     nc = tc.nc
     with ExitStack() as ctx:
         keep = ctx.enter_context(tc.tile_pool(name="keep", bufs=1))
-        ring = ctx.enter_context(tc.tile_pool(name="ring", bufs=6))
-        pair = ctx.enter_context(tc.tile_pool(name="pair", bufs=1))
-        psum = ctx.enter_context(tc.psum_pool(name="psum", bufs=3))
-        turns = ctx.enter_context(tc.psum_pool(name="turns", bufs=1))
+        psum = ctx.enter_context(tc.psum_pool(name="psum", bufs=1))
 
         src_list = keep.tile([P, LIST_COLS], U16, name="src_list")
         dst_list = keep.tile([P, LIST_COLS], U16, name="dst_list")
         lists = (src_list, dst_list)
 
-        def load_planes(planes, scales):
-            for q in range(4):
-                nc.gpsimd.dma_start(
-                    planes[32 * q : 32 * q + 4 * PASSES, :].bitcast(I32),
-                    scales[:, 4 * q : 4 * q + 4, :].bitcast(I32),
-                )
-
         scale_rows = keep.tile([P, T], U8, name="scale_rows", align_bytes=64)
         nc.vector.memset(scale_rows[32:64, :].bitcast(I32), 0)
         nc.vector.memset(scale_rows[64:128, :].bitcast(I32), 0)
         wb_planes = keep.tile([P, N], U8, name="wb_planes", align_bytes=64)
-        load_planes(wb_planes, wb_scales)
+        for q in range(4):
+            nc.gpsimd.dma_start(
+                wb_planes[32 * q : 32 * q + 4 * PASSES, :].bitcast(I32),
+                wb_scales[:, 4 * q : 4 * q + 4, :].bitcast(I32),
+            )
         identity = keep.tile([P, P], F32, name="identity")
         make_identity(nc, identity[:])
-        pages = [keep.tile([P, T], F32, name="page%d" % i) for i in range(2)]
-        for page in pages:
+        pages = {}
+
+        def clear_page(m, page):
+            pages[m] = page
             nc.gpsimd.memset(page[:], 0.0)
+
+        clear_page(0, keep.tile([P, T], F32, name="page0"))
+        clear_page(1, keep.tile([P, T], F32, name="page1"))
 
         tab = [keep.tile([P, T], U32, name="tab%d" % a) for a in range(PASSES)]
 
@@ -69,21 +69,16 @@ def tile_list_rgg_L_kernel(
 
         raw = {}
 
-        def load_weight(name, w, a):
-            raw[name, a] = keep.tile([P, PACK, N], F32, name="raw_%s%d" % (name, a), tag="raw_%s%d" % (name, a), align_bytes=64)
-            nc.sync.dma_start(
-                raw[name, a][:],
-                w[a * K_PASS : (a + 1) * K_PASS, :].rearrange("(p i) n -> p i n", i=PACK),
-            )
+        def load_weights(a, u):
+            for name, w in (("wa", wa), ("wc", wc)):
+                label = "raw_%s%d%d" % (name, a, u)
+                raw[name, a, u] = keep.tile([P, PACK, NH], F32, name=label, tag=label, align_bytes=64)
+                nc.sync.dma_start(
+                    raw[name, a, u][:],
+                    w[a * K_PASS : (a + 1) * K_PASS, u * NH : (u + 1) * NH].rearrange("(p i) n -> p i n", i=PACK),
+                )
 
-        def load_weight_half(name, w, u):
-            raw[name, 1, u] = keep.tile([P, PACK, NH], F32, name="raw_%s1_%d" % (name, u), tag="raw_%s1_%d" % (name, u), align_bytes=64)
-            nc.sync.dma_start(
-                raw[name, 1, u][:],
-                w[K_PASS:, u * NH : (u + 1) * NH].rearrange("(p i) n -> p i n", i=PACK),
-            )
-
-        state = [keep.tile([P, T], F32, name="state%d" % m, tag="state%d" % m, align_bytes=64) for m in range(TILES)]
+        state = [keep.tile([P, T], F32, name="state%d" % m, align_bytes=64) for m in range(TILES)]
         wb_codes = [keep.tile([P, PASSES, NH], U32, name="wb_codes%d" % u, align_bytes=64) for u in range(2)]
 
         def load_wb_half(u):
@@ -92,7 +87,8 @@ def tile_list_rgg_L_kernel(
                 wb_words[:, :, u * NH : (u + 1) * NH, :].rearrange("a p n i -> p a (n i)").bitcast(I32),
             )
 
-        edge_weight = keep.tile([P, J], F32, name="edge_weight")
+        edge_weight = keep.tile([P, JH], F32, name="edge_weight")
+        weight_rows = keep.tile([P, P], F32, name="weight_rows")
 
         def load_state(m):
             nc.sync.dma_start(state[m][:], rT[m * P : (m + 1) * P, :])
@@ -103,12 +99,10 @@ def tile_list_rgg_L_kernel(
         nc.sync.dma_start(src_list[:], offs)
         nc.sync.dma_start(dst_list[:], offs2)
         load_tab(0)
-        load_weight("wa", wa, 0)
-        load_weight("wc", wc, 0)
+        load_weights(0, 0)
         load_tab(1)
 
         picked_planes = [keep.tile([P, 2 * J], U8, name="picked_planes%d" % a, align_bytes=64) for a in range(PASSES)]
-
         picked_rows = keep.tile([P, 2 * J], U8, name="picked_rows", align_bytes=64)
         for li in range(2):
             nc.vector.tensor_copy(picked_rows[:, li * J : (li + 1) * J], scale_rows[:].indirect(lists[li][:]))
@@ -121,35 +115,28 @@ def tile_list_rgg_L_kernel(
                 )
 
         move_planes(0)
-        load_weight_half("wa", wa, 0)
-        load_weight_half("wc", wc, 0)
+        load_weights(1, 0)
         load_wb_half(0)
         move_planes(1)
+        nc.sync.dma_start(weight_rows[:], wgo[0 : P * P // J, :].rearrange("r (b c) -> (r b) c", c=P))
         load_state(0)
         load_state(1)
         load_state(2)
-        nc.sync.dma_start(edge_weight[:], wgo)
-        load_weight_half("wa", wa, 1)
-        load_weight_half("wc", wc, 1)
+        load_weights(0, 1)
+        nc.sync.dma_start(edge_weight[:], wgo[:, 0:JH])
+        load_weights(1, 1)
         load_wb_half(1)
         load_state(3)
 
-        turned_weight = turns.tile([P, JH], F32, name="turned")
-        for b in range(BLOCKS):
-            nc.tensor.transpose(
-                turned_weight[:, b * P : (b + 1) * P], edge_weight[:, JH + b * P : JH + (b + 1) * P], identity[:]
-            )
-        weight_cols = keep.tile([P, BLOCKS], F32, name="weight_cols")
-        nc.scalar.copy(weight_cols[:], turned_weight[:, 0:JH:P])
+        def entries(li, j0, width):
+            return lists[li][:, j0 // 16 : (j0 + width) // 16]
 
         picked = {}
 
-        def gather_words(li, a, j0, width, tag):
-            words = keep.tile([P, width], U32, name="picked%d%d_%d" % (li, a, j0), tag=tag, align_bytes=64)
-            cols = lists[li][:, j0 // 16 : (j0 + width) // 16]
-            nc.vector.tensor_copy(words[:], tab[a][:].indirect(cols))
-            for j in range(0, width, JH):
-                picked[li, a, (j0 + j) // JH] = words[:, j : j + JH]
+        def gather_words(li, a, h0, halves, words):
+            nc.vector.tensor_copy(words, tab[a][:].indirect(entries(li, h0 * JH, halves * JH)))
+            for h in range(halves):
+                picked[li, a, h0 + h] = words[:, h * JH : (h + 1) * JH]
 
         codes = {}
         scales = {}
@@ -160,35 +147,26 @@ def tile_list_rgg_L_kernel(
                 rows.rearrange("p i (c n) -> p c i n", n=4),
             )
 
-        def quantise(grouped, label):
-            words = keep.tile([P, grouped.shape[1]], U32, name="codes_" + label, align_bytes=64)
-            planes = keep.tile([P, grouped.shape[1]], U8, name="scales_" + label, align_bytes=64)
+        def round_weights(passes, u, grouped):
+            for n, a in enumerate(passes):
+                for w, name in enumerate(("wa", "wc")):
+                    c0 = n * N + w * NH
+                    interleave(grouped[:, c0 : c0 + NH, :], raw[name, a, u][:])
+            return grouped
+
+        def quantise(grouped, passes, u, tag):
+            width = len(passes) * N
+            words = keep.tile([P, width], U32, name="codes_" + tag, tag=tag, align_bytes=64)
+            planes = keep.tile([P, width], U8, name="scales_" + tag, align_bytes=64)
             nc.vector.quantize_mx(
-                out=words[:].bitcast(FP8X4),
-                scales=planes[:],
-                in_=grouped[:].rearrange("p n i -> p (n i)"),
+                out=words[:].bitcast(FP8X4), scales=planes[:], in_=grouped[:].rearrange("p n i -> p (n i)")
             )
-            return words, planes
-
-        def quantise_first_pass():
-            for name in ("wa", "wc"):
-                grouped = keep.tile([P, N, PACK], BF16, name="grouped_%s0" % name, align_bytes=64)
-                interleave(grouped[:], raw[name, 0][:])
-                words, planes = quantise(grouped, name + "0")
-                for m in range(TILES):
-                    codes[name, 0, m] = words[:, m * P : (m + 1) * P]
-                    scales[name, 0, m] = planes[:, m * P : (m + 1) * P]
-
-        def quantise_second_pass(u):
-            grouped = keep.tile([P, 2 * NH, PACK], BF16, name="grouped_half%d" % u, tag="grouped_half%d" % u, align_bytes=64)
-            for w, name in enumerate(("wa", "wc")):
-                interleave(grouped[:, w * NH : (w + 1) * NH, :], raw[name, 1, u][:])
-            words, planes = quantise(grouped, "half%d" % u)
-            for w, name in enumerate(("wa", "wc")):
-                for t in range(TILES // 2):
-                    cols = slice(w * NH + t * P, w * NH + (t + 1) * P)
-                    codes[name, 1, 2 * u + t] = words[:, cols]
-                    scales[name, 1, 2 * u + t] = planes[:, cols]
+            for n, a in enumerate(passes):
+                for w, name in enumerate(("wa", "wc")):
+                    for t in range(2):
+                        c0 = n * N + w * NH + t * P
+                        codes[name, a, 2 * u + t] = words[:, c0 : c0 + P]
+                        scales[name, a, 2 * u + t] = planes[:, c0 : c0 + P]
 
         def product(acc, w_codes, w_scales, li, a, h, start, stop):
             nc.tensor.matmul_mx(
@@ -201,126 +179,182 @@ def tile_list_rgg_L_kernel(
                 stop=stop,
             )
 
-        messages = {}
+        sum_banks = [
+            (psum.tile([P, JH], F32, name="za%d" % i), psum.tile([P, JH], F32, name="ms%d" % i)) for i in range(3)
+        ]
+        turned = psum.tile([P, JH], F32, name="turned")
+        back = psum.tile([P, JH], F32, name="back")
 
-        def sums(m, h, eta):
+        def sums(m, h, gate_inputs):
+            za, ms = sum_banks[(4 * (m // 2) + 2 * h + m % 2) % 3]
             cols = slice(m * P, (m + 1) * P)
-            za = psum.tile([P, JH], F32, name="za")
-            ms = psum.tile([P, JH], F32, name="ms")
-            for a in range(PASSES):
-                product(za, wb_codes[m // 2][:, a, (m % 2) * P : (m % 2 + 1) * P], wb_planes[4 * a :, cols], 0, a, h, a == 0, False)
-            for a in range(PASSES):
+
+            def with_wb(a, start):
+                product(za, wb_codes[m // 2][:, a, (m % 2) * P : (m % 2 + 1) * P], wb_planes[4 * a :, cols], 0, a, h, start, False)
+
+            def with_quantised(a, start):
                 last = a == PASSES - 1
-                product(za, codes["wa", a, m], scales["wa", a, m], 1, a, h, False, last)
+                product(za, codes["wa", a, m], scales["wa", a, m], 1, a, h, start, last)
                 product(ms, codes["wc", a, m], scales["wc", a, m], 0, a, h, a == 0, last)
-            nc.scalar.activation(eta, za[:], ACT.Sigmoid)
-            return ms
 
-        picked_states = {}
+            with_wb(0, True)
+            with_wb(1, False)
+            with_quantised(0, False)
+            with_quantised(1, False)
+            nc.scalar.activation(gate_inputs[:, 0, :], za[:], ACT.Sigmoid)
+            nc.scalar.copy(gate_inputs[:, 1, :], ms[:])
 
-        def gather_state(m):
-            picked_states[m] = keep.tile([P, J], F32, name="picked_state%d" % m)
-            nc.vector.tensor_copy(picked_states[m][:], state[m][:].indirect(dst_list[:]))
+        def gate(gated, gate_inputs):
+            nc.gpsimd.tensor_tensor(gated, gate_inputs[:, 1, :], gate_inputs[:, 0, :], ALU.mult)
 
-        def gate(m, h, gated):
-            if (m, h) == (1, 0):
-                eta, message = after_rounding[:, 0, :], after_rounding[:, 1, :]
-            else:
-                eta = ring.tile([P, JH], F32, name="eta")[:]
-                message = ring.tile([P, JH], F32, name="message")[:]
-            ms = sums(m, h, eta)
-            nc.scalar.copy(message, ms[:])
-            nc.gpsimd.tensor_tensor(gated, message, eta, ALU.mult)
+        def add(total, gated, states):
+            nc.gpsimd.tensor_tensor(total, gated, states, ALU.add)
 
-        def later_tile(m):
-            picked_state = picked_states[m]
-            work = pair.tile([P, J], F32, name="work")
-            for h in range(J // JH):
-                gate(m, h, work[:, h * JH : (h + 1) * JH])
-            messages[m] = keep.tile([P, J], F32, name="messages%d" % m)
-            if m == TILES - 1:
-                nc.gpsimd.tensor_tensor(messages[m][:], work[:], picked_state[:], ALU.add)
-            else:
-                nc.gpsimd.tensor_tensor(work[:], work[:], picked_state[:], ALU.add)
-                nc.gpsimd.tensor_tensor(messages[m][:], work[:], edge_weight[:], ALU.mult)
+        def weigh(message, total, q):
+            nc.gpsimd.tensor_tensor(message, total, edge_weight[:, q * JQ : (q + 1) * JQ], ALU.mult)
 
-        first, second = slice(0, JH), slice(JH, J)
+        def gather_state(m, j0, states):
+            nc.vector.tensor_copy(states, state[m][:].indirect(entries(1, j0, states.shape[1])))
 
-        def finish_by_transposes(m, gated, result):
-            turned = turns.tile([P, JH], F32, name="turned")
-            for b in range(BLOCKS):
-                cols = slice(b * P, (b + 1) * P)
-                picked_cols = slice(JH + b * P, JH + (b + 1) * P)
-                nc.tensor.matmul(turned[:, cols], picked_states[m][:, picked_cols], identity[:], start=True, stop=False, is_transpose=True)
-                nc.tensor.matmul(turned[:, cols], gated[:, cols], identity[:], start=False, stop=True, is_transpose=True)
-            weighted = after_rounding[:, 2, :] if m == 0 else keep.tile([P, JH], F32, name="weighted")
-            for b in range(BLOCKS):
-                cols = slice(b * P, (b + 1) * P)
-                nc.scalar.activation(weighted[:, cols], turned[:, cols], ACT.Copy, scale=weight_cols[:, b : b + 1])
-            back = turns.tile([P, JH], F32, name="back")
-            for b in range(BLOCKS):
-                cols = slice(b * P, (b + 1) * P)
-                nc.tensor.transpose(back[:, cols], weighted[:, cols], identity[:])
-            nc.scalar.copy(result, back[:])
-
-        def finish_on_gpsimd(m, gated, result):
-            nc.gpsimd.tensor_tensor(gated, gated, picked_states[m][:, first], ALU.add)
-            nc.gpsimd.tensor_tensor(result, gated, edge_weight[:, first], ALU.mult)
-
-        def mixed_tile(m):
-            messages[m] = keep.tile([P, J], F32, name="messages%d" % m)
-            work = pair.tile([P, J], F32, name="work")
-            gate(m, 1, work[:, second])
-            finish_by_transposes(m, work[:, second], messages[m][:, second])
-            gated = after_quantise[:, 1, :] if m == 1 else work[:, first]
-            gate(m, 0, gated)
-            finish_on_gpsimd(m, gated, messages[m][:, first])
-
-        def first_tile():
-            work = pair.tile([P, JH], F32, name="work")
-            gate(0, 0, work[:])
-            early = keep.tile([P, JH], F32, name="early")[:]
-            finish_on_gpsimd(0, work[:], early)
-            nc.vector.tensor_copy(pages[0][:].indirect(dst_list[:, : JH // 16]), early)
-            gated = pair.tile([P, JH], F32, name="work")
-            gate(0, 1, gated[:])
-            late = after_quantise[:, 0, :]
-            finish_by_transposes(0, gated[:], late)
-            nc.vector.tensor_copy(pages[0][:].indirect(dst_list[:, JH // 16 :]), late)
-            store(0)
+        def scatter(m, j0, message):
+            nc.vector.tensor_copy(pages[m][:].indirect(entries(1, j0, message.shape[1])), message)
 
         def store(m):
-            pieces = 2 if m < 2 else 1
-            for c in range(pieces):
-                cols = slice(c * T // pieces, (c + 1) * T // pieces)
-                nc.sync.dma_start(out[m * P : (m + 1) * P, cols], pages[m % 2][:, cols])
+            nc.sync.dma_start(out[m * P : (m + 1) * P, :], pages[m][:])
 
-        def place(m):
-            page = pages[m % 2]
-            if m == TILES - 1:
-                nc.vector.tensor_tensor(page[:].indirect(dst_list[:]), messages[m][:], edge_weight[:], ALU.mult)
-            else:
-                nc.vector.tensor_copy(page[:].indirect(dst_list[:]), messages[m][:])
-            store(m)
+        def turn(bank, states, gated, weighted, blocks=range(BLOCKS)):
+            for b in blocks:
+                cols = slice(b * P, (b + 1) * P)
+                nc.tensor.matmul(bank[:, cols], states[b], identity[:], start=True, stop=False, is_transpose=True)
+                nc.tensor.matmul(bank[:, cols], gated[:, cols], identity[:], start=False, stop=True, is_transpose=True)
+            for b in blocks:
+                nc.scalar.activation(
+                    weighted[b], bank[:, b * P : (b + 1) * P], ACT.Copy, scale=weight_cols[:, b : b + 1]
+                )
 
-        gather_words(1, 0, 0, J, "picked_dst0")
-        gather_words(0, 0, 0, J, "picked_src0")
-        quantise_first_pass()
-        gather_words(0, 1, 0, JH, "raw_wa0")
-        gather_words(1, 1, 0, J, "raw_wc0")
-        quantise_second_pass(0)
-        gather_words(0, 1, JH, JH, "raw_wc1_0")
-        gather_state(0)
-        gather_state(1)
-        gather_state(2)
-        quantise_second_pass(1)
-        after_quantise = keep.tile([P, 2, JH], F32, name="after_quantise", tag="grouped_half1", align_bytes=64)
-        after_rounding = keep.tile([P, 3, JH], F32, name="after_rounding", tag="raw_wc1_1", align_bytes=64)
-        gather_state(3)
-        first_tile()
-        for m in range(1, TILES):
-            if m in (1, 2):
-                mixed_tile(m)
-            else:
-                later_tile(m)
-            place(m)
+        def turn_back(message, weighted):
+            for b, block in enumerate(weighted):
+                nc.tensor.transpose(back[:, b * P : (b + 1) * P], block, identity[:])
+            nc.scalar.copy(message, back[:, 0 : len(weighted) * P])
+
+        def lane(name, blocks):
+            tile = keep.tile([P, blocks * P], F32, name=name)
+            return lambda b0, b1=None: tile[:, b0 * P : (b0 + 1 if b1 is None else b1) * P]
+
+        words_dst0 = keep.tile([P, J], U32, name="words_dst0", align_bytes=64)
+        words_first = keep.tile([P, 3, JH], U32, name="words_first", align_bytes=64)
+        gather_words(1, 0, 0, 2, words_dst0[:])
+        gather_words(0, 0, 0, 1, words_first[:, 0, :])
+        grouped0 = keep.tile([P, N, PACK], BF16, name="grouped0", align_bytes=64)
+        quantise(round_weights([0], 0, grouped0), [0], 0, "early0")
+        gather_words(0, 1, 0, 1, words_first[:, 1, :])
+        gather_words(1, 1, 0, 1, words_first[:, 2, :])
+        grouped1 = keep.tile([P, N, PACK], BF16, name="grouped1", tag="grouped1", align_bytes=64)
+        quantise(round_weights([1], 0, grouped1), [1], 0, "early1")
+        clear_page(2, keep.tile([P, T], F32, name="page2", tag="grouped1", align_bytes=64))
+        words_second = keep.tile([P, 3, JH], U32, name="words_second", tag="raw_wc10", align_bytes=64)
+        gather_words(0, 0, 1, 1, words_second[:, 0, :])
+        gather_words(0, 1, 1, 1, words_second[:, 1, :])
+        gather_words(1, 1, 1, 1, words_second[:, 2, :])
+
+        gate_inputs = [keep.tile([P, 2, JH], F32, name="gate_inputs%d" % i) for i in range(3)]
+        before_quantise = keep.tile([P, 2, JH], F32, name="before_quantise", tag="late", align_bytes=64)
+        states_a, states_b, states_c = lane("states_a", 8), lane("states_b", 8), lane("states_c", 6)
+        gated_a, gated_b = lane("gated_a", 4), lane("gated_b", 4)
+        lane1, lane2, lane3, lane4 = lane("lane1", 10), lane("lane2", 9), lane("lane3", 4), lane("lane4", 2)
+        spare = lane("spare", 4)
+        messages = lane("messages", 24)
+
+        sums(0, 0, gate_inputs[0])
+        sums(1, 0, gate_inputs[1])
+        gather_state(0, 0, states_a(0, 4))
+        gather_state(0, JH, states_a(4, 8))
+        gather_state(1, 0, states_b(0, 4))
+        gather_state(1, JH, states_b(4, 8))
+        gather_state(2, 0, states_c(0, 4))
+        gate(gated_a(0, 4), gate_inputs[0])
+        gate(gated_b(0, 4), gate_inputs[1])
+        sums(0, 1, gate_inputs[2])
+        sums(1, 1, before_quantise)
+        add(lane1(6, 10), gated_a(0, 4), states_a(0, 4))
+
+        nc.tensor.transpose(turned[:, 0:P], weight_rows[:], identity[:])
+        weight_cols = keep.tile([P, BLOCKS], F32, name="weight_cols")
+        nc.scalar.copy(weight_cols[:], turned[:, BLOCKS : 2 * BLOCKS])
+        grouped_late = keep.tile([P, PASSES * N, PACK], BF16, name="grouped_late", tag="grouped_late", align_bytes=64)
+        round_weights([0, 1], 1, grouped_late)
+
+        weigh(messages(0, 2), lane1(6, 8), 0)
+        scatter(0, 0, messages(0, 2))
+        gather_state(2, JH, lane1(7))
+        add(lane1(3, 7), gated_b(0, 4), states_b(0, 4))
+        weigh(messages(2, 4), lane1(3, 5), 0)
+        scatter(1, 0, messages(2, 4))
+        gather_state(2, JH + P, lane1(4))
+        gate(states_b(0, 4), gate_inputs[2])
+        weigh(gated_b(0, 2), lane1(8, 10), 1)
+        scatter(0, JQ, gated_b(0, 2))
+        gather_state(2, JH + 2 * P, lane1(8))
+        gate(lane1(0, 4), before_quantise)
+        quantise(grouped_late, [0, 1], 1, "late")
+        after_rounding = keep.tile([P, JQ], F32, name="after_rounding", tag="raw_wc11", align_bytes=64)
+        weigh(after_rounding[:], lane1(5, 7), 1)
+        clear_page(3, keep.tile([P, T], F32, name="page3", tag="grouped_late", align_bytes=64))
+        scatter(1, JQ, after_rounding[:])
+        gather_state(2, JH + 3 * P, lane1(5))
+
+        weighted_a = [spare(0), lane1(6), spare(1), lane3(1)]
+        weighted_b = [spare(2), lane3(0), spare(3), lane2(0)]
+        turn(turned, [states_a(4 + b) for b in range(BLOCKS)], states_b(0, 4), weighted_a)
+        turn_back(messages(6, 8), weighted_a[:2])
+        scatter(0, 2 * JQ, messages(6, 8))
+        turn(sum_banks[0][1], [states_b(4 + b) for b in range(BLOCKS)], lane1(0, 4), weighted_b)
+        turn_back(messages(8, 10), weighted_b[:2])
+        gather_state(3, 0, lane3(0))
+        scatter(1, 2 * JQ, messages(8, 10))
+        turn_back(messages(10, 12), weighted_a[2:])
+        gather_state(3, P, lane3(1))
+        scatter(0, 3 * JQ, messages(10, 12))
+        store(0)
+        turn_back(messages(12, 14), weighted_b[2:])
+        gather_state(3, 2 * P, lane2(0))
+        scatter(1, 3 * JQ, messages(12, 14))
+        store(1)
+
+        sums(2, 0, gate_inputs[0])
+        sums(3, 0, gate_inputs[1])
+        gate(gated_a(0, 4), gate_inputs[0])
+        add(lane2(1, 5), gated_a(0, 4), states_c(0, 4))
+        weigh(messages(14, 16), lane2(1, 3), 0)
+        gather_state(3, 3 * P, lane2(1))
+        scatter(2, 0, messages(14, 16))
+        gather_state(3, JH, lane2(2))
+        gate(states_c(0, 4), gate_inputs[1])
+        add(lane4(0, 2), states_c(0, 2), lane3(0, 2))
+        sums(2, 1, gate_inputs[2])
+        sums(3, 1, gate_inputs[0])
+        weigh(messages(16, 18), lane4(0, 2), 0)
+        scatter(3, 0, messages(16, 18))
+        gather_state(3, JH + P, lane4(0))
+        gate(lane3(0, 4), gate_inputs[2])
+        weigh(states_c(0, 2), lane2(3, 5), 1)
+        scatter(2, JQ, states_c(0, 2))
+        gather_state(3, JH + 2 * P, lane2(3))
+        add(lane2(4, 6), states_c(2, 4), lane2(0, 2))
+        weigh(messages(18, 20), lane2(4, 6), 1)
+        scatter(3, JQ, messages(18, 20))
+        gather_state(3, JH + 3 * P, lane2(4))
+        gate(states_c(2, 6), gate_inputs[0])
+
+        weighted_c = [spare(b) for b in range(BLOCKS)]
+        weighted_d = [states_a(b) for b in range(BLOCKS)]
+        turn(turned, [lane1(7), lane1(4), lane1(8), lane1(5)], lane3(0, 4), weighted_c)
+        turn_back(lane2(5, 9), weighted_c)
+        scatter(2, JH, lane2(5, 9))
+        store(2)
+        states_d = [lane2(2), lane4(0), lane2(3), lane2(4)]
+        turn(sum_banks[2][0], states_d, states_c(2, 6), weighted_d, range(BLOCKS - 1))
+        turn(turned, states_d, states_c(2, 6), weighted_d, [BLOCKS - 1])
+        turn_back(messages(20, 24), weighted_d)
+        scatter(3, JH, messages(20, 24))
+        store(3)

@@ -122,8 +122,8 @@ def tile_list_rgg_L_kernel(
         load_state(0)
         load_state(1)
         load_state(2)
-        load_weights(0, 1)
         nc.sync.dma_start(edge_weight[:], wgo[:, 0:JH])
+        load_weights(0, 1)
         load_weights(1, 1)
         load_wb_half(1)
         load_state(3)
@@ -257,8 +257,7 @@ def tile_list_rgg_L_kernel(
         gather_words(0, 1, 1, 1, words_second[:, 1, :])
         gather_words(1, 1, 1, 1, words_second[:, 2, :])
 
-        gate_inputs = [keep.tile([P, 2, JH], F32, name="gate_inputs%d" % i) for i in range(3)]
-        before_quantise = keep.tile([P, 2, JH], F32, name="before_quantise", tag="late", align_bytes=64)
+        gate_inputs = [keep.tile([P, 2, JH], F32, name="gate_inputs%d" % i) for i in range(4)]
         states_a, states_b, states_c = lane("states_a", 8), lane("states_b", 8), lane("states_c", 6)
         gated_a, gated_b = lane("gated_a", 4), lane("gated_b", 4)
         lane1, lane2, lane3, lane4 = lane("lane1", 10), lane("lane2", 9), lane("lane3", 4), lane("lane4", 2)
@@ -275,7 +274,7 @@ def tile_list_rgg_L_kernel(
         gate(gated_a(0, 4), gate_inputs[0])
         gate(gated_b(0, 4), gate_inputs[1])
         sums(0, 1, gate_inputs[2])
-        sums(1, 1, before_quantise)
+        sums(1, 1, gate_inputs[3])
         add(lane1(6, 10), gated_a(0, 4), states_a(0, 4))
 
         nc.tensor.transpose(turned[:, 0:P], weight_rows[:], identity[:])
@@ -295,15 +294,16 @@ def tile_list_rgg_L_kernel(
         weigh(gated_b(0, 2), lane1(8, 10), 1)
         scatter(0, JQ, gated_b(0, 2))
         gather_state(2, JH + 2 * P, lane1(8))
-        gate(lane1(0, 4), before_quantise)
-        quantise(grouped_late, [0, 1], 1, "late")
-        after_rounding = keep.tile([P, JQ], F32, name="after_rounding", tag="raw_wc11", align_bytes=64)
-        weigh(after_rounding[:], lane1(5, 7), 1)
-        clear_page(3, keep.tile([P, T], F32, name="page3", tag="grouped_late", align_bytes=64))
-        scatter(1, JQ, after_rounding[:])
+        gate(lane1(0, 4), gate_inputs[3])
+        before_quantise = keep.tile([P, JQ], F32, name="before_quantise", tag="late", align_bytes=64)
+        weigh(before_quantise[:], lane1(5, 7), 1)
+        scatter(1, JQ, before_quantise[:])
         gather_state(2, JH + 3 * P, lane1(5))
+        quantise(grouped_late, [0, 1], 1, "late")
+        clear_page(3, keep.tile([P, T], F32, name="page3", tag="grouped_late", align_bytes=64))
+        after_rounding = keep.tile([P, P], F32, name="after_rounding", tag="raw_wc11", align_bytes=64)
 
-        weighted_a = [spare(0), lane1(6), spare(1), lane3(1)]
+        weighted_a = [after_rounding[:], lane1(6), spare(1), lane3(1)]
         weighted_b = [spare(2), lane3(0), spare(3), lane2(0)]
         turn(turned, [states_a(4 + b) for b in range(BLOCKS)], states_b(0, 4), weighted_a)
         turn_back(messages(6, 8), weighted_a[:2])

@@ -59,6 +59,7 @@ def tile_list_rgg_L_kernel(
 
         clear_page(0, keep.tile([P, T], F32, name="page0"))
         clear_page(1, keep.tile([P, T], F32, name="page1"))
+        clear_page(2, keep.tile([P, T], F32, name="page2"))
 
         tab = [keep.tile([P, T], U32, name="tab%d" % a) for a in range(PASSES)]
 
@@ -69,13 +70,13 @@ def tile_list_rgg_L_kernel(
 
         raw = {}
 
-        def load_weights(a, u):
+        def load_weights(a, n0, width):
             for name, w in (("wa", wa), ("wc", wc)):
-                label = "raw_%s%d%d" % (name, a, u)
-                raw[name, a, u] = keep.tile([P, PACK, NH], F32, name=label, tag=label, align_bytes=64)
+                label = "raw_%s%d_%d" % (name, a, n0)
+                raw[name, a, n0] = keep.tile([P, PACK, width], F32, name=label, tag=label, align_bytes=64)
                 nc.sync.dma_start(
-                    raw[name, a, u][:],
-                    w[a * K_PASS : (a + 1) * K_PASS, u * NH : (u + 1) * NH].rearrange("(p i) n -> p i n", i=PACK),
+                    raw[name, a, n0][:],
+                    w[a * K_PASS : (a + 1) * K_PASS, n0 : n0 + width].rearrange("(p i) n -> p i n", i=PACK),
                 )
 
         state = [keep.tile([P, T], F32, name="state%d" % m, align_bytes=64) for m in range(TILES)]
@@ -99,7 +100,7 @@ def tile_list_rgg_L_kernel(
         nc.sync.dma_start(src_list[:], offs)
         nc.sync.dma_start(dst_list[:], offs2)
         load_tab(0)
-        load_weights(0, 0)
+        load_weights(0, 0, N)
         load_tab(1)
 
         picked_planes = [keep.tile([P, 2 * J], U8, name="picked_planes%d" % a, align_bytes=64) for a in range(PASSES)]
@@ -115,16 +116,15 @@ def tile_list_rgg_L_kernel(
                 )
 
         move_planes(0)
-        load_weights(1, 0)
+        load_weights(1, 0, NH)
         load_wb_half(0)
         move_planes(1)
-        nc.sync.dma_start(weight_rows[:], wgo[0 : P * P // J, :].rearrange("r (b c) -> (r b) c", c=P))
         load_state(0)
+        nc.sync.dma_start(weight_rows[:], wgo[0 : P * P // J, :].rearrange("r (b c) -> (r b) c", c=P))
         load_state(1)
         load_state(2)
         nc.sync.dma_start(edge_weight[:], wgo[:, 0:JH])
-        load_weights(0, 1)
-        load_weights(1, 1)
+        load_weights(1, NH, NH)
         load_wb_half(1)
         load_state(3)
 
@@ -147,26 +147,27 @@ def tile_list_rgg_L_kernel(
                 rows.rearrange("p i (c n) -> p c i n", n=4),
             )
 
-        def round_weights(passes, u, grouped):
-            for n, a in enumerate(passes):
-                for w, name in enumerate(("wa", "wc")):
-                    c0 = n * N + w * NH
-                    interleave(grouped[:, c0 : c0 + NH, :], raw[name, a, u][:])
+        def round_weights(parts, tag):
+            grouped = keep.tile([P, N, PACK], BF16, name=tag, tag=tag, align_bytes=64)
+            c0 = 0
+            for part in parts:
+                width = raw[part].shape[2]
+                interleave(grouped[:, c0 : c0 + width, :], raw[part][:])
+                c0 = c0 + width
             return grouped
 
-        def quantise(grouped, passes, u, tag):
-            width = len(passes) * N
-            words = keep.tile([P, width], U32, name="codes_" + tag, tag=tag, align_bytes=64)
-            planes = keep.tile([P, width], U8, name="scales_" + tag, align_bytes=64)
+        def quantise(grouped, parts, label):
+            words = keep.tile([P, N], U32, name="codes_" + label, align_bytes=64)
+            planes = keep.tile([P, N], U8, name="scales_" + label, align_bytes=64)
             nc.vector.quantize_mx(
                 out=words[:].bitcast(FP8X4), scales=planes[:], in_=grouped[:].rearrange("p n i -> p (n i)")
             )
-            for n, a in enumerate(passes):
-                for w, name in enumerate(("wa", "wc")):
-                    for t in range(2):
-                        c0 = n * N + w * NH + t * P
-                        codes[name, a, 2 * u + t] = words[:, c0 : c0 + P]
-                        scales[name, a, 2 * u + t] = planes[:, c0 : c0 + P]
+            c0 = 0
+            for name, a, n0 in parts:
+                for m in range(n0 // P, (n0 + raw[name, a, n0].shape[2]) // P):
+                    codes[name, a, m] = words[:, c0 : c0 + P]
+                    scales[name, a, m] = planes[:, c0 : c0 + P]
+                    c0 = c0 + P
 
         def product(acc, w_codes, w_scales, li, a, h, start, stop):
             nc.tensor.matmul_mx(
@@ -210,8 +211,8 @@ def tile_list_rgg_L_kernel(
         def add(total, gated, states):
             nc.gpsimd.tensor_tensor(total, gated, states, ALU.add)
 
-        def weigh(message, total, q):
-            nc.gpsimd.tensor_tensor(message, total, edge_weight[:, q * JQ : (q + 1) * JQ], ALU.mult)
+        def weigh(message, total, j0):
+            nc.gpsimd.tensor_tensor(message, total, edge_weight[:, j0 : j0 + message.shape[1]], ALU.mult)
 
         def gather_state(m, j0, states):
             nc.vector.tensor_copy(states, state[m][:].indirect(entries(1, j0, states.shape[1])))
@@ -222,14 +223,16 @@ def tile_list_rgg_L_kernel(
         def store(m):
             nc.sync.dma_start(out[m * P : (m + 1) * P, :], pages[m][:])
 
-        def turn(bank, states, gated, weighted, blocks=range(BLOCKS)):
+        def turn(bank, h, states, gated, weighted, blocks=range(BLOCKS)):
             for b in blocks:
                 cols = slice(b * P, (b + 1) * P)
-                nc.tensor.matmul(bank[:, cols], states[b], identity[:], start=True, stop=False, is_transpose=True)
-                nc.tensor.matmul(bank[:, cols], gated[:, cols], identity[:], start=False, stop=True, is_transpose=True)
+                nc.tensor.matmul(bank[:, cols], gated[:, cols], identity[:], start=b == blocks[0], stop=False, is_transpose=True)
+            for b in blocks:
+                cols = slice(b * P, (b + 1) * P)
+                nc.tensor.matmul(bank[:, cols], states[b], identity[:], start=False, stop=b == blocks[-1], is_transpose=True)
             for b in blocks:
                 nc.scalar.activation(
-                    weighted[b], bank[:, b * P : (b + 1) * P], ACT.Copy, scale=weight_cols[:, b : b + 1]
+                    weighted[b], bank[:, b * P : (b + 1) * P], ACT.Copy, scale=weight_cols[:, h * BLOCKS + b : h * BLOCKS + b + 1]
                 )
 
         def turn_back(message, weighted):
@@ -237,124 +240,110 @@ def tile_list_rgg_L_kernel(
                 nc.tensor.transpose(back[:, b * P : (b + 1) * P], block, identity[:])
             nc.scalar.copy(message, back[:, 0 : len(weighted) * P])
 
-        def lane(name, blocks):
-            tile = keep.tile([P, blocks * P], F32, name=name)
+        def lane(name, blocks, tag=None):
+            tile = keep.tile([P, blocks * P], F32, name=name, tag=tag or name, align_bytes=64)
             return lambda b0, b1=None: tile[:, b0 * P : (b0 + 1 if b1 is None else b1) * P]
 
-        words_dst0 = keep.tile([P, J], U32, name="words_dst0", align_bytes=64)
-        words_first = keep.tile([P, 3, JH], U32, name="words_first", align_bytes=64)
-        gather_words(1, 0, 0, 2, words_dst0[:])
-        gather_words(0, 0, 0, 1, words_first[:, 0, :])
-        grouped0 = keep.tile([P, N, PACK], BF16, name="grouped0", align_bytes=64)
-        quantise(round_weights([0], 0, grouped0), [0], 0, "early0")
-        gather_words(0, 1, 0, 1, words_first[:, 1, :])
-        gather_words(1, 1, 0, 1, words_first[:, 2, :])
-        grouped1 = keep.tile([P, N, PACK], BF16, name="grouped1", tag="grouped1", align_bytes=64)
-        quantise(round_weights([1], 0, grouped1), [1], 0, "early1")
-        clear_page(2, keep.tile([P, T], F32, name="page2", tag="grouped1", align_bytes=64))
-        words_second = keep.tile([P, 3, JH], U32, name="words_second", tag="raw_wc10", align_bytes=64)
-        gather_words(0, 0, 1, 1, words_second[:, 0, :])
-        gather_words(0, 1, 1, 1, words_second[:, 1, :])
-        gather_words(1, 1, 1, 1, words_second[:, 2, :])
+        def words_tile(label, width, tag):
+            return keep.tile([P, width], U32, name=label, tag=tag, align_bytes=64)[:]
+
+        gather_words(1, 0, 0, 2, words_tile("words_dst0", J, "words_dst0"))
+        gather_words(0, 0, 0, 2, words_tile("words_src0", J, "words_src0"))
+        for part in (("wa", 0, 0), ("wc", 0, 0)):
+            quantise(round_weights([part], "grouped_" + part[0]), [part], part[0])
+        gather_words(0, 1, 0, 1, words_tile("words_src1_0", JH, "raw_wa0_0"))
+        gather_words(1, 1, 0, 2, words_tile("words_dst1", J, "raw_wc0_0"))
+        early_parts = [("wa", 1, 0), ("wc", 1, 0)]
+        quantise(round_weights(early_parts, "grouped_early"), early_parts, "early")
+        gather_words(0, 1, 1, 1, words_tile("words_src1_1", JH, "raw_wc1_0"))
 
         gate_inputs = [keep.tile([P, 2, JH], F32, name="gate_inputs%d" % i) for i in range(4)]
-        states_a, states_b, states_c = lane("states_a", 8), lane("states_b", 8), lane("states_c", 6)
-        gated_a, gated_b = lane("gated_a", 4), lane("gated_b", 4)
-        lane1, lane2, lane3, lane4 = lane("lane1", 10), lane("lane2", 9), lane("lane3", 4), lane("lane4", 2)
+        states_a, states_b, states_c = lane("states_a", 8), lane("states_b", 8), lane("states_c", 8)
+        gated_a, gated_b, work = lane("gated_a", 6), lane("gated_b", 4), lane("work", 4)
+        lane2, lane4 = lane("lane2", 9), lane("lane4", 2)
         spare = lane("spare", 4)
-        messages = lane("messages", 24)
+        messages = lane("messages", 22)
 
+        gather_state(0, 0, states_a(0, 8))
+        gather_state(1, 0, states_b(0, 8))
+        gather_state(2, 0, states_c(0, 8))
         sums(0, 0, gate_inputs[0])
         sums(1, 0, gate_inputs[1])
-        gather_state(0, 0, states_a(0, 4))
-        gather_state(0, JH, states_a(4, 8))
-        gather_state(1, 0, states_b(0, 4))
-        gather_state(1, JH, states_b(4, 8))
-        gather_state(2, 0, states_c(0, 4))
-        gate(gated_a(0, 4), gate_inputs[0])
-        gate(gated_b(0, 4), gate_inputs[1])
         sums(0, 1, gate_inputs[2])
         sums(1, 1, gate_inputs[3])
-        add(lane1(6, 10), gated_a(0, 4), states_a(0, 4))
+        gate(gated_a(0, 4), gate_inputs[0])
+        gate(gated_b(0, 4), gate_inputs[1])
+        add(work(0, 4), gated_a(0, 4), states_a(0, 4))
+        weigh(messages(0, 4), work(0, 4), 0)
+        scatter(0, 0, messages(0, 4))
 
         nc.tensor.transpose(turned[:, 0:P], weight_rows[:], identity[:])
-        weight_cols = keep.tile([P, BLOCKS], F32, name="weight_cols")
-        nc.scalar.copy(weight_cols[:], turned[:, BLOCKS : 2 * BLOCKS])
-        grouped_late = keep.tile([P, PASSES * N, PACK], BF16, name="grouped_late", tag="grouped_late", align_bytes=64)
-        round_weights([0, 1], 1, grouped_late)
+        weight_cols = keep.tile([P, 2 * BLOCKS], F32, name="weight_cols")
+        nc.scalar.copy(weight_cols[:], turned[:, 0 : 2 * BLOCKS])
+        weighted_b0 = [spare(b) for b in range(BLOCKS)]
+        turn(turned, 0, [states_b(b) for b in range(BLOCKS)], gated_b(0, 4), weighted_b0)
 
-        weigh(messages(0, 2), lane1(6, 8), 0)
-        scatter(0, 0, messages(0, 2))
-        gather_state(2, JH, lane1(7))
-        add(lane1(3, 7), gated_b(0, 4), states_b(0, 4))
-        weigh(messages(2, 4), lane1(3, 5), 0)
-        scatter(1, 0, messages(2, 4))
-        gather_state(2, JH + P, lane1(4))
-        gate(states_b(0, 4), gate_inputs[2])
-        weigh(gated_b(0, 2), lane1(8, 10), 1)
-        scatter(0, JQ, gated_b(0, 2))
-        gather_state(2, JH + 2 * P, lane1(8))
-        gate(lane1(0, 4), gate_inputs[3])
-        before_quantise = keep.tile([P, JQ], F32, name="before_quantise", tag="late", align_bytes=64)
-        weigh(before_quantise[:], lane1(5, 7), 1)
-        scatter(1, JQ, before_quantise[:])
-        gather_state(2, JH + 3 * P, lane1(5))
-        quantise(grouped_late, [0, 1], 1, "late")
+        late_parts = [("wa", 1, NH), ("wc", 1, NH)]
+        quantise(round_weights(late_parts, "grouped_late"), late_parts, "late")
+        after_rounding = lane("after_rounding", 11, "raw_wc1_%d" % NH)
+        turn_back(after_rounding(0, 4), weighted_b0)
+        scatter(1, 0, after_rounding(0, 4))
+        gate(work(0, 4), gate_inputs[2])
+        gate(gate_inputs[2][:, 0, :], gate_inputs[3])
         clear_page(3, keep.tile([P, T], F32, name="page3", tag="grouped_late", align_bytes=64))
-        after_rounding = keep.tile([P, P], F32, name="after_rounding", tag="raw_wc11", align_bytes=64)
 
-        weighted_a = [after_rounding[:], lane1(6), spare(1), lane3(1)]
-        weighted_b = [spare(2), lane3(0), spare(3), lane2(0)]
-        turn(turned, [states_a(4 + b) for b in range(BLOCKS)], states_b(0, 4), weighted_a)
-        turn_back(messages(6, 8), weighted_a[:2])
-        scatter(0, 2 * JQ, messages(6, 8))
-        turn(sum_banks[0][1], [states_b(4 + b) for b in range(BLOCKS)], lane1(0, 4), weighted_b)
-        turn_back(messages(8, 10), weighted_b[:2])
-        gather_state(3, 0, lane3(0))
-        scatter(1, 2 * JQ, messages(8, 10))
-        turn_back(messages(10, 12), weighted_a[2:])
-        gather_state(3, P, lane3(1))
-        scatter(0, 3 * JQ, messages(10, 12))
+        weighted_a = [after_rounding(4), after_rounding(5), after_rounding(6), after_rounding(8)]
+        weighted_b = [spare(0), after_rounding(7), lane2(1), lane2(0)]
+        turn(turned, 1, [states_a(4 + b) for b in range(BLOCKS)], work(0, 4), weighted_a)
+        turn_back(messages(4, 6), weighted_a[:2])
+        scatter(0, 2 * JQ, messages(4, 6))
+        turn(sum_banks[0][1], 1, [states_b(4 + b) for b in range(BLOCKS)], gate_inputs[2][:, 0, :], weighted_b)
+        turn_back(messages(6, 8), weighted_b[:2])
+        gather_state(3, 0, after_rounding(7))
+        scatter(1, 2 * JQ, messages(6, 8))
+        turn_back(messages(8, 10), weighted_a[2:])
+        gather_state(3, P, after_rounding(8))
+        scatter(0, 3 * JQ, messages(8, 10))
         store(0)
-        turn_back(messages(12, 14), weighted_b[2:])
+        turn_back(messages(10, 12), weighted_b[2:])
         gather_state(3, 2 * P, lane2(0))
-        scatter(1, 3 * JQ, messages(12, 14))
+        scatter(1, 3 * JQ, messages(10, 12))
         store(1)
 
         sums(2, 0, gate_inputs[0])
         sums(3, 0, gate_inputs[1])
         gate(gated_a(0, 4), gate_inputs[0])
         add(lane2(1, 5), gated_a(0, 4), states_c(0, 4))
-        weigh(messages(14, 16), lane2(1, 3), 0)
+        weigh(messages(12, 14), lane2(1, 3), 0)
         gather_state(3, 3 * P, lane2(1))
-        scatter(2, 0, messages(14, 16))
+        scatter(2, 0, messages(12, 14))
         gather_state(3, JH, lane2(2))
-        gate(states_c(0, 4), gate_inputs[1])
-        add(lane4(0, 2), states_c(0, 2), lane3(0, 2))
-        sums(2, 1, gate_inputs[2])
+        gate(gated_a(0, 4), gate_inputs[1])
+        add(lane4(0, 2), gated_a(0, 2), after_rounding(7, 9))
+        sums(2, 1, gate_inputs[3])
         sums(3, 1, gate_inputs[0])
-        weigh(messages(16, 18), lane4(0, 2), 0)
-        scatter(3, 0, messages(16, 18))
+        weigh(messages(14, 16), lane4(0, 2), 0)
+        scatter(3, 0, messages(14, 16))
         gather_state(3, JH + P, lane4(0))
-        gate(lane3(0, 4), gate_inputs[2])
-        weigh(states_c(0, 2), lane2(3, 5), 1)
-        scatter(2, JQ, states_c(0, 2))
+        gate(after_rounding(7, 11), gate_inputs[3])
+        weigh(gated_a(0, 2), lane2(3, 5), JQ)
+        scatter(2, JQ, gated_a(0, 2))
         gather_state(3, JH + 2 * P, lane2(3))
-        add(lane2(4, 6), states_c(2, 4), lane2(0, 2))
-        weigh(messages(18, 20), lane2(4, 6), 1)
-        scatter(3, JQ, messages(18, 20))
+        add(lane2(4, 6), gated_a(2, 4), lane2(0, 2))
+        weigh(messages(16, 18), lane2(4, 6), JQ)
+        scatter(3, JQ, messages(16, 18))
         gather_state(3, JH + 3 * P, lane2(4))
-        gate(states_c(2, 6), gate_inputs[0])
+        gate(gated_a(2, 6), gate_inputs[0])
 
         weighted_c = [spare(b) for b in range(BLOCKS)]
         weighted_d = [states_a(b) for b in range(BLOCKS)]
-        turn(turned, [lane1(7), lane1(4), lane1(8), lane1(5)], lane3(0, 4), weighted_c)
+        turn(turned, 1, [states_c(4 + b) for b in range(BLOCKS)], after_rounding(7, 11), weighted_c)
         turn_back(lane2(5, 9), weighted_c)
         scatter(2, JH, lane2(5, 9))
         store(2)
         states_d = [lane2(2), lane4(0), lane2(3), lane2(4)]
-        turn(sum_banks[2][0], states_d, states_c(2, 6), weighted_d, range(BLOCKS - 1))
-        turn(turned, states_d, states_c(2, 6), weighted_d, [BLOCKS - 1])
-        turn_back(messages(20, 24), weighted_d)
-        scatter(3, JH, messages(20, 24))
+        turn(sum_banks[2][0], 1, states_d, gated_a(2, 6), weighted_d, range(BLOCKS - 1))
+        turn(turned, 1, states_d, gated_a(2, 6), weighted_d, [BLOCKS - 1])
+        turn_back(messages(18, 22), weighted_d)
+        scatter(3, JH, messages(18, 22))
         store(3)

@@ -186,8 +186,8 @@ def tile_list_rgg_L_kernel(
         turned = psum.tile([P, JH], F32, name="turned")
         back = psum.tile([P, JH], F32, name="back")
 
-        def sums(m, h, gate_inputs):
-            za, ms = sum_banks[(4 * (m // 2) + 2 * h + m % 2) % 3]
+        def sums(m, h, banks, gate_inputs):
+            za, ms = banks
             cols = slice(m * P, (m + 1) * P)
 
             def with_wb(a, start):
@@ -235,10 +235,10 @@ def tile_list_rgg_L_kernel(
                     weighted[b], bank[:, b * P : (b + 1) * P], ACT.Copy, scale=weight_cols[:, h * BLOCKS + b : h * BLOCKS + b + 1]
                 )
 
-        def turn_back(message, weighted):
+        def turn_back(bank, message, weighted):
             for b, block in enumerate(weighted):
-                nc.tensor.transpose(back[:, b * P : (b + 1) * P], block, identity[:])
-            nc.scalar.copy(message, back[:, 0 : len(weighted) * P])
+                nc.tensor.transpose(bank[:, b * P : (b + 1) * P], block, identity[:])
+            nc.scalar.copy(message, bank[:, 0 : len(weighted) * P])
 
         def lane(name, blocks, tag=None):
             tile = keep.tile([P, blocks * P], F32, name=name, tag=tag or name, align_bytes=64)
@@ -267,10 +267,10 @@ def tile_list_rgg_L_kernel(
         gather_state(0, 0, states_a(0, 8))
         gather_state(1, 0, states_b(0, 8))
         gather_state(2, 0, states_c(0, 8))
-        sums(0, 0, gate_inputs[0])
-        sums(1, 0, gate_inputs[1])
-        sums(0, 1, gate_inputs[2])
-        sums(1, 1, gate_inputs[3])
+        sums(0, 0, sum_banks[0], gate_inputs[0])
+        sums(1, 0, sum_banks[1], gate_inputs[1])
+        sums(0, 1, sum_banks[2], gate_inputs[2])
+        sums(1, 1, sum_banks[0], gate_inputs[3])
         gate(gated_a(0, 4), gate_inputs[0])
         gate(gated_b(0, 4), gate_inputs[1])
         add(work(0, 4), gated_a(0, 4), states_a(0, 4))
@@ -285,65 +285,64 @@ def tile_list_rgg_L_kernel(
 
         late_parts = [("wa", 1, NH), ("wc", 1, NH)]
         quantise(round_weights(late_parts, "grouped_late"), late_parts, "late")
-        after_rounding = lane("after_rounding", 11, "raw_wc1_%d" % NH)
-        turn_back(after_rounding(0, 4), weighted_b0)
+        after_rounding = lane("after_rounding", 12, "raw_wc1_%d" % NH)
+        turn_back(back, after_rounding(0, 4), weighted_b0)
         scatter(1, 0, after_rounding(0, 4))
         gate(work(0, 4), gate_inputs[2])
         gate(gate_inputs[2][:, 0, :], gate_inputs[3])
         clear_page(3, keep.tile([P, T], F32, name="page3", tag="grouped_late", align_bytes=64))
 
-        weighted_a = [after_rounding(4), after_rounding(5), after_rounding(6), after_rounding(8)]
-        weighted_b = [spare(0), after_rounding(7), lane2(1), lane2(0)]
+        weighted_a = [after_rounding(4), after_rounding(8), after_rounding(5), after_rounding(6)]
+        weighted_b = [spare(0), after_rounding(9), lane2(1), after_rounding(7)]
         turn(turned, 1, [states_a(4 + b) for b in range(BLOCKS)], work(0, 4), weighted_a)
-        turn_back(messages(4, 6), weighted_a[:2])
+        turn_back(back, messages(4, 6), weighted_a[:2])
+        gather_state(3, 0, after_rounding(8))
         scatter(0, 2 * JQ, messages(4, 6))
         turn(sum_banks[0][1], 1, [states_b(4 + b) for b in range(BLOCKS)], gate_inputs[2][:, 0, :], weighted_b)
-        turn_back(messages(6, 8), weighted_b[:2])
-        gather_state(3, 0, after_rounding(7))
+        turn_back(back, messages(6, 8), weighted_b[:2])
+        gather_state(3, P, after_rounding(9))
         scatter(1, 2 * JQ, messages(6, 8))
-        turn_back(messages(8, 10), weighted_a[2:])
-        gather_state(3, P, after_rounding(8))
+        turn_back(back, messages(8, 10), weighted_a[2:])
+        gather_state(3, 2 * P, after_rounding(6))
         scatter(0, 3 * JQ, messages(8, 10))
         store(0)
-        turn_back(messages(10, 12), weighted_b[2:])
-        gather_state(3, 2 * P, lane2(0))
+        turn_back(back, messages(10, 12), weighted_b[2:])
+        gather_state(3, 3 * P, after_rounding(7))
         scatter(1, 3 * JQ, messages(10, 12))
         store(1)
 
-        sums(2, 0, gate_inputs[0])
-        sums(3, 0, gate_inputs[1])
+        sums(2, 0, sum_banks[1], gate_inputs[0])
+        sums(3, 0, (back, turned), gate_inputs[1])
         gate(gated_a(0, 4), gate_inputs[0])
         add(lane2(1, 5), gated_a(0, 4), states_c(0, 4))
         weigh(messages(12, 14), lane2(1, 3), 0)
-        gather_state(3, 3 * P, lane2(1))
+        gather_state(3, JH, lane2(1))
         scatter(2, 0, messages(12, 14))
-        gather_state(3, JH, lane2(2))
+        gather_state(3, JH + P, lane2(2))
         gate(gated_a(0, 4), gate_inputs[1])
-        add(lane4(0, 2), gated_a(0, 2), after_rounding(7, 9))
-        sums(2, 1, gate_inputs[3])
-        sums(3, 1, gate_inputs[0])
+        add(lane4(0, 2), gated_a(0, 2), after_rounding(8, 10))
+        sums(2, 1, (back, turned), gate_inputs[3])
+        sums(3, 1, (back, turned), gate_inputs[0])
         weigh(messages(14, 16), lane4(0, 2), 0)
         scatter(3, 0, messages(14, 16))
-        gather_state(3, JH + P, lane4(0))
-        gate(after_rounding(7, 11), gate_inputs[3])
+        gather_state(3, JH + 2 * P, lane4(0))
+        gate(after_rounding(8, 12), gate_inputs[3])
         weigh(gated_a(0, 2), lane2(3, 5), JQ)
         scatter(2, JQ, gated_a(0, 2))
-        gather_state(3, JH + 2 * P, lane2(3))
-        add(lane2(4, 6), gated_a(2, 4), lane2(0, 2))
+        gather_state(3, JH + 3 * P, lane2(3))
+        add(lane2(4, 6), gated_a(2, 4), after_rounding(6, 8))
         weigh(messages(16, 18), lane2(4, 6), JQ)
         scatter(3, JQ, messages(16, 18))
-        gather_state(3, JH + 3 * P, lane2(4))
         gate(gated_a(2, 6), gate_inputs[0])
 
         weighted_c = [spare(b) for b in range(BLOCKS)]
         weighted_d = [states_a(b) for b in range(BLOCKS)]
-        turn(turned, 1, [states_c(4 + b) for b in range(BLOCKS)], after_rounding(7, 11), weighted_c)
-        turn_back(lane2(5, 9), weighted_c)
+        turn(sum_banks[0][0], 1, [states_c(4 + b) for b in range(BLOCKS)], after_rounding(8, 12), weighted_c)
+        turn_back(sum_banks[2][1], lane2(5, 9), weighted_c)
         scatter(2, JH, lane2(5, 9))
         store(2)
-        states_d = [lane2(2), lane4(0), lane2(3), lane2(4)]
-        turn(sum_banks[2][0], 1, states_d, gated_a(2, 6), weighted_d, range(BLOCKS - 1))
-        turn(turned, 1, states_d, gated_a(2, 6), weighted_d, [BLOCKS - 1])
-        turn_back(messages(18, 22), weighted_d)
+        states_d = [lane2(1), lane2(2), lane4(0), lane2(3)]
+        turn(sum_banks[2][0], 1, states_d, gated_a(2, 6), weighted_d)
+        turn_back(sum_banks[2][1], messages(18, 22), weighted_d)
         scatter(3, JH, messages(18, 22))
         store(3)

@@ -53,13 +53,13 @@ def tile_list_rgg_L_kernel(
         make_identity(nc, identity[:])
         pages = {}
 
-        def clear_page(m, page):
-            pages[m] = page
-            nc.gpsimd.memset(page[:], 0.0)
-
-        clear_page(0, keep.tile([P, T], F32, name="page0"))
-        clear_page(1, keep.tile([P, T], F32, name="page1"))
-        clear_page(2, keep.tile([P, T], F32, name="page2"))
+        for m in range(3):
+            pages[m] = keep.tile([P, T], F32, name="page%d" % m)
+        nc.gpsimd.memset(pages[0][:], 0.0)
+        nc.gpsimd.memset(pages[1][:], 0.0)
+        nc.gpsimd.memset(pages[2][:, T // 2 :], 0.0)
+        nc.vector.memset(pages[2][:, : T // 2], 0.0)
+        pages[3] = pages[0]
 
         tab = [keep.tile([P, T], U32, name="tab%d" % a) for a in range(PASSES)]
 
@@ -259,10 +259,10 @@ def tile_list_rgg_L_kernel(
 
         gate_inputs = [keep.tile([P, 2, JH], F32, name="gate_inputs%d" % i) for i in range(4)]
         states_a, states_b, states_c = lane("states_a", 8), lane("states_b", 8), lane("states_c", 8)
-        gated_a, gated_b, work = lane("gated_a", 6), lane("gated_b", 4), lane("work", 4)
-        lane2, lane4 = lane("lane2", 9), lane("lane4", 2)
+        gated_a, gated_b, work = lane("gated_a", 4), lane("gated_b", 4), lane("work", 4)
+        lane2, lane4 = lane("lane2", 5), lane("lane4", 4)
         spare = lane("spare", 4)
-        messages = lane("messages", 22)
+        messages = lane("messages", 24)
 
         gather_state(0, 0, states_a(0, 8))
         gather_state(1, 0, states_b(0, 8))
@@ -285,29 +285,28 @@ def tile_list_rgg_L_kernel(
 
         late_parts = [("wa", 1, NH), ("wc", 1, NH)]
         quantise(round_weights(late_parts, "grouped_late"), late_parts, "late")
-        after_rounding = lane("after_rounding", 12, "raw_wc1_%d" % NH)
+        after_rounding = lane("after_rounding", 10, "raw_wc1_%d" % NH)
         turn_back(back, after_rounding(0, 4), weighted_b0)
         scatter(1, 0, after_rounding(0, 4))
         gate(work(0, 4), gate_inputs[2])
         gate(gate_inputs[2][:, 0, :], gate_inputs[3])
-        clear_page(3, keep.tile([P, T], F32, name="page3", tag="grouped_late", align_bytes=64))
 
-        weighted_a = [after_rounding(4), after_rounding(8), after_rounding(5), after_rounding(6)]
-        weighted_b = [spare(0), after_rounding(9), lane2(1), after_rounding(7)]
+        weighted_a = [after_rounding(4), after_rounding(6), after_rounding(5), after_rounding(8)]
+        weighted_b = [spare(0), after_rounding(7), lane2(1), after_rounding(9)]
         turn(turned, 1, [states_a(4 + b) for b in range(BLOCKS)], work(0, 4), weighted_a)
         turn_back(back, messages(4, 6), weighted_a[:2])
-        gather_state(3, 0, after_rounding(8))
+        gather_state(3, 0, after_rounding(6))
         scatter(0, 2 * JQ, messages(4, 6))
         turn(sum_banks[0][1], 1, [states_b(4 + b) for b in range(BLOCKS)], gate_inputs[2][:, 0, :], weighted_b)
         turn_back(back, messages(6, 8), weighted_b[:2])
-        gather_state(3, P, after_rounding(9))
+        gather_state(3, P, after_rounding(7))
         scatter(1, 2 * JQ, messages(6, 8))
         turn_back(back, messages(8, 10), weighted_a[2:])
-        gather_state(3, 2 * P, after_rounding(6))
+        gather_state(3, 2 * P, after_rounding(8))
         scatter(0, 3 * JQ, messages(8, 10))
         store(0)
         turn_back(back, messages(10, 12), weighted_b[2:])
-        gather_state(3, 3 * P, after_rounding(7))
+        gather_state(3, 3 * P, after_rounding(9))
         scatter(1, 3 * JQ, messages(10, 12))
         store(1)
 
@@ -318,31 +317,26 @@ def tile_list_rgg_L_kernel(
         weigh(messages(12, 14), lane2(1, 3), 0)
         gather_state(3, JH, lane2(1))
         scatter(2, 0, messages(12, 14))
-        gather_state(3, JH + P, lane2(2))
+        weigh(messages(14, 16), lane2(3, 5), JQ)
+        gather_state(3, JH + P, lane2(2, 4))
+        scatter(2, JQ, messages(14, 16))
+        gather_state(3, JH + 3 * P, lane2(4))
         gate(gated_a(0, 4), gate_inputs[1])
-        add(lane4(0, 2), gated_a(0, 2), after_rounding(8, 10))
+        add(lane4(0, 4), gated_a(0, 4), after_rounding(6, 10))
         sums(2, 1, (back, turned), gate_inputs[3])
         sums(3, 1, (back, turned), gate_inputs[0])
-        weigh(messages(14, 16), lane4(0, 2), 0)
-        scatter(3, 0, messages(14, 16))
-        gather_state(3, JH + 2 * P, lane4(0))
-        gate(after_rounding(8, 12), gate_inputs[3])
-        weigh(gated_a(0, 2), lane2(3, 5), JQ)
-        scatter(2, JQ, gated_a(0, 2))
-        gather_state(3, JH + 3 * P, lane2(3))
-        add(lane2(4, 6), gated_a(2, 4), after_rounding(6, 8))
-        weigh(messages(16, 18), lane2(4, 6), JQ)
-        scatter(3, JQ, messages(16, 18))
-        gate(gated_a(2, 6), gate_inputs[0])
+        weigh(messages(16, 20), lane4(0, 4), 0)
+        scatter(3, 0, messages(16, 20))
+        gate(after_rounding(6, 10), gate_inputs[3])
+        gate(gated_a(0, 4), gate_inputs[0])
 
         weighted_c = [spare(b) for b in range(BLOCKS)]
         weighted_d = [states_a(b) for b in range(BLOCKS)]
-        turn(sum_banks[0][0], 1, [states_c(4 + b) for b in range(BLOCKS)], after_rounding(8, 12), weighted_c)
-        turn_back(sum_banks[2][1], lane2(5, 9), weighted_c)
-        scatter(2, JH, lane2(5, 9))
+        turn(sum_banks[0][0], 1, [states_c(4 + b) for b in range(BLOCKS)], after_rounding(6, 10), weighted_c)
+        turn_back(sum_banks[2][1], lane4(0, 4), weighted_c)
+        scatter(2, JH, lane4(0, 4))
         store(2)
-        states_d = [lane2(1), lane2(2), lane4(0), lane2(3)]
-        turn(sum_banks[2][0], 1, states_d, gated_a(2, 6), weighted_d)
-        turn_back(sum_banks[2][1], messages(18, 22), weighted_d)
-        scatter(3, JH, messages(18, 22))
+        turn(sum_banks[2][0], 1, [lane2(1 + b) for b in range(BLOCKS)], gated_a(0, 4), weighted_d)
+        turn_back(sum_banks[2][1], messages(20, 24), weighted_d)
+        scatter(3, JH, messages(20, 24))
         store(3)

@@ -41,24 +41,16 @@ def tile_list_rgg_L_kernel(
         lists = (src_list, dst_list)
 
         scale_rows = keep.tile([P, T], U8, name="scale_rows", align_bytes=64)
-        nc.vector.memset(scale_rows[32:64, :].bitcast(I32), 0)
-        nc.vector.memset(scale_rows[64:128, :].bitcast(I32), 0)
+        nc.gpsimd.memset(scale_rows[32:64, :].bitcast(I32), 0)
+        nc.gpsimd.memset(scale_rows[64:128, :].bitcast(I32), 0)
         wb_planes = keep.tile([P, N], U8, name="wb_planes", align_bytes=64)
-        for q in range(4):
-            nc.gpsimd.dma_start(
-                wb_planes[32 * q : 32 * q + 4 * PASSES, :].bitcast(I32),
-                wb_scales[:, 4 * q : 4 * q + 4, :].bitcast(I32),
-            )
         identity = keep.tile([P, P], F32, name="identity")
         make_identity(nc, identity[:])
         pages = {}
 
         for m in range(3):
             pages[m] = keep.tile([P, T], F32, name="page%d" % m)
-        nc.gpsimd.memset(pages[0][:], 0.0)
-        nc.gpsimd.memset(pages[1][:], 0.0)
-        nc.gpsimd.memset(pages[2][:, T // 2 :], 0.0)
-        nc.vector.memset(pages[2][:, : T // 2], 0.0)
+            nc.gpsimd.memset(pages[m][:], 0.0)
         pages[3] = pages[0]
 
         tab = [keep.tile([P, T], U32, name="tab%d" % a) for a in range(PASSES)]
@@ -100,6 +92,11 @@ def tile_list_rgg_L_kernel(
         nc.sync.dma_start(src_list[:], offs)
         nc.sync.dma_start(dst_list[:], offs2)
         load_tab(0)
+        for q in range(4):
+            nc.sync.dma_start(
+                wb_planes[32 * q : 32 * q + 4 * PASSES, :].bitcast(I32),
+                wb_scales[:, 4 * q : 4 * q + 4, :].bitcast(I32),
+            )
         load_weights(0, 0, N)
         load_tab(1)
 
@@ -260,7 +257,7 @@ def tile_list_rgg_L_kernel(
         gate_inputs = [keep.tile([P, 2, JH], F32, name="gate_inputs%d" % i) for i in range(4)]
         states_a, states_b, states_c = lane("states_a", 8), lane("states_b", 8), lane("states_c", 8)
         gated_a, gated_b, work = lane("gated_a", 4), lane("gated_b", 4), lane("work", 4)
-        lane2, lane4 = lane("lane2", 5), lane("lane4", 4)
+        lane4 = lane("lane4", 4)
         spare = lane("spare", 4)
         messages = lane("messages", 24)
 
@@ -285,14 +282,14 @@ def tile_list_rgg_L_kernel(
 
         late_parts = [("wa", 1, NH), ("wc", 1, NH)]
         quantise(round_weights(late_parts, "grouped_late"), late_parts, "late")
-        after_rounding = lane("after_rounding", 10, "raw_wc1_%d" % NH)
+        after_rounding = lane("after_rounding", 15, "raw_wc1_%d" % NH)
         turn_back(back, after_rounding(0, 4), weighted_b0)
         scatter(1, 0, after_rounding(0, 4))
         gate(work(0, 4), gate_inputs[2])
         gate(gate_inputs[2][:, 0, :], gate_inputs[3])
 
         weighted_a = [after_rounding(4), after_rounding(6), after_rounding(5), after_rounding(8)]
-        weighted_b = [spare(0), after_rounding(7), lane2(1), after_rounding(9)]
+        weighted_b = [after_rounding(10), after_rounding(7), after_rounding(11), after_rounding(9)]
         turn(turned, 1, [states_a(4 + b) for b in range(BLOCKS)], work(0, 4), weighted_a)
         turn_back(back, messages(4, 6), weighted_a[:2])
         gather_state(3, 0, after_rounding(6))
@@ -313,14 +310,14 @@ def tile_list_rgg_L_kernel(
         sums(2, 0, sum_banks[1], gate_inputs[0])
         sums(3, 0, (back, turned), gate_inputs[1])
         gate(gated_a(0, 4), gate_inputs[0])
-        add(lane2(1, 5), gated_a(0, 4), states_c(0, 4))
-        weigh(messages(12, 14), lane2(1, 3), 0)
-        gather_state(3, JH, lane2(1))
+        add(after_rounding(11, 15), gated_a(0, 4), states_c(0, 4))
+        weigh(messages(12, 14), after_rounding(11, 13), 0)
+        gather_state(3, JH, after_rounding(11))
         scatter(2, 0, messages(12, 14))
-        weigh(messages(14, 16), lane2(3, 5), JQ)
-        gather_state(3, JH + P, lane2(2, 4))
+        weigh(messages(14, 16), after_rounding(13, 15), JQ)
+        gather_state(3, JH + P, after_rounding(12, 14))
         scatter(2, JQ, messages(14, 16))
-        gather_state(3, JH + 3 * P, lane2(4))
+        gather_state(3, JH + 3 * P, after_rounding(14))
         gate(gated_a(0, 4), gate_inputs[1])
         add(lane4(0, 4), gated_a(0, 4), after_rounding(6, 10))
         sums(2, 1, (back, turned), gate_inputs[3])
@@ -336,7 +333,7 @@ def tile_list_rgg_L_kernel(
         turn_back(sum_banks[2][1], lane4(0, 4), weighted_c)
         scatter(2, JH, lane4(0, 4))
         store(2)
-        turn(sum_banks[2][0], 1, [lane2(1 + b) for b in range(BLOCKS)], gated_a(0, 4), weighted_d)
+        turn(sum_banks[2][0], 1, [after_rounding(11 + b) for b in range(BLOCKS)], gated_a(0, 4), weighted_d)
         turn_back(sum_banks[2][1], messages(20, 24), weighted_d)
         scatter(3, JH, messages(20, 24))
         store(3)

@@ -154,7 +154,7 @@ def tile_list_rgg_L_kernel(
             return grouped
 
         def quantise(grouped, parts, label):
-            words = keep.tile([P, N], U32, name="codes_" + label, align_bytes=64)
+            words = keep.tile([P, N], U32, name="codes_" + label, tag="codes_" + label, align_bytes=64)
             planes = keep.tile([P, N], U8, name="scales_" + label, align_bytes=64)
             nc.vector.quantize_mx(
                 out=words[:].bitcast(FP8X4), scales=planes[:], in_=grouped[:].rearrange("p n i -> p (n i)")
@@ -256,10 +256,9 @@ def tile_list_rgg_L_kernel(
 
         gate_inputs = [keep.tile([P, 2, JH], F32, name="gate_inputs%d" % i) for i in range(4)]
         states_a, states_b, states_c = lane("states_a", 8), lane("states_b", 8), lane("states_c", 8)
-        gated_a, gated_b, work = lane("gated_a", 4), lane("gated_b", 4), lane("work", 4)
-        lane4 = lane("lane4", 4)
+        gated_a, gated_b, work = lane("gated_a", 4), lane("gated_b", 4), lane("work", 10)
         spare = lane("spare", 4)
-        messages = lane("messages", 24)
+        messages = lane("messages", 28)
 
         gather_state(0, 0, states_a(0, 8))
         gather_state(1, 0, states_b(0, 8))
@@ -270,8 +269,8 @@ def tile_list_rgg_L_kernel(
         sums(1, 1, sum_banks[0], gate_inputs[3])
         gate(gated_a(0, 4), gate_inputs[0])
         gate(gated_b(0, 4), gate_inputs[1])
-        add(work(0, 4), gated_a(0, 4), states_a(0, 4))
-        weigh(messages(0, 4), work(0, 4), 0)
+        add(work(3, 7), gated_a(0, 4), states_a(0, 4))
+        weigh(messages(0, 4), work(3, 7), 0)
         scatter(0, 0, messages(0, 4))
 
         nc.tensor.transpose(turned[:, 0:P], weight_rows[:], identity[:])
@@ -280,19 +279,21 @@ def tile_list_rgg_L_kernel(
         weighted_b0 = [spare(b) for b in range(BLOCKS)]
         turn(turned, 0, [states_b(b) for b in range(BLOCKS)], gated_b(0, 4), weighted_b0)
 
+        turn_back(back, work(6, 10), weighted_b0)
+        scatter(1, 0, work(6, 10))
         late_parts = [("wa", 1, NH), ("wc", 1, NH)]
-        quantise(round_weights(late_parts, "grouped_late"), late_parts, "late")
+        grouped_late = round_weights(late_parts, "grouped_late")
         after_rounding = lane("after_rounding", 15, "raw_wc1_%d" % NH)
-        turn_back(back, after_rounding(0, 4), weighted_b0)
-        scatter(1, 0, after_rounding(0, 4))
+        before_quantise = keep.tile([P, P], F32, name="before_quantise", tag="codes_late", align_bytes=64)
         gate(work(0, 4), gate_inputs[2])
         gate(gate_inputs[2][:, 0, :], gate_inputs[3])
 
-        weighted_a = [after_rounding(4), after_rounding(6), after_rounding(5), after_rounding(8)]
+        weighted_a = [after_rounding(6), before_quantise[:], after_rounding(5), after_rounding(8)]
         weighted_b = [after_rounding(10), after_rounding(7), after_rounding(11), after_rounding(9)]
         turn(turned, 1, [states_a(4 + b) for b in range(BLOCKS)], work(0, 4), weighted_a)
         turn_back(back, messages(4, 6), weighted_a[:2])
         gather_state(3, 0, after_rounding(6))
+        quantise(grouped_late, late_parts, "late")
         scatter(0, 2 * JQ, messages(4, 6))
         turn(sum_banks[0][1], 1, [states_b(4 + b) for b in range(BLOCKS)], gate_inputs[2][:, 0, :], weighted_b)
         turn_back(back, messages(6, 8), weighted_b[:2])
@@ -308,32 +309,31 @@ def tile_list_rgg_L_kernel(
         store(1)
 
         sums(2, 0, sum_banks[1], gate_inputs[0])
-        sums(3, 0, (back, turned), gate_inputs[1])
+        sums(3, 0, (turned, sum_banks[0][1]), gate_inputs[1])
         gate(gated_a(0, 4), gate_inputs[0])
         add(after_rounding(11, 15), gated_a(0, 4), states_c(0, 4))
         weigh(messages(12, 14), after_rounding(11, 13), 0)
         gather_state(3, JH, after_rounding(11))
         scatter(2, 0, messages(12, 14))
+        gate(gated_a(0, 4), gate_inputs[1])
         weigh(messages(14, 16), after_rounding(13, 15), JQ)
         gather_state(3, JH + P, after_rounding(12, 14))
         scatter(2, JQ, messages(14, 16))
         gather_state(3, JH + 3 * P, after_rounding(14))
-        gate(gated_a(0, 4), gate_inputs[1])
-        add(lane4(0, 4), gated_a(0, 4), after_rounding(6, 10))
-        sums(2, 1, (back, turned), gate_inputs[3])
-        sums(3, 1, (back, turned), gate_inputs[0])
-        weigh(messages(16, 20), lane4(0, 4), 0)
-        scatter(3, 0, messages(16, 20))
-        gate(after_rounding(6, 10), gate_inputs[3])
-        gate(gated_a(0, 4), gate_inputs[0])
+        sums(2, 1, sum_banks[1], gate_inputs[3])
+        sums(3, 1, (turned, sum_banks[0][1]), gate_inputs[0])
 
-        weighted_c = [spare(b) for b in range(BLOCKS)]
-        weighted_d = [states_a(b) for b in range(BLOCKS)]
-        turn(sum_banks[0][0], 1, [states_c(4 + b) for b in range(BLOCKS)], after_rounding(6, 10), weighted_c)
-        turn_back(sum_banks[2][1], lane4(0, 4), weighted_c)
-        scatter(2, JH, lane4(0, 4))
+        def finish_by_transposes(n, m, h, bank, states, b0, gated):
+            weighted = [states_a(4 * (n % 2) + b) for b in range(BLOCKS)]
+            message = messages(16 + 4 * n, 20 + 4 * n)
+            turn(bank, h, [states(b0 + b) for b in range(BLOCKS)], gated, weighted)
+            turn_back(sum_banks[2][1], message, weighted)
+            scatter(m, h * JH, message)
+
+        finish_by_transposes(0, 3, 0, sum_banks[2][0], after_rounding, 6, gated_a(0, 4))
+        gate(gated_b(0, 4), gate_inputs[3])
+        finish_by_transposes(1, 2, 1, sum_banks[0][0], states_c, 4, gated_b(0, 4))
         store(2)
-        turn(sum_banks[2][0], 1, [after_rounding(11 + b) for b in range(BLOCKS)], gated_a(0, 4), weighted_d)
-        turn_back(sum_banks[2][1], messages(20, 24), weighted_d)
-        scatter(3, JH, messages(20, 24))
+        gate(work(0, 4), gate_inputs[0])
+        finish_by_transposes(2, 3, 1, sum_banks[2][0], after_rounding, 11, work(0, 4))
         store(3)

@@ -256,7 +256,7 @@ def tile_list_rgg_L_kernel(
 
         gate_inputs = [keep.tile([P, 2, JH], F32, name="gate_inputs%d" % i) for i in range(4)]
         states_a, states_b, states_c = lane("states_a", 8), lane("states_b", 8), lane("states_c", 8)
-        gated_a, gated_b, work = lane("gated_a", 4), lane("gated_b", 4), lane("work", 10)
+        gated_a, gated_b, work = lane("gated_a", 4), lane("gated_b", 4), lane("work", 8)
         spare = lane("spare", 4)
         messages = lane("messages", 28)
 
@@ -279,21 +279,21 @@ def tile_list_rgg_L_kernel(
         weighted_b0 = [spare(b) for b in range(BLOCKS)]
         turn(turned, 0, [states_b(b) for b in range(BLOCKS)], gated_b(0, 4), weighted_b0)
 
-        turn_back(back, work(6, 10), weighted_b0)
-        scatter(1, 0, work(6, 10))
+        turn_back(back, work(6, 8), weighted_b0[:2])
+        scatter(1, 0, work(6, 8))
         late_parts = [("wa", 1, NH), ("wc", 1, NH)]
-        grouped_late = round_weights(late_parts, "grouped_late")
+        quantise(round_weights(late_parts, "grouped_late"), late_parts, "late")
         after_rounding = lane("after_rounding", 15, "raw_wc1_%d" % NH)
-        before_quantise = keep.tile([P, P], F32, name="before_quantise", tag="codes_late", align_bytes=64)
+        turn_back(back, after_rounding(0, 2), weighted_b0[2:])
+        scatter(1, JQ, after_rounding(0, 2))
         gate(work(0, 4), gate_inputs[2])
         gate(gate_inputs[2][:, 0, :], gate_inputs[3])
 
-        weighted_a = [after_rounding(6), before_quantise[:], after_rounding(5), after_rounding(8)]
+        weighted_a = [after_rounding(4), after_rounding(6), after_rounding(5), after_rounding(8)]
         weighted_b = [after_rounding(10), after_rounding(7), after_rounding(11), after_rounding(9)]
         turn(turned, 1, [states_a(4 + b) for b in range(BLOCKS)], work(0, 4), weighted_a)
         turn_back(back, messages(4, 6), weighted_a[:2])
         gather_state(3, 0, after_rounding(6))
-        quantise(grouped_late, late_parts, "late")
         scatter(0, 2 * JQ, messages(4, 6))
         turn(sum_banks[0][1], 1, [states_b(4 + b) for b in range(BLOCKS)], gate_inputs[2][:, 0, :], weighted_b)
         turn_back(back, messages(6, 8), weighted_b[:2])

@@ -154,7 +154,7 @@ def tile_list_rgg_L_kernel(
             return grouped
 
         def quantise(grouped, parts, label):
-            words = keep.tile([P, N], U32, name="codes_" + label, tag="codes_" + label, align_bytes=64)
+            words = keep.tile([P, N], U32, name="codes_" + label, align_bytes=64)
             planes = keep.tile([P, N], U8, name="scales_" + label, align_bytes=64)
             nc.vector.quantize_mx(
                 out=words[:].bitcast(FP8X4), scales=planes[:], in_=grouped[:].rearrange("p n i -> p (n i)")
@@ -256,7 +256,7 @@ def tile_list_rgg_L_kernel(
 
         gate_inputs = [keep.tile([P, 2, JH], F32, name="gate_inputs%d" % i) for i in range(4)]
         states_a, states_b, states_c = lane("states_a", 8), lane("states_b", 8), lane("states_c", 8)
-        gated_a, gated_b, work = lane("gated_a", 4), lane("gated_b", 4), lane("work", 8)
+        gated_a, gated_b, work = lane("gated_a", 4), lane("gated_b", 4), lane("work", 4)
         spare = lane("spare", 4)
         messages = lane("messages", 28)
 
@@ -269,8 +269,8 @@ def tile_list_rgg_L_kernel(
         sums(1, 1, sum_banks[0], gate_inputs[3])
         gate(gated_a(0, 4), gate_inputs[0])
         gate(gated_b(0, 4), gate_inputs[1])
-        add(work(3, 7), gated_a(0, 4), states_a(0, 4))
-        weigh(messages(0, 4), work(3, 7), 0)
+        add(work(0, 4), gated_a(0, 4), states_a(0, 4))
+        weigh(messages(0, 4), work(0, 4), 0)
         scatter(0, 0, messages(0, 4))
 
         nc.tensor.transpose(turned[:, 0:P], weight_rows[:], identity[:])
@@ -279,13 +279,11 @@ def tile_list_rgg_L_kernel(
         weighted_b0 = [spare(b) for b in range(BLOCKS)]
         turn(turned, 0, [states_b(b) for b in range(BLOCKS)], gated_b(0, 4), weighted_b0)
 
-        turn_back(back, work(6, 8), weighted_b0[:2])
-        scatter(1, 0, work(6, 8))
         late_parts = [("wa", 1, NH), ("wc", 1, NH)]
         quantise(round_weights(late_parts, "grouped_late"), late_parts, "late")
         after_rounding = lane("after_rounding", 15, "raw_wc1_%d" % NH)
-        turn_back(back, after_rounding(0, 2), weighted_b0[2:])
-        scatter(1, JQ, after_rounding(0, 2))
+        turn_back(back, after_rounding(0, 4), weighted_b0)
+        scatter(1, 0, after_rounding(0, 4))
         gate(work(0, 4), gate_inputs[2])
         gate(gate_inputs[2][:, 0, :], gate_inputs[3])
 

@@ -183,24 +183,24 @@ def tile_list_rgg_L_kernel(
         turned = psum.tile([P, JH], F32, name="turned")
         back = psum.tile([P, JH], F32, name="back")
 
-        def sums(m, h, banks, gate_inputs):
-            za, ms = banks
-            cols = slice(m * P, (m + 1) * P)
+        def with_wb(banks, m, h, a, start):
+            codes_wb = wb_codes[m // 2][:, a, (m % 2) * P : (m % 2 + 1) * P]
+            product(banks[0], codes_wb, wb_planes[4 * a :, m * P : (m + 1) * P], 0, a, h, start, False)
 
-            def with_wb(a, start):
-                product(za, wb_codes[m // 2][:, a, (m % 2) * P : (m % 2 + 1) * P], wb_planes[4 * a :, cols], 0, a, h, start, False)
+        def with_quantised(banks, m, h, a, opens_za, last):
+            product(banks[0], codes["wa", a, m], scales["wa", a, m], 1, a, h, opens_za, last)
+            product(banks[1], codes["wc", a, m], scales["wc", a, m], 0, a, h, not last, last)
 
-            def with_quantised(a, start):
-                last = a == PASSES - 1
-                product(za, codes["wa", a, m], scales["wa", a, m], 1, a, h, start, last)
-                product(ms, codes["wc", a, m], scales["wc", a, m], 0, a, h, a == 0, last)
+        def close_sums(banks, m, h, a, gate_inputs):
+            with_quantised(banks, m, h, a, False, True)
+            nc.scalar.activation(gate_inputs[:, 0, :], banks[0][:], ACT.Sigmoid)
+            nc.scalar.copy(gate_inputs[:, 1, :], banks[1][:])
 
-            with_wb(0, True)
-            with_wb(1, False)
-            with_quantised(0, False)
-            with_quantised(1, False)
-            nc.scalar.activation(gate_inputs[:, 0, :], za[:], ACT.Sigmoid)
-            nc.scalar.copy(gate_inputs[:, 1, :], ms[:])
+        def sums(m, h, banks, gate_inputs, passes=(0, 1)):
+            with_wb(banks, m, h, passes[0], True)
+            with_wb(banks, m, h, passes[1], False)
+            with_quantised(banks, m, h, passes[0], False, False)
+            close_sums(banks, m, h, passes[1], gate_inputs)
 
         def gate(gated, gate_inputs):
             nc.gpsimd.tensor_tensor(gated, gate_inputs[:, 1, :], gate_inputs[:, 0, :], ALU.mult)
@@ -218,7 +218,10 @@ def tile_list_rgg_L_kernel(
             nc.vector.tensor_copy(pages[m][:].indirect(entries(1, j0, message.shape[1])), message)
 
         def store(m):
-            nc.sync.dma_start(out[m * P : (m + 1) * P, :], pages[m][:])
+            pieces = (4, 2, 2, 1)[m]
+            for c in range(pieces):
+                cols = slice(c * T // pieces, (c + 1) * T // pieces)
+                nc.sync.dma_start(out[m * P : (m + 1) * P, cols], pages[m][:, cols])
 
         def turn(bank, h, states, gated, weighted, blocks=range(BLOCKS)):
             for b in blocks:
@@ -263,9 +266,14 @@ def tile_list_rgg_L_kernel(
         gather_state(0, 0, states_a(0, 8))
         gather_state(1, 0, states_b(0, 8))
         gather_state(2, 0, states_c(0, 8))
-        sums(0, 0, sum_banks[0], gate_inputs[0])
-        sums(1, 0, sum_banks[1], gate_inputs[1])
-        sums(0, 1, sum_banks[2], gate_inputs[2])
+        for m in range(2):
+            with_quantised(sum_banks[m], m, 0, 0, True, False)
+        for m in range(2):
+            with_wb(sum_banks[m], m, 0, 0, False)
+            with_wb(sum_banks[m], m, 0, 1, False)
+        for m in range(2):
+            close_sums(sum_banks[m], m, 0, 1, gate_inputs[m])
+        sums(0, 1, sum_banks[2], gate_inputs[2], (1, 0))
         sums(1, 1, sum_banks[0], gate_inputs[3])
         gate(gated_a(0, 4), gate_inputs[0])
         gate(gated_b(0, 4), gate_inputs[1])

from contextlib import ExitStack

import concourse.mybir as mybir
from concourse.masks import make_identity

K, N, T, J = 1024, 512, 2048, 1024
FLOPS = 3 * 2 * K * N * J

F32 = mybir.dt.float32
BF16 = mybir.dt.bfloat16
I32 = mybir.dt.int32
U32 = mybir.dt.uint32
U16 = mybir.dt.uint16
U8 = mybir.dt.uint8
FP8X4 = mybir.dt.float8_e4m3fn_x4
ALU = mybir.AluOpType
ACT = mybir.ActivationFunctionType

P = 128
PACK = 4
K_PASS = P * PACK
PASSES = K // K_PASS
JH = 512
JQ = 256
LIST_COLS = J // 16
TILES = N // P
BLOCKS = JH // P
NH = N // 2


def tile_list_rgg_L_kernel(
    tc, tab_words, tab_scales, wa, wb_words, wb_scales, wc, rT, wgo, offs, offs2, out
):
    nc = tc.nc
    with ExitStack() as ctx:
        keep = ctx.enter_context(tc.tile_pool(name="keep", bufs=1))
        psum = ctx.enter_context(tc.psum_pool(name="psum", bufs=1))

        src_list = keep.tile([P, LIST_COLS], U16, name="src_list")
        dst_list = keep.tile([P, LIST_COLS], U16, name="dst_list")
        lists = (src_list, dst_list)

        scale_rows = keep.tile([P, T], U8, name="scale_rows", align_bytes=64)
        nc.gpsimd.memset(scale_rows[32:64, :].bitcast(I32), 0)
        nc.gpsimd.memset(scale_rows[64:128, :].bitcast(I32), 0)
        wb_planes = keep.tile([P, N], U8, name="wb_planes", align_bytes=64)
        identity = keep.tile([P, P], F32, name="identity")
        make_identity(nc, identity[:])
        pages = {}

        for m in range(3):
            pages[m] = keep.tile([P, T], F32, name="page%d" % m)
            nc.gpsimd.memset(pages[m][:], 0.0)
        pages[3] = pages[0]

        tab = [keep.tile([P, T], U32, name="tab%d" % a) for a in range(PASSES)]

        def load_tab(a):
            nc.sync.dma_start(
                tab[a][:].bitcast(I32), tab_words[a].rearrange("p t i -> p (t i)").bitcast(I32)
            )

        raw = {}

        def load_weights(a, n0, width):
            for name, w in (("wa", wa), ("wc", wc)):
                label = "raw_%s%d_%d" % (name, a, n0)
                raw[name, a, n0] = keep.tile([P, PACK, width], F32, name=label, tag=label, align_bytes=64)
                nc.sync.dma_start(
                    raw[name, a, n0][:],
                    w[a * K_PASS : (a + 1) * K_PASS, n0 : n0 + width].rearrange("(p i) n -> p i n", i=PACK),
                )

        state = [keep.tile([P, T], F32, name="state%d" % m, align_bytes=64) for m in range(TILES)]
        wb_codes = [keep.tile([P, PASSES, NH], U32, name="wb_codes%d" % u, align_bytes=64) for u in range(2)]

        def load_wb_half(u):
            nc.sync.dma_start(
                wb_codes[u][:].bitcast(I32),
                wb_words[:, :, u * NH : (u + 1) * NH, :].rearrange("a p n i -> p a (n i)").bitcast(I32),
            )

        edge_weight = keep.tile([P, JH], F32, name="edge_weight")
        weight_rows = keep.tile([P, P], F32, name="weight_rows")

        def load_state(m):
            nc.sync.dma_start(state[m][:], rT[m * P : (m + 1) * P, :])

        nc.sync.dma_start(
            scale_rows[0:32, :].bitcast(I32), tab_scales.rearrange("a q t -> (a q) t").bitcast(I32)
        )
        nc.sync.dma_start(src_list[:], offs)
        nc.sync.dma_start(dst_list[:], offs2)
        load_tab(0)
        for q in range(4):
            nc.sync.dma_start(
                wb_planes[32 * q : 32 * q + 4 * PASSES, :].bitcast(I32),
                wb_scales[:, 4 * q : 4 * q + 4, :].bitcast(I32),
            )
        load_weights(0, 0, N)
        load_tab(1)

        picked_planes = [keep.tile([P, 2 * J], U8, name="picked_planes%d" % a, align_bytes=64) for a in range(PASSES)]
        picked_rows = keep.tile([P, 2 * J], U8, name="picked_rows", align_bytes=64)
        for li in range(2):
            nc.vector.tensor_copy(picked_rows[:, li * J : (li + 1) * J], scale_rows[:].indirect(lists[li][:]))

        def move_planes(a):
            for q in range(4):
                nc.sync.dma_start(
                    picked_planes[a][32 * q : 32 * q + 4, :].bitcast(I32),
                    picked_rows[16 * a + 4 * q : 16 * a + 4 * q + 4, :].bitcast(I32),
                )

        move_planes(0)
        load_weights(1, 0, NH)
        load_wb_half(0)
        move_planes(1)
        load_state(0)
        nc.sync.dma_start(weight_rows[:], wgo[0 : P * P // J, :].rearrange("r (b c) -> (r b) c", c=P))
        load_state(1)
        load_state(2)
        nc.sync.dma_start(edge_weight[:], wgo[:, 0:JH])
        load_weights(1, NH, NH)
        load_wb_half(1)
        load_state(3)

        def entries(li, j0, width):
            return lists[li][:, j0 // 16 : (j0 + width) // 16]

        picked = {}

        def gather_words(li, a, h0, halves, words):
            nc.vector.tensor_copy(words, tab[a][:].indirect(entries(li, h0 * JH, halves * JH)))
            for h in range(halves):
                picked[li, a, h0 + h] = words[:, h * JH : (h + 1) * JH]

        codes = {}
        scales = {}

        def interleave(grouped, rows):
            nc.scalar.copy(
                grouped.rearrange("p (c n) i -> p c i n", n=4),
                rows.rearrange("p i (c n) -> p c i n", n=4),
            )

        def round_weights(parts, tag):
            grouped = keep.tile([P, N, PACK], BF16, name=tag, tag=tag, align_bytes=64)
            c0 = 0
            for part in parts:
                width = raw[part].shape[2]
                interleave(grouped[:, c0 : c0 + width, :], raw[part][:])
                c0 = c0 + width
            return grouped

        def quantise(grouped, parts, label):
            words = keep.tile([P, N], U32, name="codes_" + label, align_bytes=64)
            planes = keep.tile([P, N], U8, name="scales_" + label, align_bytes=64)
            nc.vector.quantize_mx(
                out=words[:].bitcast(FP8X4), scales=planes[:], in_=grouped[:].rearrange("p n i -> p (n i)")
            )
            c0 = 0
            for name, a, n0 in parts:
                for m in range(n0 // P, (n0 + raw[name, a, n0].shape[2]) // P):
                    codes[name, a, m] = words[:, c0 : c0 + P]
                    scales[name, a, m] = planes[:, c0 : c0 + P]
                    c0 = c0 + P

        def product(acc, w_codes, w_scales, li, a, h, start, stop):
            nc.tensor.matmul_mx(
                out=acc[:],
                lhsT=w_codes.bitcast(FP8X4),
                lhsT_scale=w_scales,
                rhs=picked[li, a, h].bitcast(FP8X4),
                rhs_scale=picked_planes[a][:, li * J + h * JH : li * J + (h + 1) * JH],
                start=start,
                stop=stop,
            )

        sum_banks = [
            (psum.tile([P, JH], F32, name="za%d" % i), psum.tile([P, JH], F32, name="ms%d" % i)) for i in range(3)
        ]
        turned = psum.tile([P, JH], F32, name="turned")
        back = psum.tile([P, JH], F32, name="back")

        def with_wb(banks, m, h, a, start):
            codes_wb = wb_codes[m // 2][:, a, (m % 2) * P : (m % 2 + 1) * P]
            product(banks[0], codes_wb, wb_planes[4 * a :, m * P : (m + 1) * P], 0, a, h, start, False)

        def with_quantised(banks, m, h, a, opens_za, last):
            product(banks[0], codes["wa", a, m], scales["wa", a, m], 1, a, h, opens_za, last)
            product(banks[1], codes["wc", a, m], scales["wc", a, m], 0, a, h, not last, last)

        def close_sums(banks, m, h, a, gate_inputs):
            with_quantised(banks, m, h, a, False, True)
            nc.scalar.activation(gate_inputs[:, 0, :], banks[0][:], ACT.Sigmoid)
            nc.scalar.copy(gate_inputs[:, 1, :], banks[1][:])

        def sums(m, h, banks, gate_inputs, passes=(0, 1)):
            with_wb(banks, m, h, passes[0], True)
            with_wb(banks, m, h, passes[1], False)
            with_quantised(banks, m, h, passes[0], False, False)
            close_sums(banks, m, h, passes[1], gate_inputs)

        def gate(gated, gate_inputs):
            nc.gpsimd.tensor_tensor(gated, gate_inputs[:, 1, :], gate_inputs[:, 0, :], ALU.mult)

        def add(total, gated, states):
            nc.gpsimd.tensor_tensor(total, gated, states, ALU.add)

        def weigh(message, total, j0):
            nc.gpsimd.tensor_tensor(message, total, edge_weight[:, j0 : j0 + message.shape[1]], ALU.mult)

        def gather_state(m, j0, states):
            nc.vector.tensor_copy(states, state[m][:].indirect(entries(1, j0, states.shape[1])))

        def scatter(m, j0, message):
            nc.vector.tensor_copy(pages[m][:].indirect(entries(1, j0, message.shape[1])), message)

        def store(m):
            pieces = (4, 2, 2, 1)[m]
            for c in range(pieces):
                cols = slice(c * T // pieces, (c + 1) * T // pieces)
                nc.sync.dma_start(out[m * P : (m + 1) * P, cols], pages[m][:, cols])

        def turn(bank, h, states, gated, weighted, blocks=range(BLOCKS)):
            for b in blocks:
                cols = slice(b * P, (b + 1) * P)
                nc.tensor.matmul(bank[:, cols], gated[:, cols], identity[:], start=b == blocks[0], stop=False, is_transpose=True)
            for b in blocks:
                cols = slice(b * P, (b + 1) * P)
                nc.tensor.matmul(bank[:, cols], states[b], identity[:], start=False, stop=b == blocks[-1], is_transpose=True)
            for b in blocks:
                nc.scalar.activation(
                    weighted[b], bank[:, b * P : (b + 1) * P], ACT.Copy, scale=weight_cols[:, h * BLOCKS + b : h * BLOCKS + b + 1]
                )

        def turn_back(bank, message, weighted):
            for b, block in enumerate(weighted):
                nc.tensor.transpose(bank[:, b * P : (b + 1) * P], block, identity[:])
            nc.scalar.copy(message, bank[:, 0 : len(weighted) * P])

        def lane(name, blocks, tag=None):
            tile = keep.tile([P, blocks * P], F32, name=name, tag=tag or name, align_bytes=64)
            return lambda b0, b1=None: tile[:, b0 * P : (b0 + 1 if b1 is None else b1) * P]

        def words_tile(label, width, tag):
            return keep.tile([P, width], U32, name=label, tag=tag, align_bytes=64)[:]

        gather_words(1, 0, 0, 2, words_tile("words_dst0", J, "words_dst0"))
        gather_words(0, 0, 0, 2, words_tile("words_src0", J, "words_src0"))
        for part in (("wa", 0, 0), ("wc", 0, 0)):
            quantise(round_weights([part], "grouped_" + part[0]), [part], part[0])
        gather_words(0, 1, 0, 1, words_tile("words_src1_0", JH, "raw_wa0_0"))
        gather_words(1, 1, 0, 2, words_tile("words_dst1", J, "raw_wc0_0"))
        early_parts = [("wa", 1, 0), ("wc", 1, 0)]
        quantise(round_weights(early_parts, "grouped_early"), early_parts, "early")
        gather_words(0, 1, 1, 1, words_tile("words_src1_1", JH, "raw_wc1_0"))

        gate_inputs = [keep.tile([P, 2, JH], F32, name="gate_inputs%d" % i) for i in range(4)]
        states_a, states_b, states_c = lane("states_a", 8), lane("states_b", 8), lane("states_c", 8)
        gated_a, gated_b, work = lane("gated_a", 4), lane("gated_b", 4), lane("work", 4)
        spare = lane("spare", 4)
        messages = lane("messages", 28)

        gather_state(0, 0, states_a(0, 8))
        gather_state(1, 0, states_b(0, 8))
        gather_state(2, 0, states_c(0, 8))
        for m in range(2):
            with_quantised(sum_banks[m], m, 0, 0, True, False)
        for m in range(2):
            with_wb(sum_banks[m], m, 0, 0, False)
            with_wb(sum_banks[m], m, 0, 1, False)
        for m in range(2):
            close_sums(sum_banks[m], m, 0, 1, gate_inputs[m])
        sums(0, 1, sum_banks[2], gate_inputs[2], (1, 0))
        sums(1, 1, sum_banks[0], gate_inputs[3])
        gate(gated_a(0, 4), gate_inputs[0])
        gate(gated_b(0, 4), gate_inputs[1])
        add(work(0, 4), gated_a(0, 4), states_a(0, 4))
        weigh(messages(0, 4), work(0, 4), 0)
        scatter(0, 0, messages(0, 4))

        nc.tensor.transpose(turned[:, 0:P], weight_rows[:], identity[:])
        weight_cols = keep.tile([P, 2 * BLOCKS], F32, name="weight_cols")
        nc.scalar.copy(weight_cols[:], turned[:, 0 : 2 * BLOCKS])
        weighted_b0 = [spare(b) for b in range(BLOCKS)]
        turn(turned, 0, [states_b(b) for b in range(BLOCKS)], gated_b(0, 4), weighted_b0)

        late_parts = [("wa", 1, NH), ("wc", 1, NH)]
        quantise(round_weights(late_parts, "grouped_late"), late_parts, "late")
        after_rounding = lane("after_rounding", 15, "raw_wc1_%d" % NH)
        turn_back(back, after_rounding(0, 4), weighted_b0)
        scatter(1, 0, after_rounding(0, 4))
        gate(work(0, 4), gate_inputs[2])
        gate(gate_inputs[2][:, 0, :], gate_inputs[3])

        weighted_a = [after_rounding(4), after_rounding(6), after_rounding(5), after_rounding(8)]
        weighted_b = [after_rounding(10), after_rounding(7), after_rounding(11), after_rounding(9)]
        turn(turned, 1, [states_a(4 + b) for b in range(BLOCKS)], work(0, 4), weighted_a)
        turn_back(back, messages(4, 6), weighted_a[:2])
        gather_state(3, 0, after_rounding(6))
        scatter(0, 2 * JQ, messages(4, 6))
        turn(sum_banks[0][1], 1, [states_b(4 + b) for b in range(BLOCKS)], gate_inputs[2][:, 0, :], weighted_b)
        turn_back(back, messages(6, 8), weighted_b[:2])
        gather_state(3, P, after_rounding(7))
        scatter(1, 2 * JQ, messages(6, 8))
        turn_back(back, messages(8, 10), weighted_a[2:])
        gather_state(3, 2 * P, after_rounding(8))
        scatter(0, 3 * JQ, messages(8, 10))
        store(0)
        turn_back(back, messages(10, 12), weighted_b[2:])
        gather_state(3, 3 * P, after_rounding(9))
        scatter(1, 3 * JQ, messages(10, 12))
        store(1)

        sums(2, 0, sum_banks[1], gate_inputs[0])
        sums(3, 0, (turned, sum_banks[0][1]), gate_inputs[1])
        gate(gated_a(0, 4), gate_inputs[0])
        add(after_rounding(11, 15), gated_a(0, 4), states_c(0, 4))
        weigh(messages(12, 14), after_rounding(11, 13), 0)
        gather_state(3, JH, after_rounding(11))
        scatter(2, 0, messages(12, 14))
        gate(gated_a(0, 4), gate_inputs[1])
        weigh(messages(14, 16), after_rounding(13, 15), JQ)
        gather_state(3, JH + P, after_rounding(12, 14))
        scatter(2, JQ, messages(14, 16))
        gather_state(3, JH + 3 * P, after_rounding(14))
        sums(2, 1, sum_banks[1], gate_inputs[3])
        sums(3, 1, (turned, sum_banks[0][1]), gate_inputs[0])

        def finish_by_transposes(n, m, h, bank, states, b0, gated):
            weighted = [states_a(4 * (n % 2) + b) for b in range(BLOCKS)]
            message = messages(16 + 4 * n, 20 + 4 * n)
            turn(bank, h, [states(b0 + b) for b in range(BLOCKS)], gated, weighted)
            turn_back(sum_banks[2][1], message, weighted)
            scatter(m, h * JH, message)

        finish_by_transposes(0, 3, 0, sum_banks[2][0], after_rounding, 6, gated_a(0, 4))
        gate(gated_b(0, 4), gate_inputs[3])
        finish_by_transposes(1, 2, 1, sum_banks[0][0], states_c, 4, gated_b(0, 4))
        store(2)
        gate(work(0, 4), gate_inputs[0])
        finish_by_transposes(2, 3, 1, sum_banks[2][0], after_rounding, 11, work(0, 4))
        store(3)
